import numpy as np
import ml_dtypes


def mxq(x, axis, fmt="e4m3"):
    dtype, down = {"e4m3": (ml_dtypes.float8_e4m3fn, 7), "e5m2": (ml_dtypes.float8_e5m2, 14)}[fmt]
    v = np.moveaxis(np.asarray(x, np.float32).astype(ml_dtypes.bfloat16).astype(np.float64), axis, -1)
    blocks = v.reshape(v.shape[:-1] + (-1, 32))
    amax = np.abs(blocks).max(-1, keepdims=True)
    byte = np.maximum(np.where(amax > 0, np.frexp(amax)[1] - 1 + 127, 0) - down, 1)
    scale = np.exp2(byte - 127.0)
    codes = (blocks / scale).astype(np.float32).astype(dtype).astype(np.float64)
    return np.moveaxis((codes * scale).reshape(v.shape), -1, axis)


WIDE = False


def mx_kscale(k):
    if not WIDE:
        return np.ones(k)
    levels = np.array([10, -10, 5, -5, 0])
    if k % 512:
        return np.exp2(np.random.permutation(np.resize(levels, k // 32))).repeat(32)
    a = np.empty((k // 512, 16))
    for p in range(k // 512):
        a[p, :8] = np.random.permutation(np.resize(levels, 8))
        for g in range(8):
            far = levels[np.abs(levels - a[p, g]) >= 10]
            a[p, g + 8] = far[np.random.randint(len(far))]
    return np.exp2(a.ravel()).repeat(32)


def f64(x):
    return np.asarray(x).astype(np.float64)


def striped(idx):
    return np.tile(idx.reshape(-1, 16).T, (8, 1)).astype(np.uint16)


def unstriped(offs):
    return offs[:16].T.reshape(-1).astype(np.int64)


E2M1 = np.array([0.0, 0.5, 1.0, 1.5, 2.0, 3.0, 4.0, 6.0, -0.0, -0.5, -1.0, -1.5, -2.0, -3.0, -4.0, -6.0])


def pack_weight(w, fmt):
    k, n = w.shape
    w = f64(np.asarray(w, np.float32).astype(ml_dtypes.bfloat16)).reshape(k // 32, 32, n)
    amax = np.abs(w).max(1)
    if fmt == "e4m3":
        byte = np.frexp(amax)[1] - 1 + 127 - 7
    else:
        mant, ex = np.frexp(amax / 6.0)
        byte = np.where(mant > 0.5, ex, ex - 1) + 127
    byte = np.clip(np.where(amax > 0, byte, 1), 1, 254)
    scaled = (w * np.exp2(127.0 - byte)[:, None, :]).reshape(k, n).astype(np.float32)
    by_word = np.ascontiguousarray(scaled.reshape(k // 512, 128, 4, n).transpose(0, 1, 3, 2))
    if fmt == "e4m3":
        words = by_word.astype(ml_dtypes.float8_e4m3fn).view(np.uint8)
    else:
        c = by_word.astype(ml_dtypes.float4_e2m1fn).view(np.uint8) & 0xF
        words = (c[..., 0::2] | (c[..., 1::2] << 4)).reshape(k // 512, 128, 2 * n)
    return np.ascontiguousarray(words), np.ascontiguousarray(byte.astype(np.uint8).reshape(k // 512, 16, n))


def unpack_weight(words, scales, fmt):
    g, _, n = scales.shape
    words = np.ascontiguousarray(words).reshape(g, 128, n, -1)
    if fmt == "e4m3":
        vals = words.view(ml_dtypes.float8_e4m3fn).astype(np.float64)
    else:
        nib = np.empty((g, 128, n, 4), np.uint8)
        nib[..., 0::2] = words & 0xF
        nib[..., 1::2] = words >> 4
        vals = E2M1[nib]
    vals = vals * np.repeat(np.exp2(scales.astype(np.float64) - 127.0), 8, axis=1)[..., None]
    return vals.transpose(0, 1, 3, 2).reshape(g * 512, n)


def relu(v):
    return np.maximum(v, 0.0)


def d_relu(v):
    return (v > 0).astype(np.float64)


K, T, E1, C1, E2, C2, H = 512, 768, 6, 128, 3, 256, 512
N = 1024


def by_expert(wq, xq, E, C):
    return np.concatenate([wq[e].T @ xq[:, e * C:(e + 1) * C] for e in range(E)], axis=1)


def setup_inputs():
    n = np.random.standard_normal
    v = mx_kscale(N)
    u = mx_kscale(H)
    slots1, slots2 = np.random.permutation(T), np.random.permutation(T)
    dy = pack_weight(n((N, T)) * v[:, None], "e4m3")
    w2t = pack_weight(n((N, H)) / np.sqrt(N) / v[:, None] * u, "e4m3")
    wat = [pack_weight(m, "e4m3") for m in n((E1, H, K)) / np.sqrt(H) / u[None, :, None]]
    wbt = [pack_weight(m, "e2m1") for m in n((E2, H, K)) / np.sqrt(H) / u[None, :, None]]
    return {
        "dy_words": dy[0],
        "dy_scales": dy[1],
        "w2t_words": w2t[0],
        "w2t_scales": w2t[1],
        "wat_words": np.stack([m[0] for m in wat]),
        "wat_scales": np.stack([m[1] for m in wat]),
        "wbt_words": np.stack([m[0] for m in wbt]),
        "wbt_scales": np.stack([m[1] for m in wbt]),
        "a": (n((H, T))).astype(np.float32),
        "c": (n((H, T))).astype(np.float32),
        "offs": striped(slots1),
        "offs2": striped(slots2),
    }


def reference(dy_words, dy_scales, w2t_words, w2t_scales, wat_words, wat_scales, wbt_words, wbt_scales, a, c, offs, offs2):
    w2t = unpack_weight(w2t_words, w2t_scales, "e4m3")
    wat = np.stack([unpack_weight(wat_words[e], wat_scales[e], "e4m3") for e in range(E1)])
    wbt = np.stack([unpack_weight(wbt_words[e], wbt_scales[e], "e2m1") for e in range(E2)])
    idx, idx2 = unstriped(offs), unstriped(offs2)
    dh = w2t.T @ unpack_weight(dy_words, dy_scales, "e4m3")
    da = dh * f64(c) * d_relu(f64(a))
    dc = dh * relu(f64(a))
    out = np.zeros((K, T))
    out[:, idx] = by_expert(wat, mxq(da[:, idx], 0, "e4m3"), E1, C1)
    out[:, idx2] += by_expert(wbt, mxq(dc[:, idx2], 0, "e4m3"), E2, C2)
    return out

@@ -1,0 +1,266 @@
+from contextlib import ExitStack
+
+import concourse.mybir as mybir
+
+K, T, H, N = 512, 768, 512, 1024
+E1, C1, E2, C2 = 6, 128, 3, 256
+FLOPS = 2 * T * H * (N + 2 * K)
+
+F32 = mybir.dt.float32
+BF16 = mybir.dt.bfloat16
+I32 = mybir.dt.int32
+U32 = mybir.dt.uint32
+U16 = mybir.dt.uint16
+U8 = mybir.dt.uint8
+FP8X4 = mybir.dt.float8_e4m3fn_x4
+FP4X4 = mybir.dt.float4_e2m1fn_x4
+ALU = mybir.AluOpType
+COPY = mybir.ActivationFunctionType.Copy
+
+P = 128
+PACK = 4
+PASSES = N // (P * PACK)
+CHUNK = 256
+CHUNKS = T // CHUNK
+BLOCKS = K // P
+BANK = 512
+WIDE = 1024
+
+
+def tile_moe_plb_relu_kernel(
+    tc, dy_words, dy_scales, w2t_words, w2t_scales, wat_words, wat_scales, wbt_words, wbt_scales, a, c, offs, offs2, out
+):
+    nc = tc.nc
+    with ExitStack() as ctx:
+        keep = ctx.enter_context(tc.tile_pool(name="keep", bufs=1))
+        psum = ctx.enter_context(tc.psum_pool(name="psum", bufs=1))
+
+        def sbuf(shape, dtype, name, tag=None):
+            return keep.tile(shape, dtype, name=name, tag=tag or name, align_bytes=64)
+
+        def bank(index, name):
+            return psum.tile([P, BANK], F32, name=name, tag="bank%d" % index)
+
+        def load_scale_rows(plane, rows):
+            by_row = rows.rearrange("g (q r) w -> r q g w", r=4)
+            for r in range(4):
+                nc.sync.dma_start(out=plane[r:P:32, :, :].bitcast(I32), in_=by_row[r].bitcast(I32))
+
+        w2_scale_raw = sbuf([P, PASSES, H], U8, "w2_scale_raw")
+        dy_scale = sbuf([P, PASSES, T], U8, "dy_scale")
+        wb_scale = sbuf([P, E2, K], U8, "wb_scale")
+        wa_scale = sbuf([P, E1, K], U8, "wa_scale")
+        nc.vector.memset(w2_scale_raw[:].bitcast(I32), 0)
+        nc.vector.memset(dy_scale[:].bitcast(I32), 0)
+        nc.gpsimd.memset(wb_scale[:].bitcast(I32), 0)
+        nc.gpsimd.memset(wa_scale[:].bitcast(I32), 0)
+
+        w2_raw = sbuf([P, PASSES, H], I32, "w2_raw")
+        nc.sync.dma_start(out=w2_raw[:], in_=w2t_words.rearrange("s p i d -> p s (i d)").bitcast(I32))
+        load_scale_rows(w2_scale_raw, w2t_scales)
+        load_scale_rows(dy_scale, dy_scales)
+        dy_view = dy_words.rearrange("s p t d -> p s (t d)").bitcast(I32)
+        a_view = a.rearrange("(q r) t -> q r t", r=PACK)
+        c_view = c.rearrange("(q r) t -> q r t", r=PACK)
+        dy_codes, a_sb = [], []
+        for u in range(CHUNKS):
+            cols = slice(u * CHUNK, (u + 1) * CHUNK)
+            dy_codes.append(sbuf([P, PASSES, CHUNK], I32, "dy%d" % u))
+            a_sb.append(sbuf([P, PACK, CHUNK], F32, "a%d" % u))
+            nc.sync.dma_start(out=dy_codes[u][:], in_=dy_view[:, :, cols])
+            nc.sync.dma_start(out=a_sb[u][:], in_=a_view[:, :, cols])
+        list_b = sbuf([P, T // 16], U16, "list_b")
+        nc.sync.dma_start(list_b[:], offs2)
+        wb_codes = sbuf([P, E2, 2 * K], U8, "wb_codes")
+        nc.sync.dma_start(out=wb_codes[:].bitcast(I32), in_=wbt_words.rearrange("f s p w -> p (f s) w").bitcast(I32))
+        load_scale_rows(wb_scale, wbt_scales.rearrange("f s b k -> (f s) b k"))
+        c_sb = []
+        for j in range(PACK):
+            c_sb.append(sbuf([P, T], F32, "c%d" % j))
+            nc.sync.dma_start(out=c_sb[j][:], in_=c_view[:, j, :])
+        list_a = sbuf([P, T // 16], U16, "list_a")
+        nc.sync.dma_start(list_a[:], offs)
+        wa_codes = sbuf([P, E1, K], I32, "wa_codes")
+        nc.sync.dma_start(out=wa_codes[:], in_=wat_words.rearrange("e s p k d -> p (e s) (k d)").bitcast(I32))
+        load_scale_rows(wa_scale, wat_scales.rearrange("e s b k -> (e s) b k"))
+
+        w2_codes = sbuf([P, PASSES, H], I32, "w2_codes")
+        w2_scale = sbuf([P, PASSES, H], U8, "w2_scale")
+        nc.vector.tensor_copy(
+            out=w2_codes[:].rearrange("p s (j g m) -> p s g j m", j=PACK, m=4),
+            in_=w2_raw[:].rearrange("p s (g m j) -> p s g j m", j=PACK, m=4),
+        )
+        nc.vector.tensor_copy(
+            out=w2_scale[:].rearrange("p s (j g m) -> p s g j m", j=PACK, m=16),
+            in_=w2_scale_raw[:].rearrange("p s (g m j) -> p s g j m", j=PACK, m=16),
+        )
+
+        dc_pairs = sbuf([P, 2 * T], BF16, "dc_pairs")
+        dc_rows = sbuf([P, 2, T], BF16, "dc_rows")
+        live = [sbuf([P, PACK, CHUNK], F32, "live%d" % u) for u in range(CHUNKS)]
+        dh_sb = [sbuf([P, PACK, CHUNK], F32, "dh%d" % u) for u in range(CHUNKS)]
+        dh_live = sbuf([P, PACK, T], F32, "dh_live")
+        dh_banks = {}
+
+        def dh_product(u, half):
+            acc = bank(2 * u + half, "dh_bank")
+            dh_banks[u, half] = acc
+            for e in range(2):
+                j = 2 * half + e
+                for s in range(PASSES):
+                    nc.tensor.matmul_mx(
+                        out=acc[:, e * CHUNK : (e + 1) * CHUNK],
+                        lhsT=w2_codes[:, s, j * P : (j + 1) * P].bitcast(FP8X4),
+                        lhsT_scale=w2_scale[:, s, j * P : (j + 1) * P],
+                        rhs=dy_codes[u][:, s, :].bitcast(FP8X4),
+                        rhs_scale=dy_scale[:, s, u * CHUNK : (u + 1) * CHUNK],
+                        start=(s == 0),
+                        stop=(s == PASSES - 1),
+                    )
+
+        def make_dc(u, half):
+            acc = dh_banks[u, half][:].rearrange("p (e n) -> p e n", e=2)
+            rows = a_sb[u][:, 2 * half : 2 * half + 2, :]
+            if half == 0:
+                dst = dc_pairs[:, 2 * u * CHUNK : 2 * (u + 1) * CHUNK].rearrange("p (n e) -> p n e", e=2)
+                acc = acc.rearrange("p e n -> p n e")
+                rows = rows.rearrange("p e n -> p n e")
+            else:
+                dst = dc_rows[:, :, u * CHUNK : (u + 1) * CHUNK]
+            nc.vector.scalar_tensor_tensor(out=dst, in0=rows, scalar=0.0, in1=acc, op0=ALU.max, op1=ALU.mult)
+
+        def make_live(u):
+            nc.vector.tensor_scalar(out=live[u][:], in0=a_sb[u][:], scalar1=0.0, scalar2=None, op0=ALU.is_gt)
+
+        def keep_dh(u, half):
+            nc.scalar.copy(
+                out=dh_sb[u][:, 2 * half : 2 * half + 2, :].rearrange("p e n -> p (e n)"), in_=dh_banks[u, half][:]
+            )
+
+        def mask_dh(u):
+            nc.gpsimd.tensor_tensor(
+                out=dh_live[:, :, u * CHUNK : (u + 1) * CHUNK], in0=dh_sb[u][:], in1=live[u][:], op=ALU.mult
+            )
+
+        def slots_of(lst, first, count):
+            return lst[:, first // 16 : (first + count) // 16]
+
+        def gather_row(dst, j, window, offsets):
+            nc.scalar.activation(dst[:].rearrange("p (n j) -> p n j", j=PACK)[:, :, j], window.indirect(offsets), COPY)
+
+        def gather_pair(dst, offsets):
+            words = dst[:].bitcast(U32).rearrange("p (n h) -> p n h", h=2)[:, :, 0]
+            nc.vector.tensor_copy(words, dc_pairs[:].bitcast(U32).indirect(offsets))
+
+        def quantize(src, count, name):
+            codes = sbuf([P, count], U32, name + "_codes")
+            scale = sbuf([P, count], U8, name + "_scale")
+            nc.vector.quantize_mx(out=codes[:].bitcast(FP8X4), scales=scale[:], in_=src[:])
+            return codes, scale
+
+        def product_b(dst, f, b, codes, scale, cols):
+            nc.tensor.matmul_mx(
+                out=dst,
+                lhsT=wb_codes[:, f, 2 * b * P : 2 * (b + 1) * P].bitcast(FP4X4),
+                lhsT_scale=wb_scale[:, f, b * P : (b + 1) * P],
+                rhs=codes[:, cols].bitcast(FP8X4),
+                rhs_scale=scale[:, cols],
+                start=True,
+                stop=True,
+            )
+
+        for u in range(CHUNKS):
+            for half in (1, 0):
+                dh_product(u, half)
+                make_dc(u, half)
+                if u < CHUNKS - 1:
+                    keep_dh(u, half)
+            if u < CHUNKS - 1:
+                make_live(u)
+                mask_dh(u)
+        last = CHUNKS - 1
+
+        head, rest = C2, T - C2
+        head_slots, rest_slots = slots_of(list_b, 0, head), slots_of(list_b, head, rest)
+        dc_head = sbuf([P, head * PACK], BF16, "dc_head")
+        dc_rest = sbuf([P, rest * PACK], BF16, "dc_rest")
+        for e in range(2):
+            gather_row(dc_head, 2 + e, dc_rows[:, e, :], head_slots)
+        gather_pair(dc_head, head_slots)
+        head_codes, head_scale = quantize(dc_head, head, "dc_head")
+        gather_pair(dc_rest, rest_slots)
+        make_live(last)
+        for half in (1, 0):
+            keep_dh(last, half)
+        mask_dh(last)
+
+        q_tok = [sbuf([P, T], F32, "q_tok%d" % b) for b in range(BLOCKS)]
+        q_head = [sbuf([P, head], F32, "q_head%d" % b) for b in range(BLOCKS)]
+        head_banks = [bank(2 * CHUNKS + g, "head_bank") for g in range(2)]
+        for b in range(BLOCKS):
+            product_b(head_banks[b // 2][:, (b % 2) * head : (b % 2 + 1) * head], 0, b, head_codes, head_scale, slice(0, head))
+
+        def scatter_head(b):
+            nc.scalar.copy(out=q_head[b][:], in_=head_banks[b // 2][:, (b % 2) * head : (b % 2 + 1) * head])
+            nc.vector.tensor_copy(q_tok[b][:].indirect(head_slots), q_head[b][:])
+
+        for b in range(BLOCKS - 1):
+            scatter_head(b)
+        for e in range(2):
+            gather_row(dc_rest, 2 + e, dc_rows[:, e, :], rest_slots)
+        rest_codes, rest_scale = quantize(dc_rest, rest, "dc_rest")
+        scatter_head(BLOCKS - 1)
+
+        rest_banks = []
+        for b in range(BLOCKS):
+            rest_banks.append(bank(b, "rest_bank"))
+            for f in range(1, E2):
+                cols = slice((f - 1) * C2, f * C2)
+                product_b(rest_banks[b][:, cols], f, b, rest_codes, rest_scale, cols)
+
+        def scatter_rest(b, tag=None):
+            q_rest = sbuf([P, rest], F32, "q_rest%d" % b, tag)
+            nc.scalar.copy(out=q_rest[:], in_=rest_banks[b][:])
+            nc.vector.tensor_copy(q_tok[b][:].indirect(rest_slots), q_rest[:])
+
+        for b in range(BLOCKS - 1):
+            scatter_rest(b)
+
+        pieces = [(0, BANK), (BANK, T - BANK)]
+        da_slots = [sbuf([P, count * PACK], BF16, "da_slots%d" % first) for first, count in pieces]
+        for j in range(PACK):
+            da_row = sbuf([P, T], BF16, "da_row%d" % j)
+            nc.gpsimd.tensor_tensor(out=da_row[:], in0=dh_live[:, j, :], in1=c_sb[j][:], op=ALU.mult)
+            for (first, count), dst in zip(pieces, da_slots):
+                gather_row(dst, j, da_row[:], slots_of(list_a, first, count))
+        da_q = [quantize(src, count, "da%d" % first) for (first, count), src in zip(pieces, da_slots)]
+        scatter_rest(BLOCKS - 1, "c%d" % (PACK - 1))
+
+        for b in range(BLOCKS):
+            r_slots = sbuf([P, T], F32, "r_slots%d" % b)
+            for g, (first, count) in enumerate(pieces):
+                acc = bank((4 + 2 * b + g) % 8, "r_bank")
+                codes, scale = da_q[g]
+                for e in range(first // C1, (first + count) // C1):
+                    cols = slice(e * C1 - first, (e + 1) * C1 - first)
+                    nc.tensor.matmul_mx(
+                        out=acc[:, cols],
+                        lhsT=wa_codes[:, e, b * P : (b + 1) * P].bitcast(FP8X4),
+                        lhsT_scale=wa_scale[:, e, b * P : (b + 1) * P],
+                        rhs=codes[:, cols].bitcast(FP8X4),
+                        rhs_scale=scale[:, cols],
+                        start=True,
+                        stop=True,
+                    )
+                nc.scalar.copy(out=r_slots[:, first : first + count], in_=acc[:, :count])
+            r_tok = sbuf([P, WIDE], F32, "r_tok%d" % b)
+            nc.vector.tensor_copy(r_tok[:].indirect(list_a[:]), r_slots[:])
+            total = sbuf([P, T], F32, "total%d" % b)
+            rows = slice(b * P, (b + 1) * P)
+            if b < BLOCKS - 1:
+                nc.gpsimd.tensor_tensor(out=total[:], in0=r_tok[:, :T], in1=q_tok[b][:], op=ALU.add)
+                nc.sync.dma_start(out=out[rows, :], in_=total[:])
+            else:
+                for queue, cols in ((nc.sync, slice(0, T // 2)), (nc.scalar, slice(T // 2, T))):
+                    nc.vector.tensor_tensor(out=total[:, cols], in0=r_tok[:, cols], in1=q_tok[b][:, cols], op=ALU.add)
+                    queue.dma_start(out=out[rows, cols], in_=total[:, cols])

@@ -16,6 +16,7 @@ FP8X4 = mybir.dt.float8_e4m3fn_x4
 FP4X4 = mybir.dt.float4_e2m1fn_x4
 ALU = mybir.AluOpType
 COPY = mybir.ActivationFunctionType.Copy
+SIGN = mybir.ActivationFunctionType.Sign
 
 P = 128
 PACK = 4
@@ -50,8 +51,8 @@ def tile_moe_plb_relu_kernel(
         dy_scale = sbuf([P, PASSES, T], U8, "dy_scale")
         wb_scale = sbuf([P, E2, K], U8, "wb_scale")
         wa_scale = sbuf([P, E1, K], U8, "wa_scale")
-        nc.vector.memset(w2_scale_raw[:].bitcast(I32), 0)
-        nc.vector.memset(dy_scale[:].bitcast(I32), 0)
+        nc.gpsimd.memset(w2_scale_raw[:].bitcast(I32), 0)
+        nc.gpsimd.memset(dy_scale[:].bitcast(I32), 0)
         nc.gpsimd.memset(wb_scale[:].bitcast(I32), 0)
         nc.gpsimd.memset(wa_scale[:].bitcast(I32), 0)
 
@@ -62,13 +63,22 @@ def tile_moe_plb_relu_kernel(
         dy_view = dy_words.rearrange("s p t d -> p s (t d)").bitcast(I32)
         a_view = a.rearrange("(q r) t -> q r t", r=PACK)
         c_view = c.rearrange("(q r) t -> q r t", r=PACK)
-        dy_codes, a_sb = [], []
-        for u in range(CHUNKS):
-            cols = slice(u * CHUNK, (u + 1) * CHUNK)
-            dy_codes.append(sbuf([P, PASSES, CHUNK], I32, "dy%d" % u))
-            a_sb.append(sbuf([P, PACK, CHUNK], F32, "a%d" % u))
-            nc.sync.dma_start(out=dy_codes[u][:], in_=dy_view[:, :, cols])
-            nc.sync.dma_start(out=a_sb[u][:], in_=a_view[:, :, cols])
+        dy_codes = [sbuf([P, PASSES, CHUNK], I32, "dy%d" % u) for u in range(CHUNKS)]
+        a_sb = [sbuf([P, PACK, CHUNK], F32, "a%d" % u) for u in range(CHUNKS)]
+
+        def load_dy(u):
+            nc.sync.dma_start(out=dy_codes[u][:], in_=dy_view[:, :, u * CHUNK : (u + 1) * CHUNK])
+
+        def load_a(u, rows):
+            nc.sync.dma_start(out=a_sb[u][:, rows, :], in_=a_view[:, rows, u * CHUNK : (u + 1) * CHUNK])
+
+        load_dy(0)
+        load_a(0, slice(0, PACK))
+        load_dy(1)
+        load_dy(2)
+        load_a(1, slice(0, PACK))
+        load_a(2, slice(2, PACK))
+        load_a(2, slice(0, 2))
         list_b = sbuf([P, T // 16], U16, "list_b")
         nc.sync.dma_start(list_b[:], offs2)
         wb_codes = sbuf([P, E2, 2 * K], U8, "wb_codes")
@@ -97,8 +107,6 @@ def tile_moe_plb_relu_kernel(
 
         dc_pairs = sbuf([P, 2 * T], BF16, "dc_pairs")
         dc_rows = sbuf([P, 2, T], BF16, "dc_rows")
-        live = [sbuf([P, PACK, CHUNK], F32, "live%d" % u) for u in range(CHUNKS)]
-        dh_sb = [sbuf([P, PACK, CHUNK], F32, "dh%d" % u) for u in range(CHUNKS)]
         dh_live = sbuf([P, PACK, T], F32, "dh_live")
         dh_banks = {}
 
@@ -129,18 +137,35 @@ def tile_moe_plb_relu_kernel(
                 dst = dc_rows[:, :, u * CHUNK : (u + 1) * CHUNK]
             nc.vector.scalar_tensor_tensor(out=dst, in0=rows, scalar=0.0, in1=acc, op0=ALU.max, op1=ALU.mult)
 
+        def mask_dh(u, half):
+            rows = slice(2 * half, 2 * half + 2)
+            nc.vector.scalar_tensor_tensor(
+                out=dh_live[:, rows, u * CHUNK : (u + 1) * CHUNK],
+                in0=a_sb[u][:, rows, :],
+                scalar=0.0,
+                in1=dh_banks[u, half][:].rearrange("p (e n) -> p e n", e=2),
+                op0=ALU.is_gt,
+                op1=ALU.mult,
+            )
+
         def make_live(u):
-            nc.vector.tensor_scalar(out=live[u][:], in0=a_sb[u][:], scalar1=0.0, scalar2=None, op0=ALU.is_gt)
+            signs = sbuf([P, PACK * CHUNK], F32, "signs%d" % u)
+            live = sbuf([P, PACK * CHUNK], F32, "live%d" % u)
+            nc.scalar.activation(signs[:], a_sb[u][:].rearrange("p j n -> p (j n)"), SIGN)
+            nc.gpsimd.tensor_scalar(out=live[:], in0=signs[:], scalar1=1.0, scalar2=0.0, op0=ALU.min, op1=ALU.max)
+            return live
 
-        def keep_dh(u, half):
-            nc.scalar.copy(
-                out=dh_sb[u][:, 2 * half : 2 * half + 2, :].rearrange("p e n -> p (e n)"), in_=dh_banks[u, half][:]
-            )
-
-        def mask_dh(u):
-            nc.gpsimd.tensor_tensor(
-                out=dh_live[:, :, u * CHUNK : (u + 1) * CHUNK], in0=dh_sb[u][:], in1=live[u][:], op=ALU.mult
-            )
+        def mask_dh_aside(u, live, tag=None):
+            kept = sbuf([P, PACK * CHUNK], F32, "dh%d" % u, tag)
+            for half in (1, 0):
+                cols = slice(half * BANK, (half + 1) * BANK)
+                nc.scalar.copy(out=kept[:, cols], in_=dh_banks[u, half][:])
+                nc.gpsimd.tensor_tensor(
+                    out=dh_live[:, 2 * half : 2 * half + 2, u * CHUNK : (u + 1) * CHUNK],
+                    in0=kept[:, cols].rearrange("p (e n) -> p e n", e=2),
+                    in1=live[:, cols].rearrange("p (e n) -> p e n", e=2),
+                    op=ALU.mult,
+                )
 
         def slots_of(lst, first, count):
             return lst[:, first // 16 : (first + count) // 16]
@@ -173,12 +198,8 @@ def tile_moe_plb_relu_kernel(
             for half in (1, 0):
                 dh_product(u, half)
                 make_dc(u, half)
-                if u < CHUNKS - 1:
-                    keep_dh(u, half)
-            if u < CHUNKS - 1:
-                make_live(u)
-                mask_dh(u)
-        last = CHUNKS - 1
+        mask_dh_aside(0, make_live(0))
+        live_second = make_live(1)
 
         head, rest = C2, T - C2
         head_slots, rest_slots = slots_of(list_b, 0, head), slots_of(list_b, head, rest)
@@ -189,10 +210,9 @@ def tile_moe_plb_relu_kernel(
         gather_pair(dc_head, head_slots)
         head_codes, head_scale = quantize(dc_head, head, "dc_head")
         gather_pair(dc_rest, rest_slots)
-        make_live(last)
+        mask_dh_aside(1, live_second, "dc_head")
         for half in (1, 0):
-            keep_dh(last, half)
-        mask_dh(last)
+            mask_dh(2, half)
 
         q_tok = [sbuf([P, T], F32, "q_tok%d" % b) for b in range(BLOCKS)]
         q_head = [sbuf([P, head], F32, "q_head%d" % b) for b in range(BLOCKS)]
@@ -229,7 +249,7 @@ def tile_moe_plb_relu_kernel(
         pieces = [(0, BANK), (BANK, T - BANK)]
         da_slots = [sbuf([P, count * PACK], BF16, "da_slots%d" % first) for first, count in pieces]
         for j in range(PACK):
-            da_row = sbuf([P, T], BF16, "da_row%d" % j)
+            da_row = sbuf([P, T], BF16, "da_row%d" % j, "dc_rest" if j == 2 else None)
             nc.gpsimd.tensor_tensor(out=da_row[:], in0=dh_live[:, j, :], in1=c_sb[j][:], op=ALU.mult)
             for (first, count), dst in zip(pieces, da_slots):
                 gather_row(dst, j, da_row[:], slots_of(list_a, first, count))

@@ -75,12 +75,12 @@ def tile_moe_plb_relu_kernel(
         load_dy(0)
         load_a(0, slice(0, PACK))
         load_dy(1)
-        load_dy(2)
-        load_a(1, slice(0, PACK))
-        load_a(2, slice(2, PACK))
-        load_a(2, slice(0, 2))
         list_b = sbuf([P, T // 16], U16, "list_b")
         nc.sync.dma_start(list_b[:], offs2)
+        load_dy(2)
+        for rows in (slice(2, PACK), slice(0, 2)):
+            load_a(1, rows)
+            load_a(2, rows)
         wb_codes = sbuf([P, E2, 2 * K], U8, "wb_codes")
         nc.sync.dma_start(out=wb_codes[:].bitcast(I32), in_=wbt_words.rearrange("f s p w -> p (f s) w").bitcast(I32))
         load_scale_rows(wb_scale, wbt_scales.rearrange("f s b k -> (f s) b k"))
@@ -148,8 +148,8 @@ def tile_moe_plb_relu_kernel(
                 op1=ALU.mult,
             )
 
-        def make_live(u):
-            signs = sbuf([P, PACK * CHUNK], F32, "signs%d" % u)
+        def make_live(u, tag=None):
+            signs = sbuf([P, PACK * CHUNK], F32, "signs%d" % u, tag)
             live = sbuf([P, PACK * CHUNK], F32, "live%d" % u)
             nc.scalar.activation(signs[:], a_sb[u][:].rearrange("p j n -> p (j n)"), SIGN)
             nc.gpsimd.tensor_scalar(out=live[:], in0=signs[:], scalar1=1.0, scalar2=0.0, op0=ALU.min, op1=ALU.max)
@@ -194,12 +194,10 @@ def tile_moe_plb_relu_kernel(
                 stop=True,
             )
 
-        for u in range(CHUNKS):
-            for half in (1, 0):
-                dh_product(u, half)
-                make_dc(u, half)
+        for u, half in ((0, 1), (0, 0), (1, 1), (2, 1), (1, 0), (2, 0)):
+            dh_product(u, half)
+            make_dc(u, half)
         mask_dh_aside(0, make_live(0))
-        live_second = make_live(1)
 
         head, rest = C2, T - C2
         head_slots, rest_slots = slots_of(list_b, 0, head), slots_of(list_b, head, rest)
@@ -210,9 +208,8 @@ def tile_moe_plb_relu_kernel(
         gather_pair(dc_head, head_slots)
         head_codes, head_scale = quantize(dc_head, head, "dc_head")
         gather_pair(dc_rest, rest_slots)
-        mask_dh_aside(1, live_second, "dc_head")
-        for half in (1, 0):
-            mask_dh(2, half)
+        for u, half in ((1, 1), (2, 1), (1, 0), (2, 0)):
+            mask_dh(u, half)
 
         q_tok = [sbuf([P, T], F32, "q_tok%d" % b) for b in range(BLOCKS)]
         q_head = [sbuf([P, head], F32, "q_head%d" % b) for b in range(BLOCKS)]
@@ -233,7 +230,7 @@ def tile_moe_plb_relu_kernel(
 
         rest_banks = []
         for b in range(BLOCKS):
-            rest_banks.append(bank(b, "rest_bank"))
+            rest_banks.append(bank((0, 1, 4, 5)[b], "rest_bank"))
             for f in range(1, E2):
                 cols = slice((f - 1) * C2, f * C2)
                 product_b(rest_banks[b][:, cols], f, b, rest_codes, rest_scale, cols)
@@ -248,18 +245,19 @@ def tile_moe_plb_relu_kernel(
 
         pieces = [(0, BANK), (BANK, T - BANK)]
         da_slots = [sbuf([P, count * PACK], BF16, "da_slots%d" % first) for first, count in pieces]
+        da_rows = sbuf([P, PACK * T], BF16, "da_rows", "dc_rest")
         for j in range(PACK):
-            da_row = sbuf([P, T], BF16, "da_row%d" % j, "dc_rest" if j == 2 else None)
-            nc.gpsimd.tensor_tensor(out=da_row[:], in0=dh_live[:, j, :], in1=c_sb[j][:], op=ALU.mult)
+            da_row = da_rows[:, j * T : (j + 1) * T]
+            nc.gpsimd.tensor_tensor(out=da_row, in0=dh_live[:, j, :], in1=c_sb[j][:], op=ALU.mult)
             for (first, count), dst in zip(pieces, da_slots):
-                gather_row(dst, j, da_row[:], slots_of(list_a, first, count))
+                gather_row(dst, j, da_row, slots_of(list_a, first, count))
         da_q = [quantize(src, count, "da%d" % first) for (first, count), src in zip(pieces, da_slots)]
         scatter_rest(BLOCKS - 1, "c%d" % (PACK - 1))
 
         for b in range(BLOCKS):
             r_slots = sbuf([P, T], F32, "r_slots%d" % b)
             for g, (first, count) in enumerate(pieces):
-                acc = bank((4 + 2 * b + g) % 8, "r_bank")
+                acc = bank((2, 3, 6, 7, 0, 1, 4, 2)[2 * b + g], "r_bank")
                 codes, scale = da_q[g]
                 for e in range(first // C1, (first + count) // C1):
                     cols = slice(e * C1 - first, (e + 1) * C1 - first)

@@ -170,11 +170,10 @@ def tile_moe_plb_relu_kernel(
         def slots_of(lst, first, count):
             return lst[:, first // 16 : (first + count) // 16]
 
-        def gather_row(dst, j, window, offsets):
-            nc.scalar.activation(dst[:].rearrange("p (n j) -> p n j", j=PACK)[:, :, j], window.indirect(offsets), COPY)
+        def gather_row(dst, place, step, window, offsets):
+            nc.scalar.activation(dst.rearrange("p (n j) -> p n j", j=step)[:, :, place], window.indirect(offsets), COPY)
 
-        def gather_pair(dst, offsets):
-            words = dst[:].bitcast(U32).rearrange("p (n h) -> p n h", h=2)[:, :, 0]
+        def gather_pair(words, offsets):
             nc.vector.tensor_copy(words, dc_pairs[:].bitcast(U32).indirect(offsets))
 
         def quantize(src, count, name):
@@ -204,10 +203,11 @@ def tile_moe_plb_relu_kernel(
         dc_head = sbuf([P, head * PACK], BF16, "dc_head")
         dc_rest = sbuf([P, rest * PACK], BF16, "dc_rest")
         for e in range(2):
-            gather_row(dc_head, 2 + e, dc_rows[:, e, :], head_slots)
-        gather_pair(dc_head, head_slots)
+            gather_row(dc_head[:], 2 + e, PACK, dc_rows[:, e, :], head_slots)
+        gather_pair(dc_head[:].bitcast(U32).rearrange("p (n h) -> p n h", h=2)[:, :, 0], head_slots)
         head_codes, head_scale = quantize(dc_head, head, "dc_head")
-        gather_pair(dc_rest, rest_slots)
+        rest_halves = sbuf([P, rest * PACK], BF16, "rest_halves")
+        gather_pair(rest_halves[:, : 2 * rest].bitcast(U32), rest_slots)
         for u, half in ((1, 1), (2, 1), (1, 0), (2, 0)):
             mask_dh(u, half)
 
@@ -224,7 +224,11 @@ def tile_moe_plb_relu_kernel(
         for b in range(BLOCKS - 1):
             scatter_head(b)
         for e in range(2):
-            gather_row(dc_rest, 2 + e, dc_rows[:, e, :], rest_slots)
+            gather_row(rest_halves[:, 2 * rest :], e, 2, dc_rows[:, e, :], rest_slots)
+        nc.scalar.copy(
+            out=dc_rest[:].bitcast(U32).rearrange("p (n h) -> p n h", h=2),
+            in_=rest_halves[:].bitcast(U32).rearrange("p (h n) -> p n h", h=2),
+        )
         rest_codes, rest_scale = quantize(dc_rest, rest, "dc_rest")
         scatter_head(BLOCKS - 1)
 
@@ -250,7 +254,7 @@ def tile_moe_plb_relu_kernel(
             da_row = da_rows[:, j * T : (j + 1) * T]
             nc.gpsimd.tensor_tensor(out=da_row, in0=dh_live[:, j, :], in1=c_sb[j][:], op=ALU.mult)
             for (first, count), dst in zip(pieces, da_slots):
-                gather_row(dst, j, da_row, slots_of(list_a, first, count))
+                gather_row(dst[:], j, PACK, da_row, slots_of(list_a, first, count))
         da_q = [quantize(src, count, "da%d" % first) for (first, count), src in zip(pieces, da_slots)]
         scatter_rest(BLOCKS - 1, "c%d" % (PACK - 1))
 

@@ -21,11 +21,19 @@ SIGN = mybir.ActivationFunctionType.Sign
 P = 128
 PACK = 4
 PASSES = N // (P * PACK)
-CHUNK = 256
+PAIR = 2
+HALVES = PACK // PAIR
+BANK = 512
+BANKS = 8
+CHUNK = BANK // PAIR
 CHUNKS = T // CHUNK
 BLOCKS = K // P
-BANK = 512
+STRIPE = 16
+QUADRANT = 32
+SCALE_ROWS = 4
+LINE = 16
 WIDE = 1024
+ASIDE = 2
 
 
 def tile_moe_plb_relu_kernel(
@@ -42,10 +50,16 @@ def tile_moe_plb_relu_kernel(
         def bank(index, name):
             return psum.tile([P, BANK], F32, name=name, tag="bank%d" % index)
 
-        def load_scale_rows(plane, rows):
-            by_row = rows.rearrange("g (q r) w -> r q g w", r=4)
-            for r in range(4):
-                nc.sync.dma_start(out=plane[r:P:32, :, :].bitcast(I32), in_=by_row[r].bitcast(I32))
+        def load_scale_rows(scale, source):
+            by_row = source.rearrange("m (g r) w -> r g m w", r=SCALE_ROWS)
+            for r in range(SCALE_ROWS):
+                nc.sync.dma_start(out=scale[r:P:QUADRANT, :, :].bitcast(I32), in_=by_row[r].bitcast(I32))
+
+        def tokens_of(u):
+            return slice(u * CHUNK, (u + 1) * CHUNK)
+
+        def rows_of(half):
+            return slice(PAIR * half, PAIR * (half + 1))
 
         w2_scale_raw = sbuf([P, PASSES, H], U8, "w2_scale_raw")
         dy_scale = sbuf([P, PASSES, T], U8, "dy_scale")
@@ -59,28 +73,16 @@ def tile_moe_plb_relu_kernel(
         w2_raw = sbuf([P, PASSES, H], I32, "w2_raw")
         nc.sync.dma_start(out=w2_raw[:], in_=w2t_words.rearrange("s p i d -> p s (i d)").bitcast(I32))
         load_scale_rows(w2_scale_raw, w2t_scales)
+        dy_codes = sbuf([P, PASSES, T], I32, "dy_codes")
+        nc.sync.dma_start(out=dy_codes[:], in_=dy_words.rearrange("s p t d -> p s (t d)").bitcast(I32))
         load_scale_rows(dy_scale, dy_scales)
-        dy_view = dy_words.rearrange("s p t d -> p s (t d)").bitcast(I32)
-        a_view = a.rearrange("(q r) t -> q r t", r=PACK)
-        c_view = c.rearrange("(q r) t -> q r t", r=PACK)
-        dy_codes = [sbuf([P, PASSES, CHUNK], I32, "dy%d" % u) for u in range(CHUNKS)]
-        a_sb = [sbuf([P, PACK, CHUNK], F32, "a%d" % u) for u in range(CHUNKS)]
-
-        def load_dy(u):
-            nc.sync.dma_start(out=dy_codes[u][:], in_=dy_view[:, :, u * CHUNK : (u + 1) * CHUNK])
-
-        def load_a(u, rows):
-            nc.sync.dma_start(out=a_sb[u][:, rows, :], in_=a_view[:, rows, u * CHUNK : (u + 1) * CHUNK])
-
-        load_dy(0)
-        load_a(0, slice(0, PACK))
-        load_dy(1)
-        list_b = sbuf([P, T // 16], U16, "list_b")
+        a_view = a.rearrange("(p j) t -> p j t", j=PACK)
+        c_view = c.rearrange("(p j) t -> p j t", j=PACK)
+        a_sb = [sbuf([P, PAIR, T], F32, "a%d" % half) for half in range(HALVES)]
+        list_b = sbuf([P, T // STRIPE], U16, "list_b")
+        nc.sync.dma_start(out=a_sb[1][:], in_=a_view[:, rows_of(1), :])
         nc.sync.dma_start(list_b[:], offs2)
-        load_dy(2)
-        for rows in (slice(2, PACK), slice(0, 2)):
-            load_a(1, rows)
-            load_a(2, rows)
+        nc.sync.dma_start(out=a_sb[0][:], in_=a_view[:, rows_of(0), :])
         wb_codes = sbuf([P, E2, 2 * K], U8, "wb_codes")
         nc.sync.dma_start(out=wb_codes[:].bitcast(I32), in_=wbt_words.rearrange("f s p w -> p (f s) w").bitcast(I32))
         load_scale_rows(wb_scale, wbt_scales.rearrange("f s b k -> (f s) b k"))
@@ -88,7 +90,7 @@ def tile_moe_plb_relu_kernel(
         for j in range(PACK):
             c_sb.append(sbuf([P, T], F32, "c%d" % j))
             nc.sync.dma_start(out=c_sb[j][:], in_=c_view[:, j, :])
-        list_a = sbuf([P, T // 16], U16, "list_a")
+        list_a = sbuf([P, T // STRIPE], U16, "list_a")
         nc.sync.dma_start(list_a[:], offs)
         wa_codes = sbuf([P, E1, K], I32, "wa_codes")
         nc.sync.dma_start(out=wa_codes[:], in_=wat_words.rearrange("e s p k d -> p (e s) (k d)").bitcast(I32))
@@ -97,78 +99,73 @@ def tile_moe_plb_relu_kernel(
         w2_codes = sbuf([P, PASSES, H], I32, "w2_codes")
         w2_scale = sbuf([P, PASSES, H], U8, "w2_scale")
         nc.vector.tensor_copy(
-            out=w2_codes[:].rearrange("p s (j g m) -> p s g j m", j=PACK, m=4),
-            in_=w2_raw[:].rearrange("p s (g m j) -> p s g j m", j=PACK, m=4),
+            out=w2_codes[:].rearrange("p s (j g m) -> p s g j m", j=PACK, m=LINE // PACK),
+            in_=w2_raw[:].rearrange("p s (g m j) -> p s g j m", j=PACK, m=LINE // PACK),
         )
         nc.vector.tensor_copy(
-            out=w2_scale[:].rearrange("p s (j g m) -> p s g j m", j=PACK, m=16),
-            in_=w2_scale_raw[:].rearrange("p s (g m j) -> p s g j m", j=PACK, m=16),
+            out=w2_scale[:].rearrange("p s (j g m) -> p s g j m", j=PACK, m=LINE),
+            in_=w2_scale_raw[:].rearrange("p s (g m j) -> p s g j m", j=PACK, m=LINE),
         )
 
-        dc_pairs = sbuf([P, 2 * T], BF16, "dc_pairs")
-        dc_rows = sbuf([P, 2, T], BF16, "dc_rows")
+        dc_pairs = sbuf([P, PAIR * T], BF16, "dc_pairs")
+        dc_rows = sbuf([P, PAIR, T], BF16, "dc_rows")
         dh_live = sbuf([P, PACK, T], F32, "dh_live")
         dh_banks = {}
 
         def dh_product(u, half):
-            acc = bank(2 * u + half, "dh_bank")
+            acc = bank(HALVES * u + half, "dh_bank")
             dh_banks[u, half] = acc
-            for e in range(2):
-                j = 2 * half + e
+            for e in range(PAIR):
+                j = PAIR * half + e
                 for s in range(PASSES):
                     nc.tensor.matmul_mx(
                         out=acc[:, e * CHUNK : (e + 1) * CHUNK],
                         lhsT=w2_codes[:, s, j * P : (j + 1) * P].bitcast(FP8X4),
                         lhsT_scale=w2_scale[:, s, j * P : (j + 1) * P],
-                        rhs=dy_codes[u][:, s, :].bitcast(FP8X4),
-                        rhs_scale=dy_scale[:, s, u * CHUNK : (u + 1) * CHUNK],
+                        rhs=dy_codes[:, s, tokens_of(u)].bitcast(FP8X4),
+                        rhs_scale=dy_scale[:, s, tokens_of(u)],
                         start=(s == 0),
                         stop=(s == PASSES - 1),
                     )
 
+        def dh_rows(u, half):
+            return dh_banks[u, half][:].rearrange("p (e n) -> p e n", e=PAIR)
+
         def make_dc(u, half):
-            acc = dh_banks[u, half][:].rearrange("p (e n) -> p e n", e=2)
-            rows = a_sb[u][:, 2 * half : 2 * half + 2, :]
+            dh_in = dh_rows(u, half)
+            a_in = a_sb[half][:, :, tokens_of(u)]
             if half == 0:
-                dst = dc_pairs[:, 2 * u * CHUNK : 2 * (u + 1) * CHUNK].rearrange("p (n e) -> p n e", e=2)
-                acc = acc.rearrange("p e n -> p n e")
-                rows = rows.rearrange("p e n -> p n e")
+                dst = dc_pairs[:, PAIR * u * CHUNK : PAIR * (u + 1) * CHUNK].rearrange("p (n e) -> p n e", e=PAIR)
+                dh_in = dh_in.rearrange("p e n -> p n e")
+                a_in = a_in.rearrange("p e n -> p n e")
             else:
-                dst = dc_rows[:, :, u * CHUNK : (u + 1) * CHUNK]
-            nc.vector.scalar_tensor_tensor(out=dst, in0=rows, scalar=0.0, in1=acc, op0=ALU.max, op1=ALU.mult)
+                dst = dc_rows[:, :, tokens_of(u)]
+            nc.vector.scalar_tensor_tensor(out=dst, in0=a_in, scalar=0.0, in1=dh_in, op0=ALU.max, op1=ALU.mult)
 
         def mask_dh(u, half):
-            rows = slice(2 * half, 2 * half + 2)
             nc.vector.scalar_tensor_tensor(
-                out=dh_live[:, rows, u * CHUNK : (u + 1) * CHUNK],
-                in0=a_sb[u][:, rows, :],
+                out=dh_live[:, rows_of(half), tokens_of(u)],
+                in0=a_sb[half][:, :, tokens_of(u)],
                 scalar=0.0,
-                in1=dh_banks[u, half][:].rearrange("p (e n) -> p e n", e=2),
+                in1=dh_rows(u, half),
                 op0=ALU.is_gt,
                 op1=ALU.mult,
             )
 
-        def make_live(u, tag=None):
-            signs = sbuf([P, PACK * CHUNK], F32, "signs%d" % u, tag)
-            live = sbuf([P, PACK * CHUNK], F32, "live%d" % u)
-            nc.scalar.activation(signs[:], a_sb[u][:].rearrange("p j n -> p (j n)"), SIGN)
+        def make_live(u, half):
+            signs = sbuf([P, PAIR, CHUNK], F32, "signs%d" % u)
+            live = sbuf([P, PAIR, CHUNK], F32, "live%d" % u)
+            nc.scalar.activation(signs[:], a_sb[half][:, :, tokens_of(u)], SIGN)
             nc.gpsimd.tensor_scalar(out=live[:], in0=signs[:], scalar1=1.0, scalar2=0.0, op0=ALU.min, op1=ALU.max)
             return live
 
-        def mask_dh_aside(u, live, tag=None):
-            kept = sbuf([P, PACK * CHUNK], F32, "dh%d" % u, tag)
-            for half in (1, 0):
-                cols = slice(half * BANK, (half + 1) * BANK)
-                nc.scalar.copy(out=kept[:, cols], in_=dh_banks[u, half][:])
-                nc.gpsimd.tensor_tensor(
-                    out=dh_live[:, 2 * half : 2 * half + 2, u * CHUNK : (u + 1) * CHUNK],
-                    in0=kept[:, cols].rearrange("p (e n) -> p e n", e=2),
-                    in1=live[:, cols].rearrange("p (e n) -> p e n", e=2),
-                    op=ALU.mult,
-                )
+        def mask_dh_aside(u, half, live):
+            kept = sbuf([P, PAIR, CHUNK], F32, "dh%d" % u)
+            nc.scalar.copy(out=kept[:], in_=dh_rows(u, half))
+            nc.gpsimd.tensor_tensor(out=dh_live[:, rows_of(half), tokens_of(u)], in0=kept[:], in1=live[:], op=ALU.mult)
 
-        def slots_of(lst, first, count):
-            return lst[:, first // 16 : (first + count) // 16]
+        def slots_of(slot_list, first, count):
+            return slot_list[:, first // STRIPE : (first + count) // STRIPE]
 
         def gather_row(dst, place, step, window, offsets):
             nc.scalar.activation(dst.rearrange("p (n j) -> p n j", j=step)[:, :, place], window.indirect(offsets), COPY)
@@ -193,48 +190,56 @@ def tile_moe_plb_relu_kernel(
                 stop=True,
             )
 
-        for u, half in ((0, 1), (0, 0), (1, 1), (2, 1), (1, 0), (2, 0)):
+        order = [(u, half) for half in reversed(range(HALVES)) for u in range(CHUNKS)]
+        lives = [make_live(u, half) for u, half in order[:ASIDE]]
+        for u, half in order:
             dh_product(u, half)
             make_dc(u, half)
-        mask_dh_aside(0, make_live(0))
+        for (u, half), live in zip(order, lives):
+            mask_dh_aside(u, half, live)
 
         head, rest = C2, T - C2
         head_slots, rest_slots = slots_of(list_b, 0, head), slots_of(list_b, head, rest)
         dc_head = sbuf([P, head * PACK], BF16, "dc_head")
         dc_rest = sbuf([P, rest * PACK], BF16, "dc_rest")
-        for e in range(2):
-            gather_row(dc_head[:], 2 + e, PACK, dc_rows[:, e, :], head_slots)
-        gather_pair(dc_head[:].bitcast(U32).rearrange("p (n h) -> p n h", h=2)[:, :, 0], head_slots)
+        for e in range(PAIR):
+            gather_row(dc_head[:], PAIR + e, PACK, dc_rows[:, e, :], head_slots)
+        gather_pair(dc_head[:].bitcast(U32).rearrange("p (n h) -> p n h", h=HALVES)[:, :, 0], head_slots)
         head_codes, head_scale = quantize(dc_head, head, "dc_head")
         rest_halves = sbuf([P, rest * PACK], BF16, "rest_halves")
-        gather_pair(rest_halves[:, : 2 * rest].bitcast(U32), rest_slots)
-        for u, half in ((1, 1), (2, 1), (1, 0), (2, 0)):
+        gather_pair(rest_halves[:, : PAIR * rest].bitcast(U32), rest_slots)
+        for u, half in order[ASIDE:]:
             mask_dh(u, half)
 
         q_tok = [sbuf([P, T], F32, "q_tok%d" % b) for b in range(BLOCKS)]
         q_head = [sbuf([P, head], F32, "q_head%d" % b) for b in range(BLOCKS)]
-        head_banks = [bank(2 * CHUNKS + g, "head_bank") for g in range(2)]
+        per_bank = BANK // head
+        head_banks = [bank(HALVES * CHUNKS + g, "head_bank") for g in range(BLOCKS // per_bank)]
+
+        def head_sums(b):
+            return head_banks[b // per_bank][:, (b % per_bank) * head : (b % per_bank + 1) * head]
+
         for b in range(BLOCKS):
-            product_b(head_banks[b // 2][:, (b % 2) * head : (b % 2 + 1) * head], 0, b, head_codes, head_scale, slice(0, head))
+            product_b(head_sums(b), 0, b, head_codes, head_scale, slice(0, head))
 
         def scatter_head(b):
-            nc.scalar.copy(out=q_head[b][:], in_=head_banks[b // 2][:, (b % 2) * head : (b % 2 + 1) * head])
+            nc.scalar.copy(out=q_head[b][:], in_=head_sums(b))
             nc.vector.tensor_copy(q_tok[b][:].indirect(head_slots), q_head[b][:])
 
         for b in range(BLOCKS - 1):
             scatter_head(b)
-        for e in range(2):
-            gather_row(rest_halves[:, 2 * rest :], e, 2, dc_rows[:, e, :], rest_slots)
+        for e in range(PAIR):
+            gather_row(rest_halves[:, PAIR * rest :], e, PAIR, dc_rows[:, e, :], rest_slots)
         nc.scalar.copy(
-            out=dc_rest[:].bitcast(U32).rearrange("p (n h) -> p n h", h=2),
-            in_=rest_halves[:].bitcast(U32).rearrange("p (h n) -> p n h", h=2),
+            out=dc_rest[:].bitcast(U32).rearrange("p (n h) -> p n h", h=HALVES),
+            in_=rest_halves[:].bitcast(U32).rearrange("p (h n) -> p n h", h=HALVES),
         )
         rest_codes, rest_scale = quantize(dc_rest, rest, "dc_rest")
         scatter_head(BLOCKS - 1)
 
         rest_banks = []
         for b in range(BLOCKS):
-            rest_banks.append(bank((0, 1, 4, 5)[b], "rest_bank"))
+            rest_banks.append(bank(b, "rest_bank"))
             for f in range(1, E2):
                 cols = slice((f - 1) * C2, f * C2)
                 product_b(rest_banks[b][:, cols], f, b, rest_codes, rest_scale, cols)
@@ -261,7 +266,7 @@ def tile_moe_plb_relu_kernel(
         for b in range(BLOCKS):
             r_slots = sbuf([P, T], F32, "r_slots%d" % b)
             for g, (first, count) in enumerate(pieces):
-                acc = bank((2, 3, 6, 7, 0, 1, 4, 2)[2 * b + g], "r_bank")
+                acc = bank((BLOCKS + len(pieces) * b + g) % BANKS, "r_bank")
                 codes, scale = da_q[g]
                 for e in range(first // C1, (first + count) // C1):
                     cols = slice(e * C1 - first, (e + 1) * C1 - first)
@@ -278,11 +283,11 @@ def tile_moe_plb_relu_kernel(
             r_tok = sbuf([P, WIDE], F32, "r_tok%d" % b)
             nc.vector.tensor_copy(r_tok[:].indirect(list_a[:]), r_slots[:])
             total = sbuf([P, T], F32, "total%d" % b)
-            rows = slice(b * P, (b + 1) * P)
+            out_rows = slice(b * P, (b + 1) * P)
             if b < BLOCKS - 1:
                 nc.gpsimd.tensor_tensor(out=total[:], in0=r_tok[:, :T], in1=q_tok[b][:], op=ALU.add)
-                nc.sync.dma_start(out=out[rows, :], in_=total[:])
+                nc.sync.dma_start(out=out[out_rows, :], in_=total[:])
             else:
                 for queue, cols in ((nc.sync, slice(0, T // 2)), (nc.scalar, slice(T // 2, T))):
                     nc.vector.tensor_tensor(out=total[:, cols], in0=r_tok[:, cols], in1=q_tok[b][:, cols], op=ALU.add)
-                    queue.dma_start(out=out[rows, cols], in_=total[:, cols])
+                    queue.dma_start(out=out[out_rows, cols], in_=total[:, cols])

@@ -21,19 +21,14 @@ SIGN = mybir.ActivationFunctionType.Sign
 P = 128
 PACK = 4
 PASSES = N // (P * PACK)
-PAIR = 2
-HALVES = PACK // PAIR
 BANK = 512
-BANKS = 8
-CHUNK = BANK // PAIR
-CHUNKS = T // CHUNK
+HALF = BANK // 2
 BLOCKS = K // P
+LAST = BLOCKS - 1
 STRIPE = 16
 QUADRANT = 32
 SCALE_ROWS = 4
 LINE = 16
-WIDE = 1024
-ASIDE = 2
 
 
 def tile_moe_plb_relu_kernel(
@@ -55,12 +50,6 @@ def tile_moe_plb_relu_kernel(
             for r in range(SCALE_ROWS):
                 nc.sync.dma_start(out=scale[r:P:QUADRANT, :, :].bitcast(I32), in_=by_row[r].bitcast(I32))
 
-        def tokens_of(u):
-            return slice(u * CHUNK, (u + 1) * CHUNK)
-
-        def rows_of(half):
-            return slice(PAIR * half, PAIR * (half + 1))
-
         w2_scale_raw = sbuf([P, PASSES, H], U8, "w2_scale_raw")
         dy_scale = sbuf([P, PASSES, T], U8, "dy_scale")
         wb_scale = sbuf([P, E2, K], U8, "wb_scale")
@@ -78,17 +67,17 @@ def tile_moe_plb_relu_kernel(
         load_scale_rows(dy_scale, dy_scales)
         a_view = a.rearrange("(p j) t -> p j t", j=PACK)
         c_view = c.rearrange("(p j) t -> p j t", j=PACK)
-        a_sb = [sbuf([P, PAIR, T], F32, "a%d" % half) for half in range(HALVES)]
+        a_sb = [sbuf([P, T], F32, "a%d" % j) for j in range(PACK)]
+        c_sb = [sbuf([P, T], F32, "c%d" % j) for j in range(PACK)]
         list_b = sbuf([P, T // STRIPE], U16, "list_b")
-        nc.sync.dma_start(out=a_sb[1][:], in_=a_view[:, rows_of(1), :])
+        nc.sync.dma_start(out=a_sb[0][:], in_=a_view[:, 0, :])
         nc.sync.dma_start(list_b[:], offs2)
-        nc.sync.dma_start(out=a_sb[0][:], in_=a_view[:, rows_of(0), :])
+        for j in range(1, PACK):
+            nc.sync.dma_start(out=a_sb[j][:], in_=a_view[:, j, :])
         wb_codes = sbuf([P, E2, 2 * K], U8, "wb_codes")
         nc.sync.dma_start(out=wb_codes[:].bitcast(I32), in_=wbt_words.rearrange("f s p w -> p (f s) w").bitcast(I32))
         load_scale_rows(wb_scale, wbt_scales.rearrange("f s b k -> (f s) b k"))
-        c_sb = []
         for j in range(PACK):
-            c_sb.append(sbuf([P, T], F32, "c%d" % j))
             nc.sync.dma_start(out=c_sb[j][:], in_=c_view[:, j, :])
         list_a = sbuf([P, T // STRIPE], U16, "list_a")
         nc.sync.dma_start(list_a[:], offs)
@@ -107,71 +96,44 @@ def tile_moe_plb_relu_kernel(
             in_=w2_scale_raw[:].rearrange("p s (g m j) -> p s g j m", j=PACK, m=LINE),
         )
 
-        dc_pairs = sbuf([P, PAIR * T], BF16, "dc_pairs")
-        dc_rows = sbuf([P, PAIR, T], BF16, "dc_rows")
-        dh_live = sbuf([P, PACK, T], F32, "dh_live")
-        dh_banks = {}
+        parts = []
+        for pair in range(PACK // 2):
+            even, odd, first_bank = 2 * pair, 2 * pair + 1, 3 * pair
+            parts.append((even, 0, BANK, first_bank, 0))
+            parts.append((even, BANK, HALF, first_bank + 1, 0))
+            parts.append((odd, 0, HALF, first_bank + 1, HALF))
+            parts.append((odd, HALF, BANK, first_bank + 2, 0))
+        dh_banks = [bank(index, "dh_bank") for index in range(6)]
+        dc_rows = [sbuf([P, T], BF16, "dc_row%d" % j) for j in range(PACK)]
+        live = [sbuf([P, T], BF16, "live0")[:]]
 
-        def dh_product(u, half):
-            acc = bank(HALVES * u + half, "dh_bank")
-            dh_banks[u, half] = acc
-            for e in range(PAIR):
-                j = PAIR * half + e
-                for s in range(PASSES):
-                    nc.tensor.matmul_mx(
-                        out=acc[:, e * CHUNK : (e + 1) * CHUNK],
-                        lhsT=w2_codes[:, s, j * P : (j + 1) * P].bitcast(FP8X4),
-                        lhsT_scale=w2_scale[:, s, j * P : (j + 1) * P],
-                        rhs=dy_codes[:, s, tokens_of(u)].bitcast(FP8X4),
-                        rhs_scale=dy_scale[:, s, tokens_of(u)],
-                        start=(s == 0),
-                        stop=(s == PASSES - 1),
-                    )
+        def dh_product(j, first, count, index, col):
+            for s in range(PASSES):
+                nc.tensor.matmul_mx(
+                    out=dh_banks[index][:, col : col + count],
+                    lhsT=w2_codes[:, s, j * P : (j + 1) * P].bitcast(FP8X4),
+                    lhsT_scale=w2_scale[:, s, j * P : (j + 1) * P],
+                    rhs=dy_codes[:, s, first : first + count].bitcast(FP8X4),
+                    rhs_scale=dy_scale[:, s, first : first + count],
+                    start=(s == 0),
+                    stop=(s == PASSES - 1),
+                )
 
-        def dh_rows(u, half):
-            return dh_banks[u, half][:].rearrange("p (e n) -> p e n", e=PAIR)
-
-        def make_dc(u, half):
-            dh_in = dh_rows(u, half)
-            a_in = a_sb[half][:, :, tokens_of(u)]
-            if half == 0:
-                dst = dc_pairs[:, PAIR * u * CHUNK : PAIR * (u + 1) * CHUNK].rearrange("p (n e) -> p n e", e=PAIR)
-                dh_in = dh_in.rearrange("p e n -> p n e")
-                a_in = a_in.rearrange("p e n -> p n e")
-            else:
-                dst = dc_rows[:, :, tokens_of(u)]
-            nc.vector.scalar_tensor_tensor(out=dst, in0=a_in, scalar=0.0, in1=dh_in, op0=ALU.max, op1=ALU.mult)
-
-        def mask_dh(u, half):
+        def make_dc(j, first, count, index, col):
             nc.vector.scalar_tensor_tensor(
-                out=dh_live[:, rows_of(half), tokens_of(u)],
-                in0=a_sb[half][:, :, tokens_of(u)],
+                out=dc_rows[j][:, first : first + count],
+                in0=a_sb[j][:, first : first + count],
                 scalar=0.0,
-                in1=dh_rows(u, half),
-                op0=ALU.is_gt,
+                in1=dh_banks[index][:, col : col + count],
+                op0=ALU.max,
                 op1=ALU.mult,
             )
-
-        def make_live(u, half):
-            signs = sbuf([P, PAIR, CHUNK], F32, "signs%d" % u)
-            live = sbuf([P, PAIR, CHUNK], F32, "live%d" % u)
-            nc.scalar.activation(signs[:], a_sb[half][:, :, tokens_of(u)], SIGN)
-            nc.gpsimd.tensor_scalar(out=live[:], in0=signs[:], scalar1=1.0, scalar2=0.0, op0=ALU.min, op1=ALU.max)
-            return live
-
-        def mask_dh_aside(u, half, live):
-            kept = sbuf([P, PAIR, CHUNK], F32, "dh%d" % u)
-            nc.scalar.copy(out=kept[:], in_=dh_rows(u, half))
-            nc.gpsimd.tensor_tensor(out=dh_live[:, rows_of(half), tokens_of(u)], in0=kept[:], in1=live[:], op=ALU.mult)
 
         def slots_of(slot_list, first, count):
             return slot_list[:, first // STRIPE : (first + count) // STRIPE]
 
-        def gather_row(dst, place, step, window, offsets):
-            nc.scalar.activation(dst.rearrange("p (n j) -> p n j", j=step)[:, :, place], window.indirect(offsets), COPY)
-
-        def gather_pair(words, offsets):
-            nc.vector.tensor_copy(words, dc_pairs[:].bitcast(U32).indirect(offsets))
+        def gather_row(dst, j, row, offsets):
+            nc.scalar.activation(dst[:].rearrange("p (n j) -> p n j", j=PACK)[:, :, j], row[:].indirect(offsets), COPY)
 
         def quantize(src, count, name):
             codes = sbuf([P, count], U32, name + "_codes")
@@ -179,115 +141,162 @@ def tile_moe_plb_relu_kernel(
             nc.vector.quantize_mx(out=codes[:].bitcast(FP8X4), scales=scale[:], in_=src[:])
             return codes, scale
 
-        def product_b(dst, f, b, codes, scale, cols):
+        def product_b(dst, f, b, quantized):
+            codes, scale = quantized
             nc.tensor.matmul_mx(
                 out=dst,
                 lhsT=wb_codes[:, f, 2 * b * P : 2 * (b + 1) * P].bitcast(FP4X4),
                 lhsT_scale=wb_scale[:, f, b * P : (b + 1) * P],
+                rhs=codes[:].bitcast(FP8X4),
+                rhs_scale=scale[:],
+                start=True,
+                stop=True,
+            )
+
+        def product_a(dst, e, b, quantized, cols):
+            codes, scale = quantized
+            nc.tensor.matmul_mx(
+                out=dst,
+                lhsT=wa_codes[:, e, b * P : (b + 1) * P].bitcast(FP8X4),
+                lhsT_scale=wa_scale[:, e, b * P : (b + 1) * P],
                 rhs=codes[:, cols].bitcast(FP8X4),
                 rhs_scale=scale[:, cols],
                 start=True,
                 stop=True,
             )
 
-        order = [(u, half) for half in reversed(range(HALVES)) for u in range(CHUNKS)]
-        lives = [make_live(u, half) for u, half in order[:ASIDE]]
-        for u, half in order:
-            dh_product(u, half)
-            make_dc(u, half)
-        for (u, half), live in zip(order, lives):
-            mask_dh_aside(u, half, live)
+        def copy_out(src, width, name, tag=None):
+            dst = sbuf([P, width], F32, name, tag)
+            nc.scalar.copy(out=dst[:], in_=src)
+            return dst
 
-        head, rest = C2, T - C2
-        head_slots, rest_slots = slots_of(list_b, 0, head), slots_of(list_b, head, rest)
-        dc_head = sbuf([P, head * PACK], BF16, "dc_head")
-        dc_rest = sbuf([P, rest * PACK], BF16, "dc_rest")
-        for e in range(PAIR):
-            gather_row(dc_head[:], PAIR + e, PACK, dc_rows[:, e, :], head_slots)
-        gather_pair(dc_head[:].bitcast(U32).rearrange("p (n h) -> p n h", h=HALVES)[:, :, 0], head_slots)
-        head_codes, head_scale = quantize(dc_head, head, "dc_head")
-        rest_halves = sbuf([P, rest * PACK], BF16, "rest_halves")
-        gather_pair(rest_halves[:, : PAIR * rest].bitcast(U32), rest_slots)
-        for u, half in order[ASIDE:]:
-            mask_dh(u, half)
+        def scatter(window, offsets, values):
+            nc.vector.tensor_copy(window[:].indirect(offsets), values)
 
-        q_tok = [sbuf([P, T], F32, "q_tok%d" % b) for b in range(BLOCKS)]
-        q_head = [sbuf([P, head], F32, "q_head%d" % b) for b in range(BLOCKS)]
-        per_bank = BANK // head
-        head_banks = [bank(HALVES * CHUNKS + g, "head_bank") for g in range(BLOCKS // per_bank)]
+        signs = sbuf([P, T], F32, "signs")
+        nc.scalar.activation(signs[:], a_sb[0][:], SIGN)
+        nc.gpsimd.tensor_scalar(out=live[0], in0=signs[:], scalar1=1.0, scalar2=0.0, op0=ALU.min, op1=ALU.max)
 
-        def head_sums(b):
-            return head_banks[b // per_bank][:, (b % per_bank) * head : (b % per_bank + 1) * head]
+        q_first = [0, P, C2, 2 * C2]
+        q_count = [P, P, C2, C2]
+        q_slots = [slots_of(list_b, first, count) for first, count in zip(q_first, q_count)]
+        dc_head = [sbuf([P, P * PACK], BF16, "dc_head%d" % g) for g in range(2)]
+        for pair in range(PACK // 2):
+            mine = parts[4 * pair : 4 * pair + 4]
+            for part in mine:
+                dh_product(*part)
+            for part in mine:
+                make_dc(*part)
+            for j in (2 * pair, 2 * pair + 1):
+                for g in range(2):
+                    gather_row(dc_head[g], j, dc_rows[j], q_slots[g])
+        head_q = [quantize(dc_head[g], P, "dc_head%d" % g) for g in range(2)]
+        live_rest = sbuf([P, PACK - 1, T], BF16, "live_rest", "dc_head0")
+        for j in range(1, PACK):
+            live.append(live_rest[:, j - 1, :])
+            nc.vector.tensor_scalar(out=live[j], in0=a_sb[j][:], scalar1=0.0, scalar2=None, op0=ALU.is_gt)
 
+        first_bank = bank(6, "q_bank")
+        product_b(first_bank[:, :P], 0, 0, head_q[0])
+        other_bank = bank(7, "q_bank")
+        for b in range(1, BLOCKS):
+            product_b(other_bank[:, (b - 1) * P : b * P], 0, b, head_q[0])
+        q00 = copy_out(first_bank[:, :P], P, "q00")
+        q0r = copy_out(other_bank[:, : LAST * P], LAST * P, "q0r")
+        second_bank = bank(6, "q_bank")
         for b in range(BLOCKS):
-            product_b(head_sums(b), 0, b, head_codes, head_scale, slice(0, head))
+            product_b(second_bank[:, b * P : (b + 1) * P], 0, b, head_q[1])
+        q1 = copy_out(second_bank[:], BANK, "q1")
+        q_tok = [sbuf([P, T], F32, "q_tok%d" % b) for b in range(LAST)]
+        scatter(q_tok[0], q_slots[0], q00[:])
+        for b in range(1, LAST):
+            scatter(q_tok[b], q_slots[0], q0r[:, (b - 1) * P : b * P])
+        for b in range(LAST):
+            scatter(q_tok[b], q_slots[1], q1[:, b * P : (b + 1) * P])
 
-        def scatter_head(b):
-            nc.scalar.copy(out=q_head[b][:], in_=head_sums(b))
-            nc.vector.tensor_copy(q_tok[b][:].indirect(head_slots), q_head[b][:])
-
-        for b in range(BLOCKS - 1):
-            scatter_head(b)
-        for e in range(PAIR):
-            gather_row(rest_halves[:, PAIR * rest :], e, PAIR, dc_rows[:, e, :], rest_slots)
-        nc.scalar.copy(
-            out=dc_rest[:].bitcast(U32).rearrange("p (n h) -> p n h", h=HALVES),
-            in_=rest_halves[:].bitcast(U32).rearrange("p (h n) -> p n h", h=HALVES),
-        )
-        rest_codes, rest_scale = quantize(dc_rest, rest, "dc_rest")
-        scatter_head(BLOCKS - 1)
-
-        rest_banks = []
-        for b in range(BLOCKS):
-            rest_banks.append(bank(b, "rest_bank"))
-            for f in range(1, E2):
-                cols = slice((f - 1) * C2, f * C2)
-                product_b(rest_banks[b][:, cols], f, b, rest_codes, rest_scale, cols)
-
-        def scatter_rest(b, tag=None):
-            q_rest = sbuf([P, rest], F32, "q_rest%d" % b, tag)
-            nc.scalar.copy(out=q_rest[:], in_=rest_banks[b][:])
-            nc.vector.tensor_copy(q_tok[b][:].indirect(rest_slots), q_rest[:])
-
-        for b in range(BLOCKS - 1):
-            scatter_rest(b)
-
-        pieces = [(0, BANK), (BANK, T - BANK)]
-        da_slots = [sbuf([P, count * PACK], BF16, "da_slots%d" % first) for first, count in pieces]
-        da_rows = sbuf([P, PACK * T], BF16, "da_rows", "dc_rest")
+        c_live = [sbuf([P, T], F32, "c_live%d" % j) for j in range(PACK)]
         for j in range(PACK):
-            da_row = da_rows[:, j * T : (j + 1) * T]
-            nc.gpsimd.tensor_tensor(out=da_row, in0=dh_live[:, j, :], in1=c_sb[j][:], op=ALU.mult)
-            for (first, count), dst in zip(pieces, da_slots):
-                gather_row(dst[:], j, PACK, da_row, slots_of(list_a, first, count))
-        da_q = [quantize(src, count, "da%d" % first) for (first, count), src in zip(pieces, da_slots)]
-        scatter_rest(BLOCKS - 1, "c%d" % (PACK - 1))
+            nc.gpsimd.tensor_tensor(out=c_live[j][:], in0=c_sb[j][:], in1=live[j], op=ALU.mult)
 
+        def q_products(quantized, f, indices):
+            banks = [bank(index, "q_bank") for index in indices]
+            for b in range(BLOCKS):
+                product_b(banks[b // 2][:, (b % 2) * HALF : (b % 2 + 1) * HALF], f, b, quantized)
+            return [banks[b // 2][:, (b % 2) * HALF : (b % 2 + 1) * HALF] for b in range(BLOCKS)]
+
+        def copy_dh(pair, tag):
+            dst = sbuf([P, 2 * T], F32, "dh%d" % pair, tag)
+            for g in range(3):
+                nc.scalar.copy(out=dst[:, g * BANK : (g + 1) * BANK], in_=dh_banks[3 * pair + g][:])
+            return dst
+
+        dc_2 = sbuf([P, C2 * PACK], BF16, "dc_2", "dc_head0_codes")
+        for j in range(PACK):
+            gather_row(dc_2, j, dc_rows[j], q_slots[2])
+        q2_q = quantize(dc_2, C2, "dc_2")
+        q_tok.append(sbuf([P, T], F32, "q_tok%d" % LAST, "dc_head0_codes"))
+        scatter(q_tok[LAST], q_slots[0], q0r[:, (LAST - 1) * P :])
+        scatter(q_tok[LAST], q_slots[1], q1[:, LAST * P :])
+        sums = q_products(q2_q, 1, (7, 6))
+        dh_sb = [copy_dh(0, "dc_head1_codes")]
+        q2 = [copy_out(sums[b], C2, "q2_%d" % b) for b in range(LAST)]
+        for b in range(LAST):
+            scatter(q_tok[b], q_slots[2], q2[b][:])
+
+        dc_3 = sbuf([P, C2 * PACK], BF16, "dc_3", "dc_head0_scale")
+        for j in range(PACK):
+            gather_row(dc_3, j, dc_rows[j], q_slots[3])
+        q2.append(copy_out(sums[LAST], C2, "q2_%d" % LAST))
+        q3_q = quantize(dc_3, C2, "dc_3")
+        scatter(q_tok[LAST], q_slots[2], q2[LAST][:])
+        dh_sb.append(copy_dh(1, "dc_head1_scale"))
+        sums = q_products(q3_q, 2, (0, 1))
+        q3 = [copy_out(sums[b], C2, "q3_%d" % b) for b in range(LAST)]
+        for b in range(LAST):
+            scatter(q_tok[b], q_slots[3], q3[b][:])
+
+        pieces = T // HALF
+        r_slots = [slots_of(list_a, g * HALF, HALF) for g in range(pieces)]
+        da_rows = [sbuf([P, T], BF16, "da_row%d" % j) for j in range(PACK)]
+        da_slots = sbuf([P, HALF * PACK], BF16, "da_0")
+        for j in range(PACK):
+            dh_row = dh_sb[j // 2][:, (j % 2) * T : (j % 2 + 1) * T]
+            nc.gpsimd.tensor_tensor(out=da_rows[j][:], in0=dh_row, in1=c_live[j][:], op=ALU.mult)
+            gather_row(da_slots, j, da_rows[j], r_slots[0])
+        q3.append(copy_out(sums[LAST], C2, "q3_%d" % LAST, "c_live%d" % (PACK - 1)))
+
+        def r_products(quantized, g, indices):
+            banks = [bank(index, "r_bank") for index in indices]
+            sums = [banks[b // 2][:, (b % 2) * HALF : (b % 2 + 1) * HALF] for b in range(BLOCKS)]
+            for b in range(BLOCKS):
+                for e in range(HALF // C1):
+                    cols = slice(e * C1, (e + 1) * C1)
+                    product_a(sums[b][:, cols], g * (HALF // C1) + e, b, quantized, cols)
+            return sums
+
+        r_tok = [sbuf([P, T], F32, "r_tok%d" % b) for b in range(BLOCKS)]
+        held = (q_tok[LAST], q_slots[3], q3[LAST][:])
+        for g in range(pieces):
+            quantized = quantize(da_slots, HALF, "da_%d" % g)
+            scatter(*held)
+            sums = r_products(quantized, g, (2 + 2 * g, 3 + 2 * g))
+            r = [copy_out(sums[b], HALF, "r%d_%d" % (g, b)) for b in range(LAST)]
+            if g + 1 < pieces:
+                da_slots = sbuf([P, HALF * PACK], BF16, "da_%d" % (g + 1), "da_%d_codes" % g)
+                for j in range(PACK):
+                    gather_row(da_slots, j, da_rows[j], r_slots[g + 1])
+            r.append(copy_out(sums[LAST], HALF, "r%d_%d" % (g, LAST)))
+            held = (r_tok[LAST], r_slots[g], r[LAST][:])
+            for b in range(LAST):
+                scatter(r_tok[b], r_slots[g], r[b][:])
+        scatter(*held)
         for b in range(BLOCKS):
-            r_slots = sbuf([P, T], F32, "r_slots%d" % b)
-            for g, (first, count) in enumerate(pieces):
-                acc = bank((BLOCKS + len(pieces) * b + g) % BANKS, "r_bank")
-                codes, scale = da_q[g]
-                for e in range(first // C1, (first + count) // C1):
-                    cols = slice(e * C1 - first, (e + 1) * C1 - first)
-                    nc.tensor.matmul_mx(
-                        out=acc[:, cols],
-                        lhsT=wa_codes[:, e, b * P : (b + 1) * P].bitcast(FP8X4),
-                        lhsT_scale=wa_scale[:, e, b * P : (b + 1) * P],
-                        rhs=codes[:, cols].bitcast(FP8X4),
-                        rhs_scale=scale[:, cols],
-                        start=True,
-                        stop=True,
-                    )
-                nc.scalar.copy(out=r_slots[:, first : first + count], in_=acc[:, :count])
-            r_tok = sbuf([P, WIDE], F32, "r_tok%d" % b)
-            nc.vector.tensor_copy(r_tok[:].indirect(list_a[:]), r_slots[:])
             total = sbuf([P, T], F32, "total%d" % b)
             out_rows = slice(b * P, (b + 1) * P)
-            if b < BLOCKS - 1:
-                nc.gpsimd.tensor_tensor(out=total[:], in0=r_tok[:, :T], in1=q_tok[b][:], op=ALU.add)
+            if b < LAST:
+                nc.gpsimd.tensor_tensor(out=total[:], in0=r_tok[b][:], in1=q_tok[b][:], op=ALU.add)
                 nc.sync.dma_start(out=out[out_rows, :], in_=total[:])
             else:
                 for queue, cols in ((nc.sync, slice(0, T // 2)), (nc.scalar, slice(T // 2, T))):
-                    nc.vector.tensor_tensor(out=total[:, cols], in0=r_tok[:, cols], in1=q_tok[b][:, cols], op=ALU.add)
+                    nc.vector.tensor_tensor(out=total[:, cols], in0=r_tok[b][:, cols], in1=q_tok[b][:, cols], op=ALU.add)
                     queue.dma_start(out=out[out_rows, cols], in_=total[:, cols])

@@ -96,6 +96,18 @@ def tile_moe_plb_relu_kernel(
             in_=w2_scale_raw[:].rearrange("p s (g m j) -> p s g j m", j=PACK, m=LINE),
         )
 
+        warm = bank(6, "warm_bank")
+        for s in range(PASSES):
+            nc.tensor.matmul_mx(
+                out=warm[:],
+                lhsT=w2_raw[:, s, :P].bitcast(FP8X4),
+                lhsT_scale=w2_scale_raw[:, s, :P],
+                rhs=w2_raw[:, s, :].bitcast(FP8X4),
+                rhs_scale=w2_scale_raw[:, s, :],
+                start=True,
+                stop=True,
+            )
+
         parts = []
         for pair in range(PACK // 2):
             even, odd, first_bank = 2 * pair, 2 * pair + 1, 3 * pair
@@ -134,6 +146,18 @@ def tile_moe_plb_relu_kernel(
 
         def gather_row(dst, j, row, offsets):
             nc.scalar.activation(dst[:].rearrange("p (n j) -> p n j", j=PACK)[:, :, j], row[:].indirect(offsets), COPY)
+
+        def gather_into_pair(pairs, j, row, offsets):
+            half = pairs[:].rearrange("p (h n e) -> p h n e", h=2, e=2)[:, j // 2, :, j % 2]
+            nc.scalar.activation(half, row[:].indirect(offsets), COPY)
+
+        def weave(pairs, name, tag=None):
+            woven = sbuf([P, HALF * PACK], BF16, name, tag)
+            nc.scalar.copy(
+                out=woven[:].bitcast(U32).rearrange("p (n h) -> p n h", h=2),
+                in_=pairs[:].bitcast(U32).rearrange("p (h n) -> p n h", h=2),
+            )
+            return woven
 
         def quantize(src, count, name):
             codes = sbuf([P, count], U32, name + "_codes")
@@ -191,9 +215,10 @@ def tile_moe_plb_relu_kernel(
                 for g in range(2):
                     gather_row(dc_head[g], j, dc_rows[j], q_slots[g])
         head_q = [quantize(dc_head[g], P, "dc_head%d" % g) for g in range(2)]
-        live_rest = sbuf([P, PACK - 1, T], BF16, "live_rest", "dc_head0")
+        live.append(sbuf([P, T], BF16, "live1")[:])
+        live_rest = sbuf([P, 2, T], BF16, "live_rest", "dc_head0")
+        live.extend(live_rest[:, e, :] for e in range(2))
         for j in range(1, PACK):
-            live.append(live_rest[:, j - 1, :])
             nc.vector.tensor_scalar(out=live[j], in0=a_sb[j][:], scalar1=0.0, scalar2=None, op0=ALU.is_gt)
 
         first_bank = bank(6, "q_bank")
@@ -214,9 +239,20 @@ def tile_moe_plb_relu_kernel(
         for b in range(LAST):
             scatter(q_tok[b], q_slots[1], q1[:, b * P : (b + 1) * P])
 
-        c_live = [sbuf([P, T], F32, "c_live%d" % j) for j in range(PACK)]
-        for j in range(PACK):
-            nc.gpsimd.tensor_tensor(out=c_live[j][:], in0=c_sb[j][:], in1=live[j], op=ALU.mult)
+        mid = T // 2
+        halves = (slice(0, mid), slice(mid, T))
+
+        def mask_c(dst, j, cols):
+            nc.gpsimd.tensor_tensor(out=dst, in0=c_sb[j][:, cols], in1=live[j][:, cols], op=ALU.mult)
+
+        def make_da(j, cols, c_live):
+            dh_row = dh_sb[j // 2][:, (j % 2) * T : (j % 2 + 1) * T]
+            nc.gpsimd.tensor_tensor(out=da_rows[j][:, cols], in0=dh_row[:, cols], in1=c_live, op=ALU.mult)
+
+        c_first = sbuf([P, 2 * T + mid], F32, "c_first", "a3")
+        for j in range(2):
+            mask_c(c_first[:, j * T : (j + 1) * T], j, slice(0, T))
+        mask_c(c_first[:, 2 * T :], 2, halves[0])
 
         def q_products(quantized, f, indices):
             banks = [bank(index, "q_bank") for index in indices]
@@ -224,73 +260,91 @@ def tile_moe_plb_relu_kernel(
                 product_b(banks[b // 2][:, (b % 2) * HALF : (b % 2 + 1) * HALF], f, b, quantized)
             return [banks[b // 2][:, (b % 2) * HALF : (b % 2 + 1) * HALF] for b in range(BLOCKS)]
 
-        def copy_dh(pair, tag):
-            dst = sbuf([P, 2 * T], F32, "dh%d" % pair, tag)
-            for g in range(3):
-                nc.scalar.copy(out=dst[:, g * BANK : (g + 1) * BANK], in_=dh_banks[3 * pair + g][:])
-            return dst
+        def copy_dh(pair, g):
+            nc.scalar.copy(out=dh_sb[pair][:, g * BANK : (g + 1) * BANK], in_=dh_banks[3 * pair + g][:])
 
-        dc_2 = sbuf([P, C2 * PACK], BF16, "dc_2", "dc_head0_codes")
+        pairs = sbuf([P, C2 * PACK], BF16, "dc_2_pairs", "dc_head0_codes")
         for j in range(PACK):
-            gather_row(dc_2, j, dc_rows[j], q_slots[2])
+            gather_into_pair(pairs, j, dc_rows[j], q_slots[2])
+        dc_2 = weave(pairs, "dc_2")
         q2_q = quantize(dc_2, C2, "dc_2")
         q_tok.append(sbuf([P, T], F32, "q_tok%d" % LAST, "dc_head0_codes"))
         scatter(q_tok[LAST], q_slots[0], q0r[:, (LAST - 1) * P :])
         scatter(q_tok[LAST], q_slots[1], q1[:, LAST * P :])
         sums = q_products(q2_q, 1, (7, 6))
-        dh_sb = [copy_dh(0, "dc_head1_codes")]
+        dh_sb = [sbuf([P, 2 * T], F32, "dh0", "dc_head1_codes"), sbuf([P, 2 * T], F32, "dh1", "dc_head1_scale")]
+        for g in range(3):
+            copy_dh(0, g)
         q2 = [copy_out(sums[b], C2, "q2_%d" % b) for b in range(LAST)]
         for b in range(LAST):
             scatter(q_tok[b], q_slots[2], q2[b][:])
 
-        dc_3 = sbuf([P, C2 * PACK], BF16, "dc_3", "dc_head0_scale")
+        da_rows = [sbuf([P, T], BF16, "da_row%d" % j) for j in range(PACK)]
+        c_2b = sbuf([P, mid], F32, "c_2b", "dc_2")
+        mask_c(c_2b[:], 2, halves[1])
+        for j in range(2):
+            make_da(j, slice(0, T), c_first[:, j * T : (j + 1) * T])
+        c_3a = sbuf([P, mid], F32, "c_3a")
+        mask_c(c_3a[:], 3, halves[0])
+
+        pairs = sbuf([P, C2 * PACK], BF16, "dc_3_pairs", "dc_head0_scale")
         for j in range(PACK):
-            gather_row(dc_3, j, dc_rows[j], q_slots[3])
-        q2.append(copy_out(sums[LAST], C2, "q2_%d" % LAST))
+            gather_into_pair(pairs, j, dc_rows[j], q_slots[3])
+            if j == 1:
+                for g in range(2):
+                    copy_dh(1, g)
+        dc_3 = weave(pairs, "dc_3")
+        q2.append(copy_out(sums[LAST], C2, "q2_%d" % LAST, "dc_head0_scale"))
         q3_q = quantize(dc_3, C2, "dc_3")
         scatter(q_tok[LAST], q_slots[2], q2[LAST][:])
-        dh_sb.append(copy_dh(1, "dc_head1_scale"))
+        copy_dh(1, 2)
         sums = q_products(q3_q, 2, (0, 1))
         q3 = [copy_out(sums[b], C2, "q3_%d" % b) for b in range(LAST)]
         for b in range(LAST):
             scatter(q_tok[b], q_slots[3], q3[b][:])
 
-        pieces = T // HALF
-        r_slots = [slots_of(list_a, g * HALF, HALF) for g in range(pieces)]
-        da_rows = [sbuf([P, T], BF16, "da_row%d" % j) for j in range(PACK)]
-        da_slots = sbuf([P, HALF * PACK], BF16, "da_0")
+        r_slots = [slots_of(list_a, g * HALF, HALF) for g in range(T // HALF)]
+        c_3b = sbuf([P, mid], F32, "c_3b", "dc_3")
+        mask_c(c_3b[:], 3, halves[1])
+        for j, c_halves in ((2, (c_first[:, 2 * T :], c_2b[:])), (3, (c_3a[:], c_3b[:]))):
+            for cols, c_live in zip(halves, c_halves):
+                make_da(j, cols, c_live)
+        da_0 = sbuf([P, HALF * PACK], BF16, "da_0")
         for j in range(PACK):
-            dh_row = dh_sb[j // 2][:, (j % 2) * T : (j % 2 + 1) * T]
-            nc.gpsimd.tensor_tensor(out=da_rows[j][:], in0=dh_row, in1=c_live[j][:], op=ALU.mult)
-            gather_row(da_slots, j, da_rows[j], r_slots[0])
-        q3.append(copy_out(sums[LAST], C2, "q3_%d" % LAST, "c_live%d" % (PACK - 1)))
+            gather_row(da_0, j, da_rows[j], r_slots[0])
+        q3.append(copy_out(sums[LAST], C2, "q3_%d" % LAST, "dc_3"))
+        pairs = sbuf([P, HALF * PACK], BF16, "da_1_pairs", "dc_head1_scale")
+        for j in range(PACK):
+            gather_into_pair(pairs, j, da_rows[j], r_slots[1])
+        da_1 = weave(pairs, "da_1")
 
-        def r_products(quantized, g, indices):
-            banks = [bank(index, "r_bank") for index in indices]
-            sums = [banks[b // 2][:, (b % 2) * HALF : (b % 2 + 1) * HALF] for b in range(BLOCKS)]
+        def r_products(sums, g, quantized):
             for b in range(BLOCKS):
                 for e in range(HALF // C1):
                     cols = slice(e * C1, (e + 1) * C1)
                     product_a(sums[b][:, cols], g * (HALF // C1) + e, b, quantized, cols)
-            return sums
 
         r_tok = [sbuf([P, T], F32, "r_tok%d" % b) for b in range(BLOCKS)]
-        held = (q_tok[LAST], q_slots[3], q3[LAST][:])
-        for g in range(pieces):
-            quantized = quantize(da_slots, HALF, "da_%d" % g)
-            scatter(*held)
-            sums = r_products(quantized, g, (2 + 2 * g, 3 + 2 * g))
-            r = [copy_out(sums[b], HALF, "r%d_%d" % (g, b)) for b in range(LAST)]
-            if g + 1 < pieces:
-                da_slots = sbuf([P, HALF * PACK], BF16, "da_%d" % (g + 1), "da_%d_codes" % g)
-                for j in range(PACK):
-                    gather_row(da_slots, j, da_rows[j], r_slots[g + 1])
-            r.append(copy_out(sums[LAST], HALF, "r%d_%d" % (g, LAST)))
-            held = (r_tok[LAST], r_slots[g], r[LAST][:])
-            for b in range(LAST):
-                scatter(r_tok[b], r_slots[g], r[b][:])
-        scatter(*held)
+        quantized = quantize(da_0, HALF, "da_0")
+        scatter(q_tok[LAST], q_slots[3], q3[LAST][:])
+        banks = [bank(index, "r_bank") for index in (2, 3)]
+        sums = [banks[b // 2][:, (b % 2) * HALF : (b % 2 + 1) * HALF] for b in range(BLOCKS)]
+        r_products(sums, 0, quantized)
+        r0 = [copy_out(sums[b], HALF, "r0_%d" % b) for b in range(LAST)]
+        banks = [bank(4 + b, "r_bank") for b in range(BLOCKS)]
+        r_products([banks[b][:, :HALF] for b in range(BLOCKS)], 1, quantize(da_1, HALF, "da_1"))
+        for b in range(LAST):
+            scatter(r_tok[b], r_slots[0], r0[b][:])
+        pairs = sbuf([P, HALF * PACK], BF16, "da_2_pairs", "da_0_codes")
+        for j in range(PACK):
+            gather_into_pair(pairs, j, da_rows[j], r_slots[2])
+        da_2 = weave(pairs, "da_2")
+        r0.append(copy_out(sums[LAST], HALF, "r0_%d" % LAST, "da_0_codes"))
+        r_products([banks[b][:, HALF:] for b in range(BLOCKS)], 2, quantize(da_2, HALF, "da_2"))
+        scatter(r_tok[LAST], r_slots[0], r0[LAST][:])
         for b in range(BLOCKS):
+            r1 = copy_out(banks[b][:], BANK, "r1_%d" % b)
+            scatter(r_tok[b], slots_of(list_a, HALF, BANK), r1[:])
             total = sbuf([P, T], F32, "total%d" % b)
             out_rows = slice(b * P, (b + 1) * P)
             if b < LAST:

@@ -45,10 +45,10 @@ def tile_moe_plb_relu_kernel(
         def bank(index, name):
             return psum.tile([P, BANK], F32, name=name, tag="bank%d" % index)
 
-        def load_scale_rows(scale, source):
+        def load_scale_rows(scale, source, first=0):
             by_row = source.rearrange("m (g r) w -> r g m w", r=SCALE_ROWS)
             for r in range(SCALE_ROWS):
-                nc.sync.dma_start(out=scale[r:P:QUADRANT, :, :].bitcast(I32), in_=by_row[r].bitcast(I32))
+                nc.sync.dma_start(out=scale[first + r : P : QUADRANT, :, :].bitcast(I32), in_=by_row[r].bitcast(I32))
 
         w2_scale_raw = sbuf([P, PASSES, H], U8, "w2_scale_raw")
         dy_scale = sbuf([P, PASSES, T], U8, "dy_scale")
@@ -64,7 +64,7 @@ def tile_moe_plb_relu_kernel(
         load_scale_rows(w2_scale_raw, w2t_scales)
         dy_codes = sbuf([P, PASSES, T], I32, "dy_codes")
         nc.sync.dma_start(out=dy_codes[:], in_=dy_words.rearrange("s p t d -> p s (t d)").bitcast(I32))
-        load_scale_rows(dy_scale, dy_scales)
+        load_scale_rows(dy_scale, dy_scales, SCALE_ROWS)
         a_view = a.rearrange("(p j) t -> p j t", j=PACK)
         c_view = c.rearrange("(p j) t -> p j t", j=PACK)
         a_sb = [sbuf([P, T], F32, "a%d" % j) for j in range(PACK)]
@@ -117,7 +117,7 @@ def tile_moe_plb_relu_kernel(
             parts.append((odd, HALF, BANK, first_bank + 2, 0))
         dh_banks = [bank(index, "dh_bank") for index in range(6)]
         dc_rows = [sbuf([P, T], BF16, "dc_row%d" % j) for j in range(PACK)]
-        live = [sbuf([P, T], BF16, "live0")[:]]
+        live = [sbuf([P, T], BF16, "live%d" % j)[:] for j in range(1)]
 
         def dh_product(j, first, count, index, col):
             for s in range(PASSES):
@@ -126,7 +126,7 @@ def tile_moe_plb_relu_kernel(
                     lhsT=w2_codes[:, s, j * P : (j + 1) * P].bitcast(FP8X4),
                     lhsT_scale=w2_scale[:, s, j * P : (j + 1) * P],
                     rhs=dy_codes[:, s, first : first + count].bitcast(FP8X4),
-                    rhs_scale=dy_scale[:, s, first : first + count],
+                    rhs_scale=dy_scale[SCALE_ROWS:, s, first : first + count],
                     start=(s == 0),
                     stop=(s == PASSES - 1),
                 )
@@ -197,9 +197,10 @@ def tile_moe_plb_relu_kernel(
         def scatter(window, offsets, values):
             nc.vector.tensor_copy(window[:].indirect(offsets), values)
 
-        signs = sbuf([P, T], F32, "signs")
-        nc.scalar.activation(signs[:], a_sb[0][:], SIGN)
-        nc.gpsimd.tensor_scalar(out=live[0], in0=signs[:], scalar1=1.0, scalar2=0.0, op0=ALU.min, op1=ALU.max)
+        for j in range(1):
+            signs = sbuf([P, T], F32, "signs%d" % j)
+            nc.scalar.activation(signs[:], a_sb[j][:], SIGN)
+            nc.gpsimd.tensor_scalar(out=live[j], in0=signs[:], scalar1=1.0, scalar2=0.0, op0=ALU.min, op1=ALU.max)
 
         q_first = [0, P, C2, 2 * C2]
         q_count = [P, P, C2, C2]
@@ -216,10 +217,19 @@ def tile_moe_plb_relu_kernel(
                     gather_row(dc_head[g], j, dc_rows[j], q_slots[g])
         head_q = [quantize(dc_head[g], P, "dc_head%d" % g) for g in range(2)]
         live.append(sbuf([P, T], BF16, "live1")[:])
-        live_rest = sbuf([P, 2, T], BF16, "live_rest", "dc_head0")
-        live.extend(live_rest[:, e, :] for e in range(2))
-        for j in range(1, PACK):
+        live.append(sbuf([P, T], BF16, "live2", "w2_scale")[:])
+        for j in (1, 2):
             nc.vector.tensor_scalar(out=live[j], in0=a_sb[j][:], scalar1=0.0, scalar2=None, op0=ALU.is_gt)
+        dh_live = sbuf([P, T], F32, "dh_live", "dc_head0")
+        for j, first, count, index, col in parts[-2:]:
+            nc.vector.scalar_tensor_tensor(
+                out=dh_live[:, first : first + count],
+                in0=a_sb[j][:, first : first + count],
+                scalar=0.0,
+                in1=dh_banks[index][:, col : col + count],
+                op0=ALU.is_gt,
+                op1=ALU.mult,
+            )
 
         first_bank = bank(6, "q_bank")
         product_b(first_bank[:, :P], 0, 0, head_q[0])
@@ -245,23 +255,20 @@ def tile_moe_plb_relu_kernel(
         def mask_c(dst, j, cols):
             nc.gpsimd.tensor_tensor(out=dst, in0=c_sb[j][:, cols], in1=live[j][:, cols], op=ALU.mult)
 
-        def make_da(j, cols, c_live):
-            dh_row = dh_sb[j // 2][:, (j % 2) * T : (j % 2 + 1) * T]
-            nc.gpsimd.tensor_tensor(out=da_rows[j][:, cols], in0=dh_row[:, cols], in1=c_live, op=ALU.mult)
+        def make_da(j, cols, dh_row, factor):
+            nc.gpsimd.tensor_tensor(out=da_rows[j][:, cols], in0=dh_row[:, cols], in1=factor, op=ALU.mult)
 
-        c_first = sbuf([P, 2 * T + mid], F32, "c_first", "a3")
+        c_first = sbuf([P, 2 * T + mid], F32, "c_first", "dc_head1")
         for j in range(2):
             mask_c(c_first[:, j * T : (j + 1) * T], j, slice(0, T))
         mask_c(c_first[:, 2 * T :], 2, halves[0])
 
-        def q_products(quantized, f, indices):
-            banks = [bank(index, "q_bank") for index in indices]
-            for b in range(BLOCKS):
-                product_b(banks[b // 2][:, (b % 2) * HALF : (b % 2 + 1) * HALF], f, b, quantized)
-            return [banks[b // 2][:, (b % 2) * HALF : (b % 2 + 1) * HALF] for b in range(BLOCKS)]
+        def half_banks(indices):
+            banks = [bank(index, "sums_bank") for index in indices]
+            return [banks[0][:, :HALF], banks[1][:, :HALF], banks[1][:, HALF:], banks[2][:, :HALF]]
 
-        def copy_dh(pair, g):
-            nc.scalar.copy(out=dh_sb[pair][:, g * BANK : (g + 1) * BANK], in_=dh_banks[3 * pair + g][:])
+        def copy_dh(dst, index, count):
+            nc.scalar.copy(out=dst, in_=dh_banks[index][:, :count])
 
         pairs = sbuf([P, C2 * PACK], BF16, "dc_2_pairs", "dc_head0_codes")
         for j in range(PACK):
@@ -271,48 +278,52 @@ def tile_moe_plb_relu_kernel(
         q_tok.append(sbuf([P, T], F32, "q_tok%d" % LAST, "dc_head0_codes"))
         scatter(q_tok[LAST], q_slots[0], q0r[:, (LAST - 1) * P :])
         scatter(q_tok[LAST], q_slots[1], q1[:, LAST * P :])
-        sums = q_products(q2_q, 1, (7, 6))
-        dh_sb = [sbuf([P, 2 * T], F32, "dh0", "dc_head1_codes"), sbuf([P, 2 * T], F32, "dh1", "dc_head1_scale")]
+        banks = [bank(index, "q_bank") for index in (6, 7)]
+        sums = [banks[b // 2][:, (b % 2) * HALF : (b % 2 + 1) * HALF] for b in range(BLOCKS)]
+        for b in (0, 2, 3):
+            product_b(sums[b], 1, b, q2_q)
+        dh_01 = sbuf([P, 2 * T], F32, "dh_01", "dc_head1_codes")
+        dh_2 = sbuf([P, T], F32, "dh_2", "dc_head1_scale")
         for g in range(3):
-            copy_dh(0, g)
-        q2 = [copy_out(sums[b], C2, "q2_%d" % b) for b in range(LAST)]
+            copy_dh(dh_01[:, g * BANK : (g + 1) * BANK], g, BANK)
+        q2 = [copy_out(sums[0], C2, "q2_0")]
+        product_b(sums[1], 1, 1, q2_q)
+        q2.extend(copy_out(sums[b], C2, "q2_%d" % b) for b in range(1, LAST))
         for b in range(LAST):
             scatter(q_tok[b], q_slots[2], q2[b][:])
 
-        da_rows = [sbuf([P, T], BF16, "da_row%d" % j) for j in range(PACK)]
+        da_rows = [sbuf([P, T], BF16, "da_row%d" % j) for j in range(PACK - 1)]
         c_2b = sbuf([P, mid], F32, "c_2b", "dc_2")
         mask_c(c_2b[:], 2, halves[1])
         for j in range(2):
-            make_da(j, slice(0, T), c_first[:, j * T : (j + 1) * T])
-        c_3a = sbuf([P, mid], F32, "c_3a")
-        mask_c(c_3a[:], 3, halves[0])
+            make_da(j, slice(0, T), dh_01[:, j * T : (j + 1) * T], c_first[:, j * T : (j + 1) * T])
 
         pairs = sbuf([P, C2 * PACK], BF16, "dc_3_pairs", "dc_head0_scale")
         for j in range(PACK):
             gather_into_pair(pairs, j, dc_rows[j], q_slots[3])
             if j == 1:
-                for g in range(2):
-                    copy_dh(1, g)
+                copy_dh(dh_2[:, :BANK], 3, BANK)
+                copy_dh(dh_2[:, BANK:], 4, HALF)
         dc_3 = weave(pairs, "dc_3")
         q2.append(copy_out(sums[LAST], C2, "q2_%d" % LAST, "dc_head0_scale"))
         q3_q = quantize(dc_3, C2, "dc_3")
         scatter(q_tok[LAST], q_slots[2], q2[LAST][:])
-        copy_dh(1, 2)
-        sums = q_products(q3_q, 2, (0, 1))
+        sums = half_banks((0, 1, 2))
+        for b in range(BLOCKS):
+            product_b(sums[b], 2, b, q3_q)
         q3 = [copy_out(sums[b], C2, "q3_%d" % b) for b in range(LAST)]
         for b in range(LAST):
             scatter(q_tok[b], q_slots[3], q3[b][:])
 
         r_slots = [slots_of(list_a, g * HALF, HALF) for g in range(T // HALF)]
-        c_3b = sbuf([P, mid], F32, "c_3b", "dc_3")
-        mask_c(c_3b[:], 3, halves[1])
-        for j, c_halves in ((2, (c_first[:, 2 * T :], c_2b[:])), (3, (c_3a[:], c_3b[:]))):
-            for cols, c_live in zip(halves, c_halves):
-                make_da(j, cols, c_live)
+        da_rows.append(sbuf([P, T], BF16, "da_row3", "dc_3"))
+        make_da(3, slice(0, T), dh_live, c_sb[3][:])
+        for cols, c_live in zip(halves, (c_first[:, 2 * T :], c_2b[:])):
+            make_da(2, cols, dh_2, c_live)
         da_0 = sbuf([P, HALF * PACK], BF16, "da_0")
-        for j in range(PACK):
+        for j in (0, 1, 3, 2):
             gather_row(da_0, j, da_rows[j], r_slots[0])
-        q3.append(copy_out(sums[LAST], C2, "q3_%d" % LAST, "dc_3"))
+        q3.append(copy_out(sums[LAST], C2, "q3_%d" % LAST, "dc_2"))
         pairs = sbuf([P, HALF * PACK], BF16, "da_1_pairs", "dc_head1_scale")
         for j in range(PACK):
             gather_into_pair(pairs, j, da_rows[j], r_slots[1])
@@ -327,14 +338,15 @@ def tile_moe_plb_relu_kernel(
         r_tok = [sbuf([P, T], F32, "r_tok%d" % b) for b in range(BLOCKS)]
         quantized = quantize(da_0, HALF, "da_0")
         scatter(q_tok[LAST], q_slots[3], q3[LAST][:])
-        banks = [bank(index, "r_bank") for index in (2, 3)]
-        sums = [banks[b // 2][:, (b % 2) * HALF : (b % 2 + 1) * HALF] for b in range(BLOCKS)]
+        sums = half_banks((3, 0, 1))
         r_products(sums, 0, quantized)
         r0 = [copy_out(sums[b], HALF, "r0_%d" % b) for b in range(LAST)]
         banks = [bank(4 + b, "r_bank") for b in range(BLOCKS)]
         r_products([banks[b][:, :HALF] for b in range(BLOCKS)], 1, quantize(da_1, HALF, "da_1"))
+        r1 = [sbuf([P, BANK], F32, "r1_%d" % b) for b in range(BLOCKS)]
         for b in range(LAST):
             scatter(r_tok[b], r_slots[0], r0[b][:])
+        nc.scalar.copy(out=r1[0][:, :HALF], in_=banks[0][:, :HALF])
         pairs = sbuf([P, HALF * PACK], BF16, "da_2_pairs", "da_0_codes")
         for j in range(PACK):
             gather_into_pair(pairs, j, da_rows[j], r_slots[2])
@@ -343,8 +355,9 @@ def tile_moe_plb_relu_kernel(
         r_products([banks[b][:, HALF:] for b in range(BLOCKS)], 2, quantize(da_2, HALF, "da_2"))
         scatter(r_tok[LAST], r_slots[0], r0[LAST][:])
         for b in range(BLOCKS):
-            r1 = copy_out(banks[b][:], BANK, "r1_%d" % b)
-            scatter(r_tok[b], slots_of(list_a, HALF, BANK), r1[:])
+            cols = slice(HALF if b == 0 else 0, BANK)
+            nc.scalar.copy(out=r1[b][:, cols], in_=banks[b][:, cols])
+            scatter(r_tok[b], slots_of(list_a, HALF, BANK), r1[b][:])
             total = sbuf([P, T], F32, "total%d" % b)
             out_rows = slice(b * P, (b + 1) * P)
             if b < LAST:

@@ -116,7 +116,7 @@ def tile_moe_plb_relu_kernel(
             parts.append((odd, 0, HALF, first_bank + 1, HALF))
             parts.append((odd, HALF, BANK, first_bank + 2, 0))
         dh_banks = [bank(index, "dh_bank") for index in range(6)]
-        dc_rows = [sbuf([P, T], BF16, "dc_row%d" % j) for j in range(PACK)]
+        dc_rows = [sbuf([P, T], BF16, "dc_row%d" % j)[:] for j in range(PACK)]
         live = [sbuf([P, T], BF16, "live%d" % j)[:] for j in range(1)]
 
         def dh_product(j, first, count, index, col):
@@ -145,11 +145,11 @@ def tile_moe_plb_relu_kernel(
             return slot_list[:, first // STRIPE : (first + count) // STRIPE]
 
         def gather_row(dst, j, row, offsets):
-            nc.scalar.activation(dst[:].rearrange("p (n j) -> p n j", j=PACK)[:, :, j], row[:].indirect(offsets), COPY)
+            nc.scalar.activation(dst[:].rearrange("p (n j) -> p n j", j=PACK)[:, :, j], row.indirect(offsets), COPY)
 
         def gather_into_pair(pairs, j, row, offsets):
             half = pairs[:].rearrange("p (h n e) -> p h n e", h=2, e=2)[:, j // 2, :, j % 2]
-            nc.scalar.activation(half, row[:].indirect(offsets), COPY)
+            nc.scalar.activation(half, row.indirect(offsets), COPY)
 
         def weave(pairs, name, tag=None):
             woven = sbuf([P, HALF * PACK], BF16, name, tag)
@@ -237,31 +237,26 @@ def tile_moe_plb_relu_kernel(
         for b in range(1, BLOCKS):
             product_b(other_bank[:, (b - 1) * P : b * P], 0, b, head_q[0])
         q00 = copy_out(first_bank[:, :P], P, "q00")
-        q0r = copy_out(other_bank[:, : LAST * P], LAST * P, "q0r")
+        q_head = sbuf([P, (LAST + BLOCKS) * P], F32, "q_head")
+        nc.scalar.copy(out=q_head[:, : LAST * P], in_=other_bank[:, : LAST * P])
         second_bank = bank(6, "q_bank")
         for b in range(BLOCKS):
-            product_b(second_bank[:, b * P : (b + 1) * P], 0, b, head_q[1])
-        q1 = copy_out(second_bank[:], BANK, "q1")
+            place = (b + 1) % BLOCKS
+            product_b(second_bank[:, place * P : (place + 1) * P], 0, b, head_q[1])
+        nc.scalar.copy(out=q_head[:, LAST * P :], in_=second_bank[:])
         q_tok = [sbuf([P, T], F32, "q_tok%d" % b) for b in range(LAST)]
         scatter(q_tok[0], q_slots[0], q00[:])
         for b in range(1, LAST):
-            scatter(q_tok[b], q_slots[0], q0r[:, (b - 1) * P : b * P])
+            scatter(q_tok[b], q_slots[0], q_head[:, (b - 1) * P : b * P])
         for b in range(LAST):
-            scatter(q_tok[b], q_slots[1], q1[:, b * P : (b + 1) * P])
+            scatter(q_tok[b], q_slots[1], q_head[:, (BLOCKS + b) * P : (BLOCKS + b + 1) * P])
 
-        mid = T // 2
-        halves = (slice(0, mid), slice(mid, T))
+        def product(dst, left, right):
+            nc.gpsimd.tensor_tensor(out=dst, in0=left, in1=right, op=ALU.mult)
 
-        def mask_c(dst, j, cols):
-            nc.gpsimd.tensor_tensor(out=dst, in0=c_sb[j][:, cols], in1=live[j][:, cols], op=ALU.mult)
-
-        def make_da(j, cols, dh_row, factor):
-            nc.gpsimd.tensor_tensor(out=da_rows[j][:, cols], in0=dh_row[:, cols], in1=factor, op=ALU.mult)
-
-        c_first = sbuf([P, 2 * T + mid], F32, "c_first", "dc_head1")
+        c_first = sbuf([P, 2 * T], F32, "c_first", "dc_head1")
         for j in range(2):
-            mask_c(c_first[:, j * T : (j + 1) * T], j, slice(0, T))
-        mask_c(c_first[:, 2 * T :], 2, halves[0])
+            product(c_first[:, j * T : (j + 1) * T], c_sb[j][:], live[j])
 
         def half_banks(indices):
             banks = [bank(index, "sums_bank") for index in indices]
@@ -276,8 +271,7 @@ def tile_moe_plb_relu_kernel(
         dc_2 = weave(pairs, "dc_2")
         q2_q = quantize(dc_2, C2, "dc_2")
         q_tok.append(sbuf([P, T], F32, "q_tok%d" % LAST, "dc_head0_codes"))
-        scatter(q_tok[LAST], q_slots[0], q0r[:, (LAST - 1) * P :])
-        scatter(q_tok[LAST], q_slots[1], q1[:, LAST * P :])
+        scatter(q_tok[LAST], slots_of(list_b, 0, C2), q_head[:, (LAST - 1) * P : BLOCKS * P])
         banks = [bank(index, "q_bank") for index in (6, 7)]
         sums = [banks[b // 2][:, (b % 2) * HALF : (b % 2 + 1) * HALF] for b in range(BLOCKS)]
         for b in (0, 2, 3):
@@ -292,20 +286,19 @@ def tile_moe_plb_relu_kernel(
         for b in range(LAST):
             scatter(q_tok[b], q_slots[2], q2[b][:])
 
-        da_rows = [sbuf([P, T], BF16, "da_row%d" % j) for j in range(PACK - 1)]
-        c_2b = sbuf([P, mid], F32, "c_2b", "dc_2")
-        mask_c(c_2b[:], 2, halves[1])
+        da_rows = [sbuf([P, T], BF16, "da_row%d" % j)[:] for j in range(2)]
+        c_2 = sbuf([P, T], F32, "c_2", "dc_2")
+        product(c_2[:], c_sb[2][:], live[2])
         for j in range(2):
-            make_da(j, slice(0, T), dh_01[:, j * T : (j + 1) * T], c_first[:, j * T : (j + 1) * T])
+            product(da_rows[j], dh_01[:, j * T : (j + 1) * T], c_first[:, j * T : (j + 1) * T])
 
         pairs = sbuf([P, C2 * PACK], BF16, "dc_3_pairs", "dc_head0_scale")
         for j in range(PACK):
             gather_into_pair(pairs, j, dc_rows[j], q_slots[3])
-            if j == 1:
-                copy_dh(dh_2[:, :BANK], 3, BANK)
-                copy_dh(dh_2[:, BANK:], 4, HALF)
         dc_3 = weave(pairs, "dc_3")
         q2.append(copy_out(sums[LAST], C2, "q2_%d" % LAST, "dc_head0_scale"))
+        copy_dh(dh_2[:, :BANK], 3, BANK)
+        copy_dh(dh_2[:, BANK:], 4, HALF)
         q3_q = quantize(dc_3, C2, "dc_3")
         scatter(q_tok[LAST], q_slots[2], q2[LAST][:])
         sums = half_banks((0, 1, 2))
@@ -316,10 +309,10 @@ def tile_moe_plb_relu_kernel(
             scatter(q_tok[b], q_slots[3], q3[b][:])
 
         r_slots = [slots_of(list_a, g * HALF, HALF) for g in range(T // HALF)]
-        da_rows.append(sbuf([P, T], BF16, "da_row3", "dc_3"))
-        make_da(3, slice(0, T), dh_live, c_sb[3][:])
-        for cols, c_live in zip(halves, (c_first[:, 2 * T :], c_2b[:])):
-            make_da(2, cols, dh_2, c_live)
+        da_late = sbuf([P, 2 * T], BF16, "da_late", "dc_3")
+        da_rows.extend(da_late[:, e * T : (e + 1) * T] for e in range(2))
+        product(da_rows[3], dh_live[:], c_sb[3][:])
+        product(da_rows[2], dh_2[:], c_2[:])
         da_0 = sbuf([P, HALF * PACK], BF16, "da_0")
         for j in (0, 1, 3, 2):
             gather_row(da_0, j, da_rows[j], r_slots[0])

@@ -151,9 +151,9 @@ def tile_moe_plb_relu_kernel(
             half = pairs[:].rearrange("p (h n e) -> p h n e", h=2, e=2)[:, j // 2, :, j % 2]
             nc.scalar.activation(half, row.indirect(offsets), COPY)
 
-        def weave(pairs, name, tag=None):
-            woven = sbuf([P, HALF * PACK], BF16, name, tag)
-            nc.scalar.copy(
+        def weave(pairs, name, copy=nc.scalar.copy):
+            woven = sbuf([P, HALF * PACK], BF16, name)
+            copy(
                 out=woven[:].bitcast(U32).rearrange("p (n h) -> p n h", h=2),
                 in_=pairs[:].bitcast(U32).rearrange("p (h n) -> p n h", h=2),
             )
@@ -257,10 +257,17 @@ def tile_moe_plb_relu_kernel(
         c_first = sbuf([P, 2 * T], F32, "c_first", "dc_head1")
         for j in range(2):
             product(c_first[:, j * T : (j + 1) * T], c_sb[j][:], live[j])
+        da_rows = [sbuf([P, T], BF16, "da_row%d" % j) for j in (0, 1, 3)]
+        product(da_rows[2][:], dh_live[:], c_sb[3][:])
 
         def half_banks(indices):
             banks = [bank(index, "sums_bank") for index in indices]
-            return [banks[0][:, :HALF], banks[1][:, :HALF], banks[1][:, HALF:], banks[2][:, :HALF]]
+            return [banks[0][:, :HALF], banks[1][:, :HALF], banks[1][:, HALF:], banks[2][:, :HALF], banks[1][:]]
+
+        def copy_three(sums, name):
+            first = copy_out(sums[0], HALF, name + "_0")
+            both = copy_out(sums[BLOCKS], BANK, name + "_12")
+            return [first[:], both[:, :HALF], both[:, HALF:]]
 
         def copy_dh(dst, index, count):
             nc.scalar.copy(out=dst, in_=dh_banks[index][:, :count])
@@ -286,11 +293,10 @@ def tile_moe_plb_relu_kernel(
         for b in range(LAST):
             scatter(q_tok[b], q_slots[2], q2[b][:])
 
-        da_rows = [sbuf([P, T], BF16, "da_row%d" % j)[:] for j in range(2)]
         c_2 = sbuf([P, T], F32, "c_2", "dc_2")
         product(c_2[:], c_sb[2][:], live[2])
         for j in range(2):
-            product(da_rows[j], dh_01[:, j * T : (j + 1) * T], c_first[:, j * T : (j + 1) * T])
+            product(da_rows[j][:], dh_01[:, j * T : (j + 1) * T], c_first[:, j * T : (j + 1) * T])
 
         pairs = sbuf([P, C2 * PACK], BF16, "dc_3_pairs", "dc_head0_scale")
         for j in range(PACK):
@@ -304,23 +310,21 @@ def tile_moe_plb_relu_kernel(
         sums = half_banks((0, 1, 2))
         for b in range(BLOCKS):
             product_b(sums[b], 2, b, q3_q)
-        q3 = [copy_out(sums[b], C2, "q3_%d" % b) for b in range(LAST)]
+        q3 = copy_three(sums, "q3")
         for b in range(LAST):
-            scatter(q_tok[b], q_slots[3], q3[b][:])
+            scatter(q_tok[b], q_slots[3], q3[b])
 
         r_slots = [slots_of(list_a, g * HALF, HALF) for g in range(T // HALF)]
-        da_late = sbuf([P, 2 * T], BF16, "da_late", "dc_3")
-        da_rows.extend(da_late[:, e * T : (e + 1) * T] for e in range(2))
-        product(da_rows[3], dh_live[:], c_sb[3][:])
-        product(da_rows[2], dh_2[:], c_2[:])
+        da_rows.insert(2, sbuf([P, T], BF16, "da_row2", "dc_3"))
+        product(da_rows[2][:], dh_2[:], c_2[:])
         da_0 = sbuf([P, HALF * PACK], BF16, "da_0")
-        for j in (0, 1, 3, 2):
-            gather_row(da_0, j, da_rows[j], r_slots[0])
+        for j in (3, 0, 1, 2):
+            gather_row(da_0, j, da_rows[j][:], r_slots[0])
         q3.append(copy_out(sums[LAST], C2, "q3_%d" % LAST, "dc_2"))
         pairs = sbuf([P, HALF * PACK], BF16, "da_1_pairs", "dc_head1_scale")
         for j in range(PACK):
-            gather_into_pair(pairs, j, da_rows[j], r_slots[1])
-        da_1 = weave(pairs, "da_1")
+            gather_into_pair(pairs, j, da_rows[j][:], r_slots[1])
+        da_1 = weave(pairs, "da_1", nc.gpsimd.tensor_copy)
 
         def r_products(sums, g, quantized):
             for b in range(BLOCKS):
@@ -328,21 +332,21 @@ def tile_moe_plb_relu_kernel(
                     cols = slice(e * C1, (e + 1) * C1)
                     product_a(sums[b][:, cols], g * (HALF // C1) + e, b, quantized, cols)
 
-        r_tok = [sbuf([P, T], F32, "r_tok%d" % b) for b in range(BLOCKS)]
         quantized = quantize(da_0, HALF, "da_0")
         scatter(q_tok[LAST], q_slots[3], q3[LAST][:])
         sums = half_banks((3, 0, 1))
         r_products(sums, 0, quantized)
-        r0 = [copy_out(sums[b], HALF, "r0_%d" % b) for b in range(LAST)]
+        r0 = copy_three(sums, "r0")
         banks = [bank(4 + b, "r_bank") for b in range(BLOCKS)]
         r_products([banks[b][:, :HALF] for b in range(BLOCKS)], 1, quantize(da_1, HALF, "da_1"))
         r1 = [sbuf([P, BANK], F32, "r1_%d" % b) for b in range(BLOCKS)]
+        r_tok = [sbuf([P, T], F32, "r_tok%d" % b, "da_1" if b == LAST - 1 else None) for b in range(BLOCKS)]
         for b in range(LAST):
-            scatter(r_tok[b], r_slots[0], r0[b][:])
+            scatter(r_tok[b], r_slots[0], r0[b])
         nc.scalar.copy(out=r1[0][:, :HALF], in_=banks[0][:, :HALF])
         pairs = sbuf([P, HALF * PACK], BF16, "da_2_pairs", "da_0_codes")
         for j in range(PACK):
-            gather_into_pair(pairs, j, da_rows[j], r_slots[2])
+            gather_into_pair(pairs, j, da_rows[j][:], r_slots[2])
         da_2 = weave(pairs, "da_2")
         r0.append(copy_out(sums[LAST], HALF, "r0_%d" % LAST, "da_0_codes"))
         r_products([banks[b][:, HALF:] for b in range(BLOCKS)], 2, quantize(da_2, HALF, "da_2"))

@@ -216,8 +216,8 @@ def tile_moe_plb_relu_kernel(
                 for g in range(2):
                     gather_row(dc_head[g], j, dc_rows[j], q_slots[g])
         head_q = [quantize(dc_head[g], P, "dc_head%d" % g) for g in range(2)]
-        live.append(sbuf([P, T], BF16, "live1")[:])
-        live.append(sbuf([P, T], BF16, "live2", "w2_scale")[:])
+        live_12 = sbuf([P, 2 * T], BF16, "live_12", "signs0")
+        live.extend(live_12[:, e * T : (e + 1) * T] for e in range(2))
         for j in (1, 2):
             nc.vector.tensor_scalar(out=live[j], in0=a_sb[j][:], scalar1=0.0, scalar2=None, op0=ALU.is_gt)
         dh_live = sbuf([P, T], F32, "dh_live", "dc_head0")

@@ -236,7 +236,9 @@ def tile_moe_plb_relu_kernel(
         other_bank = bank(7, "q_bank")
         for b in range(1, BLOCKS):
             product_b(other_bank[:, (b - 1) * P : b * P], 0, b, head_q[0])
-        q00 = copy_out(first_bank[:, :P], P, "q00")
+        stage = sbuf([P, C2 * PACK], BF16, "stage", "a2")
+        q00 = stage[:, 3 * P : 5 * P].bitcast(F32)
+        nc.scalar.copy(out=q00, in_=first_bank[:, :P])
         q_head = sbuf([P, (LAST + BLOCKS) * P], F32, "q_head")
         nc.scalar.copy(out=q_head[:, : LAST * P], in_=other_bank[:, : LAST * P])
         second_bank = bank(6, "q_bank")
@@ -245,7 +247,7 @@ def tile_moe_plb_relu_kernel(
             product_b(second_bank[:, place * P : (place + 1) * P], 0, b, head_q[1])
         nc.scalar.copy(out=q_head[:, LAST * P :], in_=second_bank[:])
         q_tok = [sbuf([P, T], F32, "q_tok%d" % b) for b in range(LAST)]
-        scatter(q_tok[0], q_slots[0], q00[:])
+        scatter(q_tok[0], q_slots[0], q00)
         for b in range(1, LAST):
             scatter(q_tok[b], q_slots[0], q_head[:, (b - 1) * P : b * P])
         for b in range(LAST):
@@ -272,12 +274,16 @@ def tile_moe_plb_relu_kernel(
         def copy_dh(dst, index, count):
             nc.scalar.copy(out=dst, in_=dh_banks[index][:, :count])
 
-        pairs = sbuf([P, C2 * PACK], BF16, "dc_2_pairs", "dc_head0_codes")
-        for j in range(PACK):
+        pairs = stage
+        for first in (0, P):
+            for e in range(2):
+                dst = pairs[:, 2 * first : 2 * (first + P)].rearrange("p (n e) -> p n e", e=2)[:, :, e]
+                nc.scalar.activation(dst, dc_rows[e].indirect(slots_of(list_b, C2 + first, P)), COPY)
+        for j in range(2, PACK):
             gather_into_pair(pairs, j, dc_rows[j], q_slots[2])
         dc_2 = weave(pairs, "dc_2")
         q2_q = quantize(dc_2, C2, "dc_2")
-        q_tok.append(sbuf([P, T], F32, "q_tok%d" % LAST, "dc_head0_codes"))
+        q_tok.append(sbuf([P, T], F32, "q_tok%d" % LAST, "a2"))
         scatter(q_tok[LAST], slots_of(list_b, 0, C2), q_head[:, (LAST - 1) * P : BLOCKS * P])
         banks = [bank(index, "q_bank") for index in (6, 7)]
         sums = [banks[b // 2][:, (b % 2) * HALF : (b % 2 + 1) * HALF] for b in range(BLOCKS)]

@@ -23,6 +23,7 @@ PACK = 4
 PASSES = N // (P * PACK)
 BANK = 512
 HALF = BANK // 2
+PARTS = T // HALF
 BLOCKS = K // P
 LAST = BLOCKS - 1
 STRIPE = 16
@@ -50,14 +51,15 @@ def tile_moe_plb_relu_kernel(
             for r in range(SCALE_ROWS):
                 nc.sync.dma_start(out=scale[first + r : P : QUADRANT, :, :].bitcast(I32), in_=by_row[r].bitcast(I32))
 
+        def two_rows(flat):
+            return flat.rearrange("p (e t) -> p e t", e=2)
+
         w2_scale_raw = sbuf([P, PASSES, H], U8, "w2_scale_raw")
         dy_scale = sbuf([P, PASSES, T], U8, "dy_scale")
         wb_scale = sbuf([P, E2, K], U8, "wb_scale")
         wa_scale = sbuf([P, E1, K], U8, "wa_scale")
-        nc.gpsimd.memset(w2_scale_raw[:].bitcast(I32), 0)
-        nc.gpsimd.memset(dy_scale[:].bitcast(I32), 0)
-        nc.gpsimd.memset(wb_scale[:].bitcast(I32), 0)
-        nc.gpsimd.memset(wa_scale[:].bitcast(I32), 0)
+        for plane in (w2_scale_raw, dy_scale, wb_scale, wa_scale):
+            nc.gpsimd.memset(plane[:].bitcast(I32), 0)
 
         w2_raw = sbuf([P, PASSES, H], I32, "w2_raw")
         nc.sync.dma_start(out=w2_raw[:], in_=w2t_words.rearrange("s p i d -> p s (i d)").bitcast(I32))
@@ -67,18 +69,22 @@ def tile_moe_plb_relu_kernel(
         load_scale_rows(dy_scale, dy_scales, SCALE_ROWS)
         a_view = a.rearrange("(p j) t -> p j t", j=PACK)
         c_view = c.rearrange("(p j) t -> p j t", j=PACK)
-        a_sb = [sbuf([P, T], F32, "a%d" % j) for j in range(PACK)]
-        c_sb = [sbuf([P, T], F32, "c%d" % j) for j in range(PACK)]
+        a_pair = [sbuf([P, 2 * T], F32, "a_pair%d" % o) for o in range(2)]
+        c_pair = [sbuf([P, 2 * T], F32, "c_pair%d" % o) for o in range(2)]
+
+        def row(pair, j):
+            return pair[j % 2][:, (j // 2) * T : (j // 2 + 1) * T]
+
         list_b = sbuf([P, T // STRIPE], U16, "list_b")
-        nc.sync.dma_start(out=a_sb[0][:], in_=a_view[:, 0, :])
+        nc.sync.dma_start(out=row(a_pair, 0), in_=a_view[:, 0, :])
         nc.sync.dma_start(list_b[:], offs2)
         for j in range(1, PACK):
-            nc.sync.dma_start(out=a_sb[j][:], in_=a_view[:, j, :])
+            nc.sync.dma_start(out=row(a_pair, j), in_=a_view[:, j, :])
         wb_codes = sbuf([P, E2, 2 * K], U8, "wb_codes")
         nc.sync.dma_start(out=wb_codes[:].bitcast(I32), in_=wbt_words.rearrange("f s p w -> p (f s) w").bitcast(I32))
         load_scale_rows(wb_scale, wbt_scales.rearrange("f s b k -> (f s) b k"))
-        for j in range(PACK):
-            nc.sync.dma_start(out=c_sb[j][:], in_=c_view[:, j, :])
+        for j in (1, 3, 0, 2):
+            nc.sync.dma_start(out=row(c_pair, j), in_=c_view[:, j, :])
         list_a = sbuf([P, T // STRIPE], U16, "list_a")
         nc.sync.dma_start(list_a[:], offs)
         wa_codes = sbuf([P, E1, K], I32, "wa_codes")
@@ -108,58 +114,44 @@ def tile_moe_plb_relu_kernel(
                 stop=True,
             )
 
-        parts = []
-        for pair in range(PACK // 2):
-            even, odd, first_bank = 2 * pair, 2 * pair + 1, 3 * pair
-            parts.append((even, 0, BANK, first_bank, 0))
-            parts.append((even, BANK, HALF, first_bank + 1, 0))
-            parts.append((odd, 0, HALF, first_bank + 1, HALF))
-            parts.append((odd, HALF, BANK, first_bank + 2, 0))
-        dh_banks = [bank(index, "dh_bank") for index in range(6)]
-        dc_rows = [sbuf([P, T], BF16, "dc_row%d" % j)[:] for j in range(PACK)]
-        live = [sbuf([P, T], BF16, "live%d" % j)[:] for j in range(1)]
+        dh_banks = [[bank(o * PARTS + t, "dh_bank") for t in range(PARTS)] for o in range(2)]
 
-        def dh_product(j, first, count, index, col):
-            for s in range(PASSES):
-                nc.tensor.matmul_mx(
-                    out=dh_banks[index][:, col : col + count],
-                    lhsT=w2_codes[:, s, j * P : (j + 1) * P].bitcast(FP8X4),
-                    lhsT_scale=w2_scale[:, s, j * P : (j + 1) * P],
-                    rhs=dy_codes[:, s, first : first + count].bitcast(FP8X4),
-                    rhs_scale=dy_scale[SCALE_ROWS:, s, first : first + count],
-                    start=(s == 0),
-                    stop=(s == PASSES - 1),
-                )
+        def tokens(t):
+            return slice(t * HALF, (t + 1) * HALF)
 
-        def make_dc(j, first, count, index, col):
-            nc.vector.scalar_tensor_tensor(
-                out=dc_rows[j][:, first : first + count],
-                in0=a_sb[j][:, first : first + count],
-                scalar=0.0,
-                in1=dh_banks[index][:, col : col + count],
-                op0=ALU.max,
-                op1=ALU.mult,
-            )
+        def dh_part(j, t):
+            return dh_banks[j % 2][t][:, tokens(j // 2)]
+
+        def dh_row(j):
+            for t in range(PARTS):
+                for s in range(PASSES):
+                    nc.tensor.matmul_mx(
+                        out=dh_part(j, t),
+                        lhsT=w2_codes[:, s, j * P : (j + 1) * P].bitcast(FP8X4),
+                        lhsT_scale=w2_scale[:, s, j * P : (j + 1) * P],
+                        rhs=dy_codes[:, s, tokens(t)].bitcast(FP8X4),
+                        rhs_scale=dy_scale[SCALE_ROWS:, s, tokens(t)],
+                        start=(s == 0),
+                        stop=(s == PASSES - 1),
+                    )
 
         def slots_of(slot_list, first, count):
             return slot_list[:, first // STRIPE : (first + count) // STRIPE]
 
-        def gather_row(dst, j, row, offsets):
-            nc.scalar.activation(dst[:].rearrange("p (n j) -> p n j", j=PACK)[:, :, j], row.indirect(offsets), COPY)
+        def gather_into_pair(pairs, j, window, offsets):
+            half = pairs.rearrange("p (h n e) -> p h n e", h=2, e=2)[:, j // 2, :, j % 2]
+            nc.scalar.activation(half, window.indirect(offsets), COPY)
 
-        def gather_into_pair(pairs, j, row, offsets):
-            half = pairs[:].rearrange("p (h n e) -> p h n e", h=2, e=2)[:, j // 2, :, j % 2]
-            nc.scalar.activation(half, row.indirect(offsets), COPY)
-
-        def weave(pairs, name, copy=nc.scalar.copy):
-            woven = sbuf([P, HALF * PACK], BF16, name)
-            copy(
+        def weave(pairs, name):
+            woven = sbuf(list(pairs.shape), BF16, name)
+            nc.scalar.copy(
                 out=woven[:].bitcast(U32).rearrange("p (n h) -> p n h", h=2),
-                in_=pairs[:].bitcast(U32).rearrange("p (h n) -> p n h", h=2),
+                in_=pairs.bitcast(U32).rearrange("p (h n) -> p n h", h=2),
             )
             return woven
 
-        def quantize(src, count, name):
+        def quantize(src, name):
+            count = src.shape[1] // PACK
             codes = sbuf([P, count], U32, name + "_codes")
             scale = sbuf([P, count], U8, name + "_scale")
             nc.vector.quantize_mx(out=codes[:].bitcast(FP8X4), scales=scale[:], in_=src[:])
@@ -177,196 +169,208 @@ def tile_moe_plb_relu_kernel(
                 stop=True,
             )
 
-        def product_a(dst, e, b, quantized, cols):
+        def product_a(dst, g, b, quantized):
             codes, scale = quantized
-            nc.tensor.matmul_mx(
-                out=dst,
-                lhsT=wa_codes[:, e, b * P : (b + 1) * P].bitcast(FP8X4),
-                lhsT_scale=wa_scale[:, e, b * P : (b + 1) * P],
-                rhs=codes[:, cols].bitcast(FP8X4),
-                rhs_scale=scale[:, cols],
-                start=True,
-                stop=True,
-            )
+            for u in range(HALF // C1):
+                e, cols = g * (HALF // C1) + u, slice(u * C1, (u + 1) * C1)
+                nc.tensor.matmul_mx(
+                    out=dst[:, cols],
+                    lhsT=wa_codes[:, e, b * P : (b + 1) * P].bitcast(FP8X4),
+                    lhsT_scale=wa_scale[:, e, b * P : (b + 1) * P],
+                    rhs=codes[:, cols].bitcast(FP8X4),
+                    rhs_scale=scale[:, cols],
+                    start=True,
+                    stop=True,
+                )
 
-        def copy_out(src, width, name, tag=None):
-            dst = sbuf([P, width], F32, name, tag)
+        def copy_out(src, name, tag=None):
+            dst = sbuf([P, src.shape[1]], F32, name, tag)
             nc.scalar.copy(out=dst[:], in_=src)
-            return dst
+            return dst[:]
 
         def scatter(window, offsets, values):
             nc.vector.tensor_copy(window[:].indirect(offsets), values)
 
-        for j in range(1):
-            signs = sbuf([P, T], F32, "signs%d" % j)
-            nc.scalar.activation(signs[:], a_sb[j][:], SIGN)
-            nc.gpsimd.tensor_scalar(out=live[j], in0=signs[:], scalar1=1.0, scalar2=0.0, op0=ALU.min, op1=ALU.max)
+        def product(dst, left, right):
+            nc.gpsimd.tensor_tensor(out=dst, in0=left, in1=right, op=ALU.mult)
 
-        q_first = [0, P, C2, 2 * C2]
-        q_count = [P, P, C2, C2]
-        q_slots = [slots_of(list_b, first, count) for first, count in zip(q_first, q_count)]
-        dc_head = [sbuf([P, P * PACK], BF16, "dc_head%d" % g) for g in range(2)]
-        for pair in range(PACK // 2):
-            mine = parts[4 * pair : 4 * pair + 4]
-            for part in mine:
-                dh_product(*part)
-            for part in mine:
-                make_dc(*part)
-            for j in (2 * pair, 2 * pair + 1):
-                for g in range(2):
-                    gather_row(dc_head[g], j, dc_rows[j], q_slots[g])
-        head_q = [quantize(dc_head[g], P, "dc_head%d" % g) for g in range(2)]
-        live_12 = sbuf([P, 2 * T], BF16, "live_12", "signs0")
-        live.extend(live_12[:, e * T : (e + 1) * T] for e in range(2))
-        for j in (1, 2):
-            nc.vector.tensor_scalar(out=live[j], in0=a_sb[j][:], scalar1=0.0, scalar2=None, op0=ALU.is_gt)
-        dh_live = sbuf([P, T], F32, "dh_live", "dc_head0")
-        for j, first, count, index, col in parts[-2:]:
+        def clamp(dst, src, top):
+            nc.gpsimd.tensor_scalar(out=dst, in0=src, scalar1=top, scalar2=0.0, op0=ALU.min, op1=ALU.max)
+
+        live = sbuf([P, 2 * T], BF16, "live")
+        signs = sbuf([P, T], F32, "signs")
+        nc.scalar.activation(signs[:], row(a_pair, 0), SIGN)
+        clamp(live[:, :T], signs[:], 1.0)
+        small = sbuf([P, T], F32, "small")
+        large = sbuf([P, T], F32, "large")
+        clamp(small[:], row(a_pair, 2), 2.0**-23)
+        nc.gpsimd.tensor_scalar(out=large[:], in0=small[:], scalar1=2.0**127, scalar2=2.0**22, op0=ALU.mult, op1=ALU.mult)
+        clamp(live[:, T:], large[:], 1.0)
+
+        head_slots = [slots_of(list_b, g * P, P) for g in range(2)]
+        dc_rows = [sbuf([P, T], BF16, "dc_row%d" % j)[:] for j in range(PACK)]
+        dc_0 = sbuf([P, P * PACK], BF16, "dc_0")
+        pairs = sbuf([P, P * PACK], BF16, "dc_1_pairs")[:]
+        for j in range(PACK):
+            dh_row(j)
+            for t in range(PARTS):
+                nc.vector.scalar_tensor_tensor(
+                    out=dc_rows[j][:, tokens(t)],
+                    in0=row(a_pair, j)[:, tokens(t)],
+                    scalar=0.0,
+                    in1=dh_part(j, t),
+                    op0=ALU.max,
+                    op1=ALU.mult,
+                )
+            by_row = dc_0[:].rearrange("p (n j) -> p n j", j=PACK)
+            nc.scalar.activation(by_row[:, :, j], dc_rows[j].indirect(head_slots[0]), COPY)
+            gather_into_pair(pairs, j, dc_rows[j], head_slots[1])
+        dc_1 = weave(pairs, "dc_1")
+
+        def mask_odd(dst, t, rows=slice(0, 2)):
             nc.vector.scalar_tensor_tensor(
-                out=dh_live[:, first : first + count],
-                in0=a_sb[j][:, first : first + count],
+                out=two_rows(dst)[:, rows, :],
+                in0=two_rows(a_pair[1][:])[:, rows, tokens(t)],
                 scalar=0.0,
-                in1=dh_banks[index][:, col : col + count],
+                in1=two_rows(dh_banks[1][t][:])[:, rows, :],
                 op0=ALU.is_gt,
                 op1=ALU.mult,
             )
 
-        first_bank = bank(6, "q_bank")
-        product_b(first_bank[:, :P], 0, 0, head_q[0])
-        other_bank = bank(7, "q_bank")
+        first = quantize(dc_0, "dc_0")
+        dh_odd = [sbuf([P, BANK], F32, "dh_odd%d" % t, "dc_0" if t == 0 else None)[:] for t in range(PARTS)]
+        mask_odd(dh_odd[2], 2)
+        mask_odd(dh_odd[1], 1, slice(1, 2))
+        mask_odd(dh_odd[0], 0)
+        second = quantize(dc_1, "dc_1")
+        late = sbuf([P, BANK], F32, "late", "dc_1_pairs")[:]
+        mask_odd(late, 1, slice(0, 1))
+
+        lone = bank(6, "q_bank")
+        product_b(lone[:, :P], 0, 0, first)
+        three = bank(7, "q_bank")
         for b in range(1, BLOCKS):
-            product_b(other_bank[:, (b - 1) * P : b * P], 0, b, head_q[0])
-        stage = sbuf([P, C2 * PACK], BF16, "stage", "a2")
-        q00 = stage[:, 3 * P : 5 * P].bitcast(F32)
-        nc.scalar.copy(out=q00, in_=first_bank[:, :P])
+            product_b(three[:, (b - 1) * P : b * P], 0, b, first)
+        q00 = copy_out(lone[:, :P], "q00")
         q_head = sbuf([P, (LAST + BLOCKS) * P], F32, "q_head")
-        nc.scalar.copy(out=q_head[:, : LAST * P], in_=other_bank[:, : LAST * P])
-        second_bank = bank(6, "q_bank")
+        nc.scalar.copy(out=q_head[:, : LAST * P], in_=three[:, : LAST * P])
+        four = bank(5, "q_bank")
         for b in range(BLOCKS):
             place = (b + 1) % BLOCKS
-            product_b(second_bank[:, place * P : (place + 1) * P], 0, b, head_q[1])
-        nc.scalar.copy(out=q_head[:, LAST * P :], in_=second_bank[:])
+            product_b(four[:, place * P : (place + 1) * P], 0, b, second)
+        nc.scalar.copy(out=q_head[:, LAST * P :], in_=four[:])
         q_tok = [sbuf([P, T], F32, "q_tok%d" % b) for b in range(LAST)]
-        scatter(q_tok[0], q_slots[0], q00)
+        scatter(q_tok[0], head_slots[0], q00)
         for b in range(1, LAST):
-            scatter(q_tok[b], q_slots[0], q_head[:, (b - 1) * P : b * P])
+            scatter(q_tok[b], head_slots[0], q_head[:, (b - 1) * P : b * P])
         for b in range(LAST):
-            scatter(q_tok[b], q_slots[1], q_head[:, (BLOCKS + b) * P : (BLOCKS + b + 1) * P])
+            scatter(q_tok[b], head_slots[1], q_head[:, (BLOCKS + b) * P : (BLOCKS + b + 1) * P])
 
-        def product(dst, left, right):
-            nc.gpsimd.tensor_tensor(out=dst, in0=left, in1=right, op=ALU.mult)
+        da_odd = sbuf([P, 2 * T], BF16, "da_odd", "dc_1")[:]
+        for t in (2, 0):
+            product(two_rows(da_odd)[:, :, tokens(t)], two_rows(dh_odd[t]), two_rows(c_pair[1][:])[:, :, tokens(t)])
+        for e, src in enumerate((late[:, :HALF], dh_odd[1][:, HALF:])):
+            product(two_rows(da_odd)[:, e, tokens(1)], src, two_rows(c_pair[1][:])[:, e, tokens(1)])
 
-        c_first = sbuf([P, 2 * T], F32, "c_first", "dc_head1")
-        for j in range(2):
-            product(c_first[:, j * T : (j + 1) * T], c_sb[j][:], live[j])
-        da_rows = [sbuf([P, T], BF16, "da_row%d" % j) for j in (0, 1, 3)]
-        product(da_rows[2][:], dh_live[:], c_sb[3][:])
-
-        def half_banks(indices):
+        def sums_in(indices):
             banks = [bank(index, "sums_bank") for index in indices]
-            return [banks[0][:, :HALF], banks[1][:, :HALF], banks[1][:, HALF:], banks[2][:, :HALF], banks[1][:]]
+            return [banks[0][:, :HALF], banks[1][:, :HALF], banks[1][:, HALF:], banks[2][:, :HALF]], banks[1][:]
 
-        def copy_three(sums, name):
-            first = copy_out(sums[0], HALF, name + "_0")
-            both = copy_out(sums[BLOCKS], BANK, name + "_12")
-            return [first[:], both[:, :HALF], both[:, HALF:]]
+        def copy_three(sums, middle, name):
+            alone = copy_out(sums[0], name + "_0")
+            both = copy_out(middle, name + "_12")
+            return [alone, both[:, :HALF], both[:, HALF:]]
 
-        def copy_dh(dst, index, count):
-            nc.scalar.copy(out=dst, in_=dh_banks[index][:, :count])
+        def woven_piece(pairs, rows, slots, name, order=range(PACK)):
+            for j in order:
+                gather_into_pair(pairs, j, rows[j], slots)
+            return weave(pairs, name)
 
-        pairs = stage
-        for first in (0, P):
-            for e in range(2):
-                dst = pairs[:, 2 * first : 2 * (first + P)].rearrange("p (n e) -> p n e", e=2)[:, :, e]
-                nc.scalar.activation(dst, dc_rows[e].indirect(slots_of(list_b, C2 + first, P)), COPY)
-        for j in range(2, PACK):
-            gather_into_pair(pairs, j, dc_rows[j], q_slots[2])
-        dc_2 = weave(pairs, "dc_2")
-        q2_q = quantize(dc_2, C2, "dc_2")
-        q_tok.append(sbuf([P, T], F32, "q_tok%d" % LAST, "a2"))
+        slots = slots_of(list_b, C2, C2)
+        dc_2 = woven_piece(sbuf([P, C2 * PACK], BF16, "dc_2_pairs", "dc_0_codes")[:], dc_rows, slots, "dc_2")
+        quantized = quantize(dc_2, "dc_2")
+        q_tok.append(sbuf([P, T], F32, "q_tok%d" % LAST, "dc_0_codes"))
         scatter(q_tok[LAST], slots_of(list_b, 0, C2), q_head[:, (LAST - 1) * P : BLOCKS * P])
-        banks = [bank(index, "q_bank") for index in (6, 7)]
-        sums = [banks[b // 2][:, (b % 2) * HALF : (b % 2 + 1) * HALF] for b in range(BLOCKS)]
-        for b in (0, 2, 3):
-            product_b(sums[b], 1, b, q2_q)
-        dh_01 = sbuf([P, 2 * T], F32, "dh_01", "dc_head1_codes")
-        dh_2 = sbuf([P, T], F32, "dh_2", "dc_head1_scale")
-        for g in range(3):
-            copy_dh(dh_01[:, g * BANK : (g + 1) * BANK], g, BANK)
-        q2 = [copy_out(sums[0], C2, "q2_0")]
-        product_b(sums[1], 1, 1, q2_q)
-        q2.extend(copy_out(sums[b], C2, "q2_%d" % b) for b in range(1, LAST))
-        for b in range(LAST):
-            scatter(q_tok[b], q_slots[2], q2[b][:])
-
-        c_2 = sbuf([P, T], F32, "c_2", "dc_2")
-        product(c_2[:], c_sb[2][:], live[2])
-        for j in range(2):
-            product(da_rows[j][:], dh_01[:, j * T : (j + 1) * T], c_first[:, j * T : (j + 1) * T])
-
-        pairs = sbuf([P, C2 * PACK], BF16, "dc_3_pairs", "dc_head0_scale")
-        for j in range(PACK):
-            gather_into_pair(pairs, j, dc_rows[j], q_slots[3])
-        dc_3 = weave(pairs, "dc_3")
-        q2.append(copy_out(sums[LAST], C2, "q2_%d" % LAST, "dc_head0_scale"))
-        copy_dh(dh_2[:, :BANK], 3, BANK)
-        copy_dh(dh_2[:, BANK:], 4, HALF)
-        q3_q = quantize(dc_3, C2, "dc_3")
-        scatter(q_tok[LAST], q_slots[2], q2[LAST][:])
-        sums = half_banks((0, 1, 2))
+        sums, middle = sums_in((3, 4, 6))
         for b in range(BLOCKS):
-            product_b(sums[b], 2, b, q3_q)
-        q3 = copy_three(sums, "q3")
+            product_b(sums[b], 1, b, quantized)
+        dh_even = sbuf([P, 2 * BANK], F32, "dh_even", "dc_1_codes")
+        for t in range(2):
+            nc.scalar.copy(out=two_rows(dh_even[:])[:, :, tokens(t)], in_=two_rows(dh_banks[0][t][:]))
+        staged = copy_three(sums, middle, "q2")
         for b in range(LAST):
-            scatter(q_tok[b], q_slots[3], q3[b])
+            scatter(q_tok[b], slots, staged[b])
 
-        r_slots = [slots_of(list_a, g * HALF, HALF) for g in range(T // HALF)]
-        da_rows.insert(2, sbuf([P, T], BF16, "da_row2", "dc_3"))
-        product(da_rows[2][:], dh_2[:], c_2[:])
-        da_0 = sbuf([P, HALF * PACK], BF16, "da_0")
-        for j in (3, 0, 1, 2):
-            gather_row(da_0, j, da_rows[j][:], r_slots[0])
-        q3.append(copy_out(sums[LAST], C2, "q3_%d" % LAST, "dc_2"))
-        pairs = sbuf([P, HALF * PACK], BF16, "da_1_pairs", "dc_head1_scale")
-        for j in range(PACK):
-            gather_into_pair(pairs, j, da_rows[j][:], r_slots[1])
-        da_1 = weave(pairs, "da_1", nc.gpsimd.tensor_copy)
+        pairs = sbuf([P, C2 * PACK], BF16, "dc_3_pairs", "dc_2_codes")[:]
 
-        def r_products(sums, g, quantized):
-            for b in range(BLOCKS):
-                for e in range(HALF // C1):
-                    cols = slice(e * C1, (e + 1) * C1)
-                    product_a(sums[b][:, cols], g * (HALF // C1) + e, b, quantized, cols)
+        c_live = sbuf([P, 2 * T], F32, "c_live", "dc_2")
+        product(c_live[:], c_pair[0][:], live[:])
+        da_even = sbuf([P, 2 * T], BF16, "da_even")
+        product(two_rows(da_even[:])[:, :, :BANK], two_rows(dh_even[:]), two_rows(c_live[:])[:, :, :BANK])
+        da_rows = [row([da_even[:], da_odd], j) for j in range(PACK)]
 
-        quantized = quantize(da_0, HALF, "da_0")
-        scatter(q_tok[LAST], q_slots[3], q3[LAST][:])
-        sums = half_banks((3, 0, 1))
-        r_products(sums, 0, quantized)
-        r0 = copy_three(sums, "r0")
-        banks = [bank(4 + b, "r_bank") for b in range(BLOCKS)]
-        r_products([banks[b][:, :HALF] for b in range(BLOCKS)], 1, quantize(da_1, HALF, "da_1"))
-        r1 = [sbuf([P, BANK], F32, "r1_%d" % b) for b in range(BLOCKS)]
-        r_tok = [sbuf([P, T], F32, "r_tok%d" % b, "da_1" if b == LAST - 1 else None) for b in range(BLOCKS)]
-        for b in range(LAST):
-            scatter(r_tok[b], r_slots[0], r0[b])
-        nc.scalar.copy(out=r1[0][:, :HALF], in_=banks[0][:, :HALF])
-        pairs = sbuf([P, HALF * PACK], BF16, "da_2_pairs", "da_0_codes")
-        for j in range(PACK):
-            gather_into_pair(pairs, j, da_rows[j][:], r_slots[2])
-        da_2 = weave(pairs, "da_2")
-        r0.append(copy_out(sums[LAST], HALF, "r0_%d" % LAST, "da_0_codes"))
-        r_products([banks[b][:, HALF:] for b in range(BLOCKS)], 2, quantize(da_2, HALF, "da_2"))
-        scatter(r_tok[LAST], r_slots[0], r0[LAST][:])
+        held_slots, held_sums = slots, sums[LAST]
+        slots = slots_of(list_b, 2 * C2, C2)
+        dc_3 = woven_piece(pairs, dc_rows, slots, "dc_3")
+        held = pairs[:, : 2 * HALF].bitcast(F32)
+        nc.scalar.copy(out=held, in_=held_sums)
+        quantized = quantize(dc_3, "dc_3")
+        scatter(q_tok[LAST], held_slots, held)
+        dh_even_last = copy_out(dh_banks[0][2][:], "dh_even_last", "dc_3")
+        product(two_rows(da_even[:])[:, :, BANK:], two_rows(dh_even_last), two_rows(c_live[:])[:, :, BANK:])
+        sums, middle = sums_in((7, 5, 3))
         for b in range(BLOCKS):
-            cols = slice(HALF if b == 0 else 0, BANK)
-            nc.scalar.copy(out=r1[b][:, cols], in_=banks[b][:, cols])
-            scatter(r_tok[b], slots_of(list_a, HALF, BANK), r1[b][:])
+            product_b(sums[b], 2, b, quantized)
+        staged = copy_three(sums, middle, "q3")
+        for b in range(LAST):
+            scatter(q_tok[b], slots, staged[b])
+
+        r_slots = [slots_of(list_a, g * HALF, HALF) for g in range(PARTS)]
+        r_tok = [sbuf([P, T], F32, "r_tok%d" % b) for b in range(BLOCKS)]
+        da_0 = woven_piece(sbuf([P, HALF * PACK], BF16, "da_0_pairs", "dc_3_codes")[:], da_rows, r_slots[0], "da_0", (1, 3, 0, 2))
+        held = copy_out(sums[LAST], "q3_last", "dc_3_codes")
+        quantized = quantize(da_0, "da_0")
+        scatter(q_tok[LAST], slots, held)
+        sums, middle = sums_in((4, 6, 7))
+        for b in range(BLOCKS):
+            product_a(sums[b], 0, b, quantized)
+        staged = copy_three(sums, middle, "r0")
+        for b in range(LAST):
+            scatter(r_tok[b], r_slots[0], staged[b])
+
+        da_1 = woven_piece(sbuf([P, HALF * PACK], BF16, "da_1_pairs", "da_0_codes")[:], da_rows, r_slots[1], "da_1")
+        pairs = sbuf([P, HALF * PACK], BF16, "da_2_pairs", "da_0_codes")[:]
+        held = pairs[:, 2 * HALF :].bitcast(F32)
+        nc.scalar.copy(out=held, in_=sums[LAST])
+        quantized = quantize(da_1, "da_1")
+        scatter(r_tok[LAST], r_slots[0], held)
+        banks = [bank(index, "r_bank") for index in (0, 1, 2, 5)]
+        for b in range(BLOCKS):
+            product_a(banks[b][:, :HALF], 1, b, quantized)
+        for b in range(LAST - 1):
+            scatter(r_tok[b], r_slots[1], copy_out(banks[b][:, :HALF], "r1_%d" % b))
+
+        da_2 = woven_piece(pairs, da_rows, r_slots[2], "da_2")
+        held = pairs[:, : 2 * HALF].bitcast(F32)
+        nc.scalar.copy(out=held, in_=banks[LAST - 1][:, :HALF])
+        quantized = quantize(da_2, "da_2")
+        scatter(r_tok[LAST - 1], r_slots[1], held)
+        alone, middle = bank(3, "r_bank"), bank(4, "r_bank")
+        sums = [alone[:, :HALF], middle[:, :HALF], middle[:, HALF:], banks[LAST][:, HALF:]]
+        for b in range(BLOCKS):
+            product_a(sums[b], 2, b, quantized)
+        staged = copy_three(sums, middle[:], "r2")
+
+        def store_rows(queue, b, cols, total):
+            queue.dma_start(out=out[b * P : (b + 1) * P, cols], in_=total[:, cols])
+
+        for b in range(LAST):
+            scatter(r_tok[b], r_slots[2], staged[b])
             total = sbuf([P, T], F32, "total%d" % b)
-            out_rows = slice(b * P, (b + 1) * P)
-            if b < LAST:
-                nc.gpsimd.tensor_tensor(out=total[:], in0=r_tok[b][:], in1=q_tok[b][:], op=ALU.add)
-                nc.sync.dma_start(out=out[out_rows, :], in_=total[:])
-            else:
-                for queue, cols in ((nc.sync, slice(0, T // 2)), (nc.scalar, slice(T // 2, T))):
-                    nc.vector.tensor_tensor(out=total[:, cols], in0=r_tok[b][:, cols], in1=q_tok[b][:, cols], op=ALU.add)
-                    queue.dma_start(out=out[out_rows, cols], in_=total[:, cols])
+            nc.gpsimd.tensor_tensor(out=total[:], in0=r_tok[b][:], in1=q_tok[b][:], op=ALU.add)
+            store_rows(nc.sync, b, slice(0, T), total)
+        scatter(r_tok[LAST], slots_of(list_a, HALF, BANK), copy_out(banks[LAST][:], "r12_last"))
+        total = sbuf([P, T], F32, "total%d" % LAST)
+        for queue, cols in ((nc.sync, slice(0, T // 2)), (nc.scalar, slice(T // 2, T))):
+            nc.vector.tensor_tensor(out=total[:, cols], in0=r_tok[LAST][:, cols], in1=q_tok[LAST][:, cols], op=ALU.add)
+            store_rows(queue, LAST, cols, total)

@@ -303,10 +303,10 @@ def tile_moe_plb_relu_kernel(
 
         pairs = sbuf([P, C2 * PACK], BF16, "dc_3_pairs", "dc_2_codes")[:]
 
-        c_live = sbuf([P, 2 * T], F32, "c_live", "dc_2")
-        product(c_live[:], c_pair[0][:], live[:])
+        c_live = sbuf([P, 2 * BANK], F32, "c_live", "dc_2")
+        product(two_rows(c_live[:]), two_rows(c_pair[0][:])[:, :, :BANK], two_rows(live[:])[:, :, :BANK])
         da_even = sbuf([P, 2 * T], BF16, "da_even")
-        product(two_rows(da_even[:])[:, :, :BANK], two_rows(dh_even[:]), two_rows(c_live[:])[:, :, :BANK])
+        product(two_rows(da_even[:])[:, :, :BANK], two_rows(dh_even[:]), two_rows(c_live[:]))
         da_rows = [row([da_even[:], da_odd], j) for j in range(PACK)]
 
         held_slots, held_sums = slots, sums[LAST]
@@ -316,8 +316,11 @@ def tile_moe_plb_relu_kernel(
         nc.scalar.copy(out=held, in_=held_sums)
         quantized = quantize(dc_3, "dc_3")
         scatter(q_tok[LAST], held_slots, held)
-        dh_even_last = copy_out(dh_banks[0][2][:], "dh_even_last", "dc_3")
-        product(two_rows(da_even[:])[:, :, BANK:], two_rows(dh_even_last), two_rows(c_live[:])[:, :, BANK:])
+        after_three = sbuf([P, 2 * BANK], F32, "after_three", "dc_3")
+        dh_last, c_last = two_rows(after_three[:, :BANK]), two_rows(after_three[:, BANK:])
+        nc.scalar.copy(out=dh_last, in_=two_rows(dh_banks[0][2][:]))
+        product(c_last, two_rows(c_pair[0][:])[:, :, BANK:], two_rows(live[:])[:, :, BANK:])
+        product(two_rows(da_even[:])[:, :, BANK:], dh_last, c_last)
         sums, middle = sums_in((7, 5, 3))
         for b in range(BLOCKS):
             product_b(sums[b], 2, b, quantized)

@@ -73,7 +73,7 @@ def tile_moe_plb_relu_kernel(
         c_pair = [sbuf([P, 2 * T], F32, "c_pair%d" % o) for o in range(2)]
 
         def row(pair, j):
-            return pair[j % 2][:, (j // 2) * T : (j // 2 + 1) * T]
+            return pair[j // 2][:, (j % 2) * T : (j % 2 + 1) * T]
 
         list_b = sbuf([P, T // STRIPE], U16, "list_b")
         nc.sync.dma_start(out=row(a_pair, 0), in_=a_view[:, 0, :])
@@ -83,7 +83,7 @@ def tile_moe_plb_relu_kernel(
         wb_codes = sbuf([P, E2, 2 * K], U8, "wb_codes")
         nc.sync.dma_start(out=wb_codes[:].bitcast(I32), in_=wbt_words.rearrange("f s p w -> p (f s) w").bitcast(I32))
         load_scale_rows(wb_scale, wbt_scales.rearrange("f s b k -> (f s) b k"))
-        for j in (1, 3, 0, 2):
+        for j in (3, 2, 0, 1):
             nc.sync.dma_start(out=row(c_pair, j), in_=c_view[:, j, :])
         list_a = sbuf([P, T // STRIPE], U16, "list_a")
         nc.sync.dma_start(list_a[:], offs)
@@ -203,7 +203,7 @@ def tile_moe_plb_relu_kernel(
         clamp(live[:, :T], signs[:], 1.0)
         small = sbuf([P, T], F32, "small")
         large = sbuf([P, T], F32, "large")
-        clamp(small[:], row(a_pair, 2), 2.0**-23)
+        clamp(small[:], row(a_pair, 1), 2.0**-23)
         nc.gpsimd.tensor_scalar(out=large[:], in0=small[:], scalar1=2.0**127, scalar2=2.0**22, op0=ALU.mult, op1=ALU.mult)
         clamp(live[:, T:], large[:], 1.0)
 
@@ -227,24 +227,26 @@ def tile_moe_plb_relu_kernel(
             gather_into_pair(pairs, j, dc_rows[j], head_slots[1])
         dc_1 = weave(pairs, "dc_1")
 
-        def mask_odd(dst, t, rows=slice(0, 2)):
+        def mask_dh(dst, j, t):
             nc.vector.scalar_tensor_tensor(
-                out=two_rows(dst)[:, rows, :],
-                in0=two_rows(a_pair[1][:])[:, rows, tokens(t)],
+                out=dst,
+                in0=row(a_pair, j)[:, tokens(t)],
                 scalar=0.0,
-                in1=two_rows(dh_banks[1][t][:])[:, rows, :],
+                in1=dh_part(j, t),
                 op0=ALU.is_gt,
                 op1=ALU.mult,
             )
 
         first = quantize(dc_0, "dc_0")
-        dh_odd = [sbuf([P, BANK], F32, "dh_odd%d" % t, "dc_0" if t == 0 else None)[:] for t in range(PARTS)]
-        mask_odd(dh_odd[2], 2)
-        mask_odd(dh_odd[1], 1, slice(1, 2))
-        mask_odd(dh_odd[0], 0)
+        dh_3 = sbuf([P, T], F32, "dh_3")
+        dh_2 = sbuf([P, BANK], F32, "dh_2", "dc_0")
+        dh_2_last = sbuf([P, HALF], F32, "dh_2_last", "dc_1_pairs")
+        for t in reversed(range(PARTS)):
+            mask_dh(dh_3[:, tokens(t)], 3, t)
+        for t in range(PARTS - 1):
+            mask_dh(dh_2[:, tokens(t)], 2, t)
         second = quantize(dc_1, "dc_1")
-        late = sbuf([P, BANK], F32, "late", "dc_1_pairs")[:]
-        mask_odd(late, 1, slice(0, 1))
+        mask_dh(dh_2_last[:], 2, PARTS - 1)
 
         lone = bank(6, "q_bank")
         product_b(lone[:, :P], 0, 0, first)
@@ -254,7 +256,7 @@ def tile_moe_plb_relu_kernel(
         q00 = copy_out(lone[:, :P], "q00")
         q_head = sbuf([P, (LAST + BLOCKS) * P], F32, "q_head")
         nc.scalar.copy(out=q_head[:, : LAST * P], in_=three[:, : LAST * P])
-        four = bank(5, "q_bank")
+        four = bank(6, "q_bank")
         for b in range(BLOCKS):
             place = (b + 1) % BLOCKS
             product_b(four[:, place * P : (place + 1) * P], 0, b, second)
@@ -266,11 +268,10 @@ def tile_moe_plb_relu_kernel(
         for b in range(LAST):
             scatter(q_tok[b], head_slots[1], q_head[:, (BLOCKS + b) * P : (BLOCKS + b + 1) * P])
 
-        da_odd = sbuf([P, 2 * T], BF16, "da_odd", "dc_1")[:]
-        for t in (2, 0):
-            product(two_rows(da_odd)[:, :, tokens(t)], two_rows(dh_odd[t]), two_rows(c_pair[1][:])[:, :, tokens(t)])
-        for e, src in enumerate((late[:, :HALF], dh_odd[1][:, HALF:])):
-            product(two_rows(da_odd)[:, e, tokens(1)], src, two_rows(c_pair[1][:])[:, e, tokens(1)])
+        da_late = sbuf([P, 2 * T], BF16, "da_late", "dc_1")[:]
+        product(da_late[:, T:], dh_3[:], row(c_pair, 3))
+        product(da_late[:, :BANK], dh_2[:], row(c_pair, 2)[:, :BANK])
+        product(da_late[:, BANK:T], dh_2_last[:], row(c_pair, 2)[:, BANK:])
 
         def sums_in(indices):
             banks = [bank(index, "sums_bank") for index in indices]
@@ -291,13 +292,16 @@ def tile_moe_plb_relu_kernel(
         quantized = quantize(dc_2, "dc_2")
         q_tok.append(sbuf([P, T], F32, "q_tok%d" % LAST, "dc_0_codes"))
         scatter(q_tok[LAST], slots_of(list_b, 0, C2), q_head[:, (LAST - 1) * P : BLOCKS * P])
-        sums, middle = sums_in((3, 4, 6))
-        for b in range(BLOCKS):
+        ends, middle = bank(6, "sums_bank"), bank(7, "sums_bank")
+        sums = [ends[:, :HALF], middle[:, :HALF], middle[:, HALF:], ends[:, HALF:]]
+        for b in range(LAST):
             product_b(sums[b], 1, b, quantized)
         dh_even = sbuf([P, 2 * BANK], F32, "dh_even", "dc_1_codes")
-        for t in range(2):
-            nc.scalar.copy(out=two_rows(dh_even[:])[:, :, tokens(t)], in_=two_rows(dh_banks[0][t][:]))
-        staged = copy_three(sums, middle, "q2")
+        for j in range(2):
+            for t in range(PARTS - 1):
+                nc.scalar.copy(out=two_rows(dh_even[:])[:, j, tokens(t)], in_=dh_part(j, t))
+        staged = copy_three(sums, middle[:], "q2")
+        product_b(sums[LAST], 1, LAST, quantized)
         for b in range(LAST):
             scatter(q_tok[b], slots, staged[b])
 
@@ -307,7 +311,7 @@ def tile_moe_plb_relu_kernel(
         product(two_rows(c_live[:]), two_rows(c_pair[0][:])[:, :, :BANK], two_rows(live[:])[:, :, :BANK])
         da_even = sbuf([P, 2 * T], BF16, "da_even")
         product(two_rows(da_even[:])[:, :, :BANK], two_rows(dh_even[:]), two_rows(c_live[:]))
-        da_rows = [row([da_even[:], da_odd], j) for j in range(PACK)]
+        da_rows = [row([da_even[:], da_late], j) for j in range(PACK)]
 
         held_slots, held_sums = slots, sums[LAST]
         slots = slots_of(list_b, 2 * C2, C2)
@@ -318,10 +322,11 @@ def tile_moe_plb_relu_kernel(
         scatter(q_tok[LAST], held_slots, held)
         after_three = sbuf([P, 2 * BANK], F32, "after_three", "dc_3")
         dh_last, c_last = two_rows(after_three[:, :BANK]), two_rows(after_three[:, BANK:])
-        nc.scalar.copy(out=dh_last, in_=two_rows(dh_banks[0][2][:]))
+        for j in range(2):
+            nc.scalar.copy(out=dh_last[:, j, :], in_=dh_part(j, PARTS - 1))
         product(c_last, two_rows(c_pair[0][:])[:, :, BANK:], two_rows(live[:])[:, :, BANK:])
         product(two_rows(da_even[:])[:, :, BANK:], dh_last, c_last)
-        sums, middle = sums_in((7, 5, 3))
+        sums, middle = sums_in((0, 1, 3))
         for b in range(BLOCKS):
             product_b(sums[b], 2, b, quantized)
         staged = copy_three(sums, middle, "q3")
@@ -330,11 +335,11 @@ def tile_moe_plb_relu_kernel(
 
         r_slots = [slots_of(list_a, g * HALF, HALF) for g in range(PARTS)]
         r_tok = [sbuf([P, T], F32, "r_tok%d" % b) for b in range(BLOCKS)]
-        da_0 = woven_piece(sbuf([P, HALF * PACK], BF16, "da_0_pairs", "dc_3_codes")[:], da_rows, r_slots[0], "da_0", (1, 3, 0, 2))
+        da_0 = woven_piece(sbuf([P, HALF * PACK], BF16, "da_0_pairs", "dc_3_codes")[:], da_rows, r_slots[0], "da_0", (2, 3, 0, 1))
         held = copy_out(sums[LAST], "q3_last", "dc_3_codes")
         quantized = quantize(da_0, "da_0")
         scatter(q_tok[LAST], slots, held)
-        sums, middle = sums_in((4, 6, 7))
+        sums, middle = sums_in((4, 7, 6))
         for b in range(BLOCKS):
             product_a(sums[b], 0, b, quantized)
         staged = copy_three(sums, middle, "r0")

@@ -59,7 +59,7 @@ def tile_moe_plb_relu_kernel(
         wb_scale = sbuf([P, E2, K], U8, "wb_scale")
         wa_scale = sbuf([P, E1, K], U8, "wa_scale")
         for plane in (w2_scale_raw, dy_scale, wb_scale, wa_scale):
-            nc.gpsimd.memset(plane[:].bitcast(I32), 0)
+            nc.vector.memset(plane[:].bitcast(I32), 0)
 
         w2_raw = sbuf([P, PASSES, H], I32, "w2_raw")
         nc.sync.dma_start(out=w2_raw[:], in_=w2t_words.rearrange("s p i d -> p s (i d)").bitcast(I32))
@@ -201,11 +201,14 @@ def tile_moe_plb_relu_kernel(
         signs = sbuf([P, T], F32, "signs")
         nc.scalar.activation(signs[:], row(a_pair, 0), SIGN)
         clamp(live[:, :T], signs[:], 1.0)
-        small = sbuf([P, T], F32, "small")
-        large = sbuf([P, T], F32, "large")
-        clamp(small[:], row(a_pair, 1), 2.0**-23)
+        more_signs = sbuf([P, BANK], F32, "more_signs")
+        nc.scalar.activation(more_signs[:], row(a_pair, 1)[:, :BANK], SIGN)
+        clamp(live[:, T : T + BANK], more_signs[:], 1.0)
+        small = sbuf([P, HALF], F32, "small")
+        large = sbuf([P, HALF], F32, "large")
+        clamp(small[:], row(a_pair, 1)[:, BANK:], 2.0**-23)
         nc.gpsimd.tensor_scalar(out=large[:], in0=small[:], scalar1=2.0**127, scalar2=2.0**22, op0=ALU.mult, op1=ALU.mult)
-        clamp(live[:, T:], large[:], 1.0)
+        clamp(live[:, T + BANK :], large[:], 1.0)
 
         head_slots = [slots_of(list_b, g * P, P) for g in range(2)]
         dc_rows = [sbuf([P, T], BF16, "dc_row%d" % j)[:] for j in range(PACK)]

@@ -242,14 +242,12 @@ def tile_moe_plb_relu_kernel(
 
         first = quantize(dc_0, "dc_0")
         dh_3 = sbuf([P, T], F32, "dh_3")
-        dh_2 = sbuf([P, BANK], F32, "dh_2", "dc_0")
-        dh_2_last = sbuf([P, HALF], F32, "dh_2_last", "dc_1_pairs")
+        dh_2 = sbuf([P, T], F32, "dh_2", "dc_0")
         for t in reversed(range(PARTS)):
             mask_dh(dh_3[:, tokens(t)], 3, t)
-        for t in range(PARTS - 1):
+        for t in range(PARTS):
             mask_dh(dh_2[:, tokens(t)], 2, t)
         second = quantize(dc_1, "dc_1")
-        mask_dh(dh_2_last[:], 2, PARTS - 1)
 
         lone = bank(6, "q_bank")
         product_b(lone[:, :P], 0, 0, first)
@@ -273,8 +271,7 @@ def tile_moe_plb_relu_kernel(
 
         da_late = sbuf([P, 2 * T], BF16, "da_late", "dc_1")[:]
         product(da_late[:, T:], dh_3[:], row(c_pair, 3))
-        product(da_late[:, :BANK], dh_2[:], row(c_pair, 2)[:, :BANK])
-        product(da_late[:, BANK:T], dh_2_last[:], row(c_pair, 2)[:, BANK:])
+        product(da_late[:, :T], dh_2[:], row(c_pair, 2))
 
         def sums_in(indices):
             banks = [bank(index, "sums_bank") for index in indices]

@@ -379,6 +379,6 @@ def tile_moe_plb_relu_kernel(
             store_rows(nc.sync, b, slice(0, T), total)
         scatter(r_tok[LAST], slots_of(list_a, HALF, BANK), copy_out(banks[LAST][:], "r12_last"))
         total = sbuf([P, T], F32, "total%d" % LAST)
-        for queue, cols in ((nc.sync, slice(0, T // 2)), (nc.scalar, slice(T // 2, T))):
+        for queue, cols in ((nc.sync, slice(0, HALF)), (nc.scalar, slice(HALF, BANK)), (nc.sync, slice(BANK, T))):
             nc.vector.tensor_tensor(out=total[:, cols], in0=r_tok[LAST][:, cols], in1=q_tok[LAST][:, cols], op=ALU.add)
             store_rows(queue, LAST, cols, total)

@@ -16,7 +16,6 @@ FP8X4 = mybir.dt.float8_e4m3fn_x4
 FP4X4 = mybir.dt.float4_e2m1fn_x4
 ALU = mybir.AluOpType
 COPY = mybir.ActivationFunctionType.Copy
-SIGN = mybir.ActivationFunctionType.Sign
 
 P = 128
 PACK = 4
@@ -24,12 +23,11 @@ PASSES = N // (P * PACK)
 BANK = 512
 HALF = BANK // 2
 PARTS = T // HALF
-BLOCKS = K // P
-LAST = BLOCKS - 1
 STRIPE = 16
 QUADRANT = 32
 SCALE_ROWS = 4
 LINE = 16
+WIDE = 1024
 
 
 def tile_moe_plb_relu_kernel(
@@ -54,6 +52,9 @@ def tile_moe_plb_relu_kernel(
         def two_rows(flat):
             return flat.rearrange("p (e t) -> p e t", e=2)
 
+        def part(t):
+            return slice(t * HALF, (t + 1) * HALF)
+
         w2_scale_raw = sbuf([P, PASSES, H], U8, "w2_scale_raw")
         dy_scale = sbuf([P, PASSES, T], U8, "dy_scale")
         wb_scale = sbuf([P, E2, K], U8, "wb_scale")
@@ -67,24 +68,29 @@ def tile_moe_plb_relu_kernel(
         dy_codes = sbuf([P, PASSES, T], I32, "dy_codes")
         nc.sync.dma_start(out=dy_codes[:], in_=dy_words.rearrange("s p t d -> p s (t d)").bitcast(I32))
         load_scale_rows(dy_scale, dy_scales, SCALE_ROWS)
-        a_view = a.rearrange("(p j) t -> p j t", j=PACK)
-        c_view = c.rearrange("(p j) t -> p j t", j=PACK)
-        a_pair = [sbuf([P, 2 * T], F32, "a_pair%d" % o) for o in range(2)]
-        c_pair = [sbuf([P, 2 * T], F32, "c_pair%d" % o) for o in range(2)]
 
-        def row(pair, j):
-            return pair[j // 2][:, (j % 2) * T : (j % 2 + 1) * T]
+        a_view = a.rearrange("(p h e) t -> h p e t", h=2, e=2)
+        c_view = c.rearrange("(p h e) t -> h p e t", h=2, e=2)
+        a_early = sbuf([P, 2, T], F32, "a_early")
+        a_late = []
+
+        def load_late(first, count):
+            piece = sbuf([P, 2, count * HALF], F32, "a_late%d" % first)
+            nc.sync.dma_start(out=piece[:], in_=a_view[1][:, :, first * HALF : (first + count) * HALF])
+            a_late.extend(piece[:, :, part(t)] for t in range(count))
 
         list_b = sbuf([P, T // STRIPE], U16, "list_b")
-        nc.sync.dma_start(out=row(a_pair, 0), in_=a_view[:, 0, :])
+        nc.sync.dma_start(out=a_early[:, 0, :], in_=a_view[0][:, 0, :])
         nc.sync.dma_start(list_b[:], offs2)
-        for j in range(1, PACK):
-            nc.sync.dma_start(out=row(a_pair, j), in_=a_view[:, j, :])
+        nc.sync.dma_start(out=a_early[:, 1, :], in_=a_view[0][:, 1, :])
+        load_late(0, 2)
+        load_late(2, 1)
         wb_codes = sbuf([P, E2, 2 * K], U8, "wb_codes")
         nc.sync.dma_start(out=wb_codes[:].bitcast(I32), in_=wbt_words.rearrange("f s p w -> p (f s) w").bitcast(I32))
         load_scale_rows(wb_scale, wbt_scales.rearrange("f s b k -> (f s) b k"))
-        for j in (3, 2, 0, 1):
-            nc.sync.dma_start(out=row(c_pair, j), in_=c_view[:, j, :])
+        c_pair = [sbuf([P, 2, T], F32, "c_pair%d" % h) for h in range(2)]
+        for h in range(2):
+            nc.sync.dma_start(out=c_pair[h][:], in_=c_view[h])
         list_a = sbuf([P, T // STRIPE], U16, "list_a")
         nc.sync.dma_start(list_a[:], offs)
         wa_codes = sbuf([P, E1, K], I32, "wa_codes")
@@ -93,10 +99,11 @@ def tile_moe_plb_relu_kernel(
 
         w2_codes = sbuf([P, PASSES, H], I32, "w2_codes")
         w2_scale = sbuf([P, PASSES, H], U8, "w2_scale")
-        nc.vector.tensor_copy(
-            out=w2_codes[:].rearrange("p s (j g m) -> p s g j m", j=PACK, m=LINE // PACK),
-            in_=w2_raw[:].rearrange("p s (g m j) -> p s g j m", j=PACK, m=LINE // PACK),
-        )
+        for s, move in enumerate((nc.vector.tensor_copy, nc.scalar.copy)):
+            move(
+                out=w2_codes[:, s, :].bitcast(U32).rearrange("p (j g m) -> p g j m", j=PACK, m=LINE // PACK),
+                in_=w2_raw[:, s, :].bitcast(U32).rearrange("p (g m j) -> p g j m", j=PACK, m=LINE // PACK),
+            )
         nc.vector.tensor_copy(
             out=w2_scale[:].rearrange("p s (j g m) -> p s g j m", j=PACK, m=LINE),
             in_=w2_scale_raw[:].rearrange("p s (g m j) -> p s g j m", j=PACK, m=LINE),
@@ -114,47 +121,67 @@ def tile_moe_plb_relu_kernel(
                 stop=True,
             )
 
-        dh_banks = [[bank(o * PARTS + t, "dh_bank") for t in range(PARTS)] for o in range(2)]
+        def dh_into(dst, j, tokens):
+            cols = slice(j * P, (j + 1) * P)
+            for s in range(PASSES):
+                nc.tensor.matmul_mx(
+                    out=dst,
+                    lhsT=w2_codes[:, s, cols].bitcast(FP8X4),
+                    lhsT_scale=w2_scale[:, s, cols],
+                    rhs=dy_codes[:, s, tokens].bitcast(FP8X4),
+                    rhs_scale=dy_scale[SCALE_ROWS:, s, tokens],
+                    start=(s == 0),
+                    stop=(s == PASSES - 1),
+                )
 
-        def tokens(t):
-            return slice(t * HALF, (t + 1) * HALF)
+        def gated(dst, saved, sums, test):
+            nc.vector.scalar_tensor_tensor(out=dst, in0=saved, scalar=0.0, in1=sums, op0=test, op1=ALU.mult)
 
-        def dh_part(j, t):
-            return dh_banks[j % 2][t][:, tokens(j // 2)]
+        long, short = slice(0, BANK), slice(BANK, T)
+        early_banks = [bank(n, "dh_bank") for n in range(PARTS)]
+        dc_rows = [sbuf([P, T], BF16, "dc_row%d" % e) for e in range(2)]
+        dh_into(early_banks[0][:], 0, long)
+        gated(dc_rows[0][:, long], a_early[:, 0, long], early_banks[0][:], ALU.max)
+        for e in range(2):
+            dh_into(early_banks[1][:, part(e)], e, short)
+        for e in range(2):
+            gated(dc_rows[e][:, short], a_early[:, e, short], early_banks[1][:, part(e)], ALU.max)
+        dh_into(early_banks[2][:], 1, long)
+        gated(dc_rows[1][:, long], a_early[:, 1, long], early_banks[2][:], ALU.max)
 
-        def dh_row(j):
-            for t in range(PARTS):
-                for s in range(PASSES):
-                    nc.tensor.matmul_mx(
-                        out=dh_part(j, t),
-                        lhsT=w2_codes[:, s, j * P : (j + 1) * P].bitcast(FP8X4),
-                        lhsT_scale=w2_scale[:, s, j * P : (j + 1) * P],
-                        rhs=dy_codes[:, s, tokens(t)].bitcast(FP8X4),
-                        rhs_scale=dy_scale[SCALE_ROWS:, s, tokens(t)],
-                        start=(s == 0),
-                        stop=(s == PASSES - 1),
-                    )
-
-        def slots_of(slot_list, first, count):
-            return slot_list[:, first // STRIPE : (first + count) // STRIPE]
-
-        def gather_into_pair(pairs, j, window, offsets):
-            half = pairs.rearrange("p (h n e) -> p h n e", h=2, e=2)[:, j // 2, :, j % 2]
-            nc.scalar.activation(half, window.indirect(offsets), COPY)
-
-        def weave(pairs, name):
-            woven = sbuf(list(pairs.shape), BF16, name)
-            nc.scalar.copy(
-                out=woven[:].bitcast(U32).rearrange("p (n h) -> p n h", h=2),
-                in_=pairs.bitcast(U32).rearrange("p (h n) -> p n h", h=2),
+        late_banks = [bank(PARTS + t, "dh_bank") for t in range(PARTS)]
+        dc_late = sbuf([P, 2 * T], BF16, "dc_late")
+        for t in range(PARTS):
+            for e in range(2):
+                dh_into(late_banks[t][:, part(e)], 2 + e, part(t))
+            gated(
+                dc_late[:, t * BANK : (t + 1) * BANK].rearrange("p (t e) -> p t e", e=2),
+                a_late[t].rearrange("p e t -> p t e"),
+                late_banks[t][:].rearrange("p (e t) -> p t e", e=2),
+                ALU.max,
             )
-            return woven
 
-        def quantize(src, name):
-            count = src.shape[1] // PACK
-            codes = sbuf([P, count], U32, name + "_codes")
-            scale = sbuf([P, count], U8, name + "_scale")
-            nc.vector.quantize_mx(out=codes[:].bitcast(FP8X4), scales=scale[:], in_=src[:])
+        def slots_of(slot_list, first, stop):
+            return slot_list[:, first // STRIPE : stop // STRIPE]
+
+        def gather_pairs(dst, pairs, slots):
+            nc.vector.tensor_copy(dst, pairs[:].bitcast(U32).indirect(slots))
+
+        dc_picked = [sbuf([P, 2 * HALF], U32, "dc_picked%d" % f) for f in range(E2)]
+        for e in range(2):
+            for f in range(E2):
+                dst = dc_picked[f][:, :HALF].bitcast(BF16).rearrange("p (n e) -> p n e", e=2)[:, :, e]
+                nc.scalar.activation(dst, dc_rows[e][:].indirect(slots_of(list_b, f * C2, (f + 1) * C2)), COPY)
+
+        def quantized_piece(picked, name):
+            woven = sbuf([P, HALF * PACK], BF16, name)
+            nc.vector.tensor_copy(
+                out=woven[:].bitcast(U32).rearrange("p (n h) -> p n h", h=2),
+                in_=picked[:].rearrange("p (h n) -> p n h", h=2),
+            )
+            codes = sbuf([P, HALF], U32, name + "_codes")
+            scale = sbuf([P, HALF], U8, name + "_scale")
+            nc.vector.quantize_mx(out=codes[:].bitcast(FP8X4), scales=scale[:], in_=woven[:])
             return codes, scale
 
         def product_b(dst, f, b, quantized):
@@ -183,202 +210,93 @@ def tile_moe_plb_relu_kernel(
                     stop=True,
                 )
 
-        def copy_out(src, name, tag=None):
-            dst = sbuf([P, src.shape[1]], F32, name, tag)
-            nc.scalar.copy(out=dst[:], in_=src)
-            return dst[:]
+        def scalar_scatter(window, offsets, values):
+            nc.scalar.activation(window[:].indirect(offsets), values, COPY)
 
-        def scatter(window, offsets, values):
+        def vector_scatter(window, offsets, values):
             nc.vector.tensor_copy(window[:].indirect(offsets), values)
 
-        def product(dst, left, right):
-            nc.gpsimd.tensor_tensor(out=dst, in0=left, in1=right, op=ALU.mult)
+        q_tok = [sbuf([P, T], F32, "q_tok%d" % b) for b in range(4)]
+        r_tok = [sbuf([P, WIDE if b == 3 else T], F32, "r_tok%d" % b) for b in range(4)]
 
-        def clamp(dst, src, top):
-            nc.gpsimd.tensor_scalar(out=dst, in0=src, scalar1=top, scalar2=0.0, op0=ALU.min, op1=ALU.max)
+        dc_q = []
+        groups = [(f, b) for f in range(E2) for b in (0, 2, 3)][:-1]
+        for n in range(0, len(groups), 2):
+            sums = bank(6 + (n // 2) % 2, "q_bank")
+            for place, (f, b) in enumerate(groups[n : n + 2]):
+                if f == len(dc_q):
+                    gather_pairs(dc_picked[f][:, HALF:], dc_late, slots_of(list_b, f * C2, (f + 1) * C2))
+                    dc_q.append(quantized_piece(dc_picked[f], "dc_%d" % f))
+                product_b(sums[:, part(place)], f, b, dc_q[f])
+            width = HALF * len(groups[n : n + 2])
+            staged = sbuf([P, width], F32, "q_staged%d" % n)
+            nc.scalar.copy(out=staged[:], in_=sums[:, :width])
+            for place, (f, b) in enumerate(groups[n : n + 2]):
+                scalar_scatter(q_tok[b], slots_of(list_b, f * C2, (f + 1) * C2), staged[:, part(place)])
 
-        live = sbuf([P, 2 * T], BF16, "live")
-        signs = sbuf([P, T], F32, "signs")
-        nc.scalar.activation(signs[:], row(a_pair, 0), SIGN)
-        clamp(live[:, :T], signs[:], 1.0)
-        more_signs = sbuf([P, BANK], F32, "more_signs")
-        nc.scalar.activation(more_signs[:], row(a_pair, 1)[:, :BANK], SIGN)
-        clamp(live[:, T : T + BANK], more_signs[:], 1.0)
-        small = sbuf([P, HALF], F32, "small")
-        large = sbuf([P, HALF], F32, "large")
-        clamp(small[:], row(a_pair, 1)[:, BANK:], 2.0**-23)
-        nc.gpsimd.tensor_scalar(out=large[:], in0=small[:], scalar1=2.0**127, scalar2=2.0**22, op0=ALU.mult, op1=ALU.mult)
-        clamp(live[:, T + BANK :], large[:], 1.0)
-
-        head_slots = [slots_of(list_b, g * P, P) for g in range(2)]
-        dc_rows = [sbuf([P, T], BF16, "dc_row%d" % j)[:] for j in range(PACK)]
-        dc_0 = sbuf([P, P * PACK], BF16, "dc_0")
-        pairs = sbuf([P, P * PACK], BF16, "dc_1_pairs")[:]
-        for j in range(PACK):
-            dh_row(j)
-            for t in range(PARTS):
-                nc.vector.scalar_tensor_tensor(
-                    out=dc_rows[j][:, tokens(t)],
-                    in0=row(a_pair, j)[:, tokens(t)],
-                    scalar=0.0,
-                    in1=dh_part(j, t),
-                    op0=ALU.max,
-                    op1=ALU.mult,
-                )
-            by_row = dc_0[:].rearrange("p (n j) -> p n j", j=PACK)
-            nc.scalar.activation(by_row[:, :, j], dc_rows[j].indirect(head_slots[0]), COPY)
-            gather_into_pair(pairs, j, dc_rows[j], head_slots[1])
-        dc_1 = weave(pairs, "dc_1")
-
-        def mask_dh(dst, j, t):
-            nc.vector.scalar_tensor_tensor(
-                out=dst,
-                in0=row(a_pair, j)[:, tokens(t)],
-                scalar=0.0,
-                in1=dh_part(j, t),
-                op0=ALU.is_gt,
-                op1=ALU.mult,
-            )
-
-        first = quantize(dc_0, "dc_0")
-        dh_3 = sbuf([P, T], F32, "dh_3")
-        dh_2 = sbuf([P, T], F32, "dh_2", "dc_0")
-        for t in reversed(range(PARTS)):
-            mask_dh(dh_3[:, tokens(t)], 3, t)
+        masked = sbuf([P, 2, 2, T], F32, "masked", "dc_2")
+        da_pair = [sbuf([P, 2 * T], BF16, "da_pair%d" % h) for h in range(2)]
+        gated(masked[:, 0, 0, long], a_early[:, 0, long], early_banks[0][:], ALU.is_gt)
+        gated(masked[:, 0, 1, long], a_early[:, 1, long], early_banks[2][:], ALU.is_gt)
+        gated(masked[:, 0, :, short], a_early[:, :, short], two_rows(early_banks[1][:]), ALU.is_gt)
         for t in range(PARTS):
-            mask_dh(dh_2[:, tokens(t)], 2, t)
-        second = quantize(dc_1, "dc_1")
+            gated(masked[:, 1, :, part(t)], a_late[t], two_rows(late_banks[t][:]), ALU.is_gt)
+        for h in range(2):
+            for t in range(PARTS):
+                nc.gpsimd.tensor_tensor(
+                    out=da_pair[h][:, t * BANK : (t + 1) * BANK].rearrange("p (g i e) -> p g e i", i=4, e=2),
+                    in0=masked[:, h, :, part(t)].rearrange("p e (g i) -> p g e i", i=4),
+                    in1=c_pair[h][:, :, part(t)].rearrange("p e (g i) -> p g e i", i=4),
+                    op=ALU.mult,
+                )
 
-        lone = bank(6, "q_bank")
-        product_b(lone[:, :P], 0, 0, first)
-        three = bank(7, "q_bank")
-        for b in range(1, BLOCKS):
-            product_b(three[:, (b - 1) * P : b * P], 0, b, first)
-        q00 = copy_out(lone[:, :P], "q00")
-        q_head = sbuf([P, (LAST + BLOCKS) * P], F32, "q_head")
-        nc.scalar.copy(out=q_head[:, : LAST * P], in_=three[:, : LAST * P])
-        four = bank(6, "q_bank")
-        for b in range(BLOCKS):
-            place = (b + 1) % BLOCKS
-            product_b(four[:, place * P : (place + 1) * P], 0, b, second)
-        nc.scalar.copy(out=q_head[:, LAST * P :], in_=four[:])
-        q_tok = [sbuf([P, T], F32, "q_tok%d" % b) for b in range(LAST)]
-        scatter(q_tok[0], head_slots[0], q00)
-        for b in range(1, LAST):
-            scatter(q_tok[b], head_slots[0], q_head[:, (b - 1) * P : b * P])
-        for b in range(LAST):
-            scatter(q_tok[b], head_slots[1], q_head[:, (BLOCKS + b) * P : (BLOCKS + b + 1) * P])
+        q1_staged = sbuf([P, T], F32, "q1_staged")
+        sums = bank(0, "q1_bank")
+        for f in range(2):
+            product_b(sums[:, part(f)], f, 1, dc_q[f])
+        nc.vector.tensor_copy(out=q1_staged[:, :BANK], in_=sums[:])
+        sums = bank(1, "q1_bank")
+        product_b(sums[:, :HALF], 2, 1, dc_q[2])
+        nc.vector.tensor_copy(out=q1_staged[:, BANK:], in_=sums[:, :HALF])
+        vector_scatter(q_tok[1], slots_of(list_b, 0, BANK), q1_staged[:, :BANK])
+        vector_scatter(q_tok[1], slots_of(list_b, BANK, T), q1_staged[:, BANK:])
 
-        da_late = sbuf([P, 2 * T], BF16, "da_late", "dc_1")[:]
-        product(da_late[:, T:], dh_3[:], row(c_pair, 3))
-        product(da_late[:, :T], dh_2[:], row(c_pair, 2))
+        r_scalar = sbuf([P, 2, T], F32, "r_scalar")
+        r_vector = sbuf([P, 2, T], F32, "r_vector")
+        for g in range(PARTS):
+            picked = sbuf([P, 2 * HALF], U32, "da_picked%d" % g)
+            for h in range(2):
+                gather_pairs(picked[:, part(h)], da_pair[h], slots_of(list_a, g * HALF, (g + 1) * HALF))
+            quantized = quantized_piece(picked, "da_%d" % g)
+            for_scalar, for_vector = bank(5 + g, "r_bank"), bank(2 + g, "r_bank")
+            for place in range(2):
+                product_a(for_scalar[:, part(place)], g, 2 * place, quantized)
+            for place in range(2):
+                product_a(for_vector[:, part(place)], g, 2 * place + 1, quantized)
+            empty = nc.vector.tensor_copy if g == 0 else nc.scalar.copy
+            empty(out=r_scalar[:, :, part(g)], in_=two_rows(for_scalar[:]))
+            nc.vector.tensor_copy(out=r_vector[:, :, part(g)], in_=two_rows(for_vector[:]))
+            scalar_scatter(r_tok[0], slots_of(list_a, g * HALF, (g + 1) * HALF), r_scalar[:, 0, part(g)])
+        for first, stop in ((T // 2, T), (0, T // 2)):
+            scalar_scatter(r_tok[2], slots_of(list_a, first, stop), r_scalar[:, 1, first:stop])
+        for first, stop in ((0, HALF), (HALF, T)):
+            vector_scatter(r_tok[1], slots_of(list_a, first, stop), r_vector[:, 0, first:stop])
+        vector_scatter(r_tok[3], list_a[:], r_vector[:, 1, :])
 
-        def sums_in(indices):
-            banks = [bank(index, "sums_bank") for index in indices]
-            return [banks[0][:, :HALF], banks[1][:, :HALF], banks[1][:, HALF:], banks[2][:, :HALF]], banks[1][:]
-
-        def copy_three(sums, middle, name):
-            alone = copy_out(sums[0], name + "_0")
-            both = copy_out(middle, name + "_12")
-            return [alone, both[:, :HALF], both[:, HALF:]]
-
-        def woven_piece(pairs, rows, slots, name, order=range(PACK)):
-            for j in order:
-                gather_into_pair(pairs, j, rows[j], slots)
-            return weave(pairs, name)
-
-        slots = slots_of(list_b, C2, C2)
-        dc_2 = woven_piece(sbuf([P, C2 * PACK], BF16, "dc_2_pairs", "dc_0_codes")[:], dc_rows, slots, "dc_2")
-        quantized = quantize(dc_2, "dc_2")
-        q_tok.append(sbuf([P, T], F32, "q_tok%d" % LAST, "dc_0_codes"))
-        scatter(q_tok[LAST], slots_of(list_b, 0, C2), q_head[:, (LAST - 1) * P : BLOCKS * P])
-        ends, middle = bank(6, "sums_bank"), bank(7, "sums_bank")
-        sums = [ends[:, :HALF], middle[:, :HALF], middle[:, HALF:], ends[:, HALF:]]
-        for b in range(LAST):
-            product_b(sums[b], 1, b, quantized)
-        dh_even = sbuf([P, 2 * BANK], F32, "dh_even", "dc_1_codes")
-        for j in range(2):
-            for t in range(PARTS - 1):
-                nc.scalar.copy(out=two_rows(dh_even[:])[:, j, tokens(t)], in_=dh_part(j, t))
-        staged = copy_three(sums, middle[:], "q2")
-        product_b(sums[LAST], 1, LAST, quantized)
-        for b in range(LAST):
-            scatter(q_tok[b], slots, staged[b])
-
-        pairs = sbuf([P, C2 * PACK], BF16, "dc_3_pairs", "dc_2_codes")[:]
-
-        c_live = sbuf([P, 2 * BANK], F32, "c_live", "dc_2")
-        product(two_rows(c_live[:]), two_rows(c_pair[0][:])[:, :, :BANK], two_rows(live[:])[:, :, :BANK])
-        da_even = sbuf([P, 2 * T], BF16, "da_even")
-        product(two_rows(da_even[:])[:, :, :BANK], two_rows(dh_even[:]), two_rows(c_live[:]))
-        da_rows = [row([da_even[:], da_late], j) for j in range(PACK)]
-
-        held_slots, held_sums = slots, sums[LAST]
-        slots = slots_of(list_b, 2 * C2, C2)
-        dc_3 = woven_piece(pairs, dc_rows, slots, "dc_3")
-        held = pairs[:, : 2 * HALF].bitcast(F32)
-        nc.scalar.copy(out=held, in_=held_sums)
-        quantized = quantize(dc_3, "dc_3")
-        scatter(q_tok[LAST], held_slots, held)
-        after_three = sbuf([P, 2 * BANK], F32, "after_three", "dc_3")
-        dh_last, c_last = two_rows(after_three[:, :BANK]), two_rows(after_three[:, BANK:])
-        for j in range(2):
-            nc.scalar.copy(out=dh_last[:, j, :], in_=dh_part(j, PARTS - 1))
-        product(c_last, two_rows(c_pair[0][:])[:, :, BANK:], two_rows(live[:])[:, :, BANK:])
-        product(two_rows(da_even[:])[:, :, BANK:], dh_last, c_last)
-        sums, middle = sums_in((0, 1, 3))
-        for b in range(BLOCKS):
-            product_b(sums[b], 2, b, quantized)
-        staged = copy_three(sums, middle, "q3")
-        for b in range(LAST):
-            scatter(q_tok[b], slots, staged[b])
-
-        r_slots = [slots_of(list_a, g * HALF, HALF) for g in range(PARTS)]
-        r_tok = [sbuf([P, T], F32, "r_tok%d" % b) for b in range(BLOCKS)]
-        da_0 = woven_piece(sbuf([P, HALF * PACK], BF16, "da_0_pairs", "dc_3_codes")[:], da_rows, r_slots[0], "da_0", (2, 3, 0, 1))
-        held = copy_out(sums[LAST], "q3_last", "dc_3_codes")
-        quantized = quantize(da_0, "da_0")
-        scatter(q_tok[LAST], slots, held)
-        sums, middle = sums_in((4, 7, 6))
-        for b in range(BLOCKS):
-            product_a(sums[b], 0, b, quantized)
-        staged = copy_three(sums, middle, "r0")
-        for b in range(LAST):
-            scatter(r_tok[b], r_slots[0], staged[b])
-
-        da_1 = woven_piece(sbuf([P, HALF * PACK], BF16, "da_1_pairs", "da_0_codes")[:], da_rows, r_slots[1], "da_1")
-        pairs = sbuf([P, HALF * PACK], BF16, "da_2_pairs", "da_0_codes")[:]
-        held = pairs[:, 2 * HALF :].bitcast(F32)
-        nc.scalar.copy(out=held, in_=sums[LAST])
-        quantized = quantize(da_1, "da_1")
-        scatter(r_tok[LAST], r_slots[0], held)
-        banks = [bank(index, "r_bank") for index in (0, 1, 2, 5)]
-        for b in range(BLOCKS):
-            product_a(banks[b][:, :HALF], 1, b, quantized)
-        for b in range(LAST - 1):
-            scatter(r_tok[b], r_slots[1], copy_out(banks[b][:, :HALF], "r1_%d" % b))
-
-        da_2 = woven_piece(pairs, da_rows, r_slots[2], "da_2")
-        held = pairs[:, : 2 * HALF].bitcast(F32)
-        nc.scalar.copy(out=held, in_=banks[LAST - 1][:, :HALF])
-        quantized = quantize(da_2, "da_2")
-        scatter(r_tok[LAST - 1], r_slots[1], held)
-        alone, middle = bank(3, "r_bank"), bank(4, "r_bank")
-        sums = [alone[:, :HALF], middle[:, :HALF], middle[:, HALF:], banks[LAST][:, HALF:]]
-        for b in range(BLOCKS):
-            product_a(sums[b], 2, b, quantized)
-        staged = copy_three(sums, middle[:], "r2")
+        sums = bank(7, "q3_bank")
+        product_b(sums[:, :HALF], 2, 3, dc_q[2])
+        staged = sbuf([P, HALF], F32, "q3_staged", "da_0")
+        nc.scalar.copy(out=staged[:], in_=sums[:, :HALF])
+        scalar_scatter(q_tok[3], slots_of(list_b, 2 * C2, T), staged[:])
 
         def store_rows(queue, b, cols, total):
             queue.dma_start(out=out[b * P : (b + 1) * P, cols], in_=total[:, cols])
 
-        for b in range(LAST):
-            scatter(r_tok[b], r_slots[2], staged[b])
+        for b in range(3):
             total = sbuf([P, T], F32, "total%d" % b)
             nc.gpsimd.tensor_tensor(out=total[:], in0=r_tok[b][:], in1=q_tok[b][:], op=ALU.add)
             store_rows(nc.sync, b, slice(0, T), total)
-        scatter(r_tok[LAST], slots_of(list_a, HALF, BANK), copy_out(banks[LAST][:], "r12_last"))
-        total = sbuf([P, T], F32, "total%d" % LAST)
-        for queue, cols in ((nc.sync, slice(0, HALF)), (nc.scalar, slice(HALF, BANK)), (nc.sync, slice(BANK, T))):
-            nc.vector.tensor_tensor(out=total[:, cols], in0=r_tok[LAST][:, cols], in1=q_tok[LAST][:, cols], op=ALU.add)
-            store_rows(queue, LAST, cols, total)
+        total = sbuf([P, T], F32, "total3")
+        for queue, t in ((nc.sync, 0), (nc.scalar, 1), (nc.sync, 2)):
+            nc.vector.tensor_tensor(out=total[:, part(t)], in0=r_tok[3][:, part(t)], in1=q_tok[3][:, part(t)], op=ALU.add)
+            store_rows(queue, 3, part(t), total)

@@ -140,14 +140,22 @@ def tile_moe_plb_relu_kernel(
         long, short = slice(0, BANK), slice(BANK, T)
         early_banks = [bank(n, "dh_bank") for n in range(PARTS)]
         dc_rows = [sbuf([P, T], BF16, "dc_row%d" % e) for e in range(2)]
+        masked_early = sbuf([P, 2, T], F32, "masked_early")
+
+        def early_part(e, tokens, sums):
+            gated(masked_early[:, e, tokens], a_early[:, e, tokens], sums, ALU.is_gt)
+            nc.gpsimd.tensor_tensor(
+                out=dc_rows[e][:, tokens], in0=masked_early[:, e, tokens], in1=a_early[:, e, tokens], op=ALU.mult
+            )
+
         dh_into(early_banks[0][:], 0, long)
-        gated(dc_rows[0][:, long], a_early[:, 0, long], early_banks[0][:], ALU.max)
+        early_part(0, long, early_banks[0][:])
         for e in range(2):
             dh_into(early_banks[1][:, part(e)], e, short)
         for e in range(2):
-            gated(dc_rows[e][:, short], a_early[:, e, short], early_banks[1][:, part(e)], ALU.max)
+            early_part(e, short, early_banks[1][:, part(e)])
         dh_into(early_banks[2][:], 1, long)
-        gated(dc_rows[1][:, long], a_early[:, 1, long], early_banks[2][:], ALU.max)
+        early_part(1, long, early_banks[2][:])
 
         late_banks = [bank(PARTS + t, "dh_bank") for t in range(PARTS)]
         dc_late = sbuf([P, 2 * T], BF16, "dc_late")
@@ -173,9 +181,9 @@ def tile_moe_plb_relu_kernel(
                 dst = dc_picked[f][:, :HALF].bitcast(BF16).rearrange("p (n e) -> p n e", e=2)[:, :, e]
                 nc.scalar.activation(dst, dc_rows[e][:].indirect(slots_of(list_b, f * C2, (f + 1) * C2)), COPY)
 
-        def quantized_piece(picked, name):
-            woven = sbuf([P, HALF * PACK], BF16, name)
-            nc.vector.tensor_copy(
+        def quantized_piece(picked, name, weaver=nc.vector, tag=None):
+            woven = sbuf([P, HALF * PACK], BF16, name, tag)
+            weaver.tensor_copy(
                 out=woven[:].bitcast(U32).rearrange("p (n h) -> p n h", h=2),
                 in_=picked[:].rearrange("p (h n) -> p n h", h=2),
             )
@@ -217,10 +225,10 @@ def tile_moe_plb_relu_kernel(
             nc.vector.tensor_copy(window[:].indirect(offsets), values)
 
         q_tok = [sbuf([P, T], F32, "q_tok%d" % b) for b in range(4)]
-        r_tok = [sbuf([P, WIDE if b == 3 else T], F32, "r_tok%d" % b) for b in range(4)]
+        r_tok = [sbuf([P, WIDE if b % 2 else T], F32, "r_tok%d" % b) for b in range(4)]
 
         dc_q = []
-        groups = [(f, b) for f in range(E2) for b in (0, 2, 3)][:-1]
+        groups = [(0, 0), (0, 2), (0, 3), (1, 0), (1, 2), (2, 0), (2, 2)]
         for n in range(0, len(groups), 2):
             sums = bank(6 + (n // 2) % 2, "q_bank")
             for place, (f, b) in enumerate(groups[n : n + 2]):
@@ -234,21 +242,17 @@ def tile_moe_plb_relu_kernel(
             for place, (f, b) in enumerate(groups[n : n + 2]):
                 scalar_scatter(q_tok[b], slots_of(list_b, f * C2, (f + 1) * C2), staged[:, part(place)])
 
-        masked = sbuf([P, 2, 2, T], F32, "masked", "dc_2")
-        da_pair = [sbuf([P, 2 * T], BF16, "da_pair%d" % h) for h in range(2)]
-        gated(masked[:, 0, 0, long], a_early[:, 0, long], early_banks[0][:], ALU.is_gt)
-        gated(masked[:, 0, 1, long], a_early[:, 1, long], early_banks[2][:], ALU.is_gt)
-        gated(masked[:, 0, :, short], a_early[:, :, short], two_rows(early_banks[1][:]), ALU.is_gt)
+        masked = [masked_early, sbuf([P, 2, T], F32, "masked_late", "dc_1")]
+        da_pair = [sbuf([P, 2 * T], BF16, "da_early", "dc_2"), sbuf([P, 2 * T], BF16, "da_late")]
         for t in range(PARTS):
-            gated(masked[:, 1, :, part(t)], a_late[t], two_rows(late_banks[t][:]), ALU.is_gt)
+            gated(masked[1][:, :, part(t)], a_late[t], two_rows(late_banks[t][:]), ALU.is_gt)
         for h in range(2):
-            for t in range(PARTS):
-                nc.gpsimd.tensor_tensor(
-                    out=da_pair[h][:, t * BANK : (t + 1) * BANK].rearrange("p (g i e) -> p g e i", i=4, e=2),
-                    in0=masked[:, h, :, part(t)].rearrange("p e (g i) -> p g e i", i=4),
-                    in1=c_pair[h][:, :, part(t)].rearrange("p e (g i) -> p g e i", i=4),
-                    op=ALU.mult,
-                )
+            nc.gpsimd.tensor_tensor(
+                out=da_pair[h][:].rearrange("p (g i e) -> p g e i", i=4, e=2),
+                in0=masked[h][:].rearrange("p e (g i) -> p g e i", i=4),
+                in1=c_pair[h][:].rearrange("p e (g i) -> p g e i", i=4),
+                op=ALU.mult,
+            )
 
         q1_staged = sbuf([P, T], F32, "q1_staged")
         sums = bank(0, "q1_bank")
@@ -264,29 +268,32 @@ def tile_moe_plb_relu_kernel(
         r_scalar = sbuf([P, 2, T], F32, "r_scalar")
         r_vector = sbuf([P, 2, T], F32, "r_vector")
         for g in range(PARTS):
-            picked = sbuf([P, 2 * HALF], U32, "da_picked%d" % g)
+            picked = sbuf([P, 2 * HALF], U32, "da_picked%d" % g, "da_picked%d" % (g % 2))
             for h in range(2):
                 gather_pairs(picked[:, part(h)], da_pair[h], slots_of(list_a, g * HALF, (g + 1) * HALF))
-            quantized = quantized_piece(picked, "da_%d" % g)
+            quantized = quantized_piece(picked, "da_%d" % g, nc.vector if g == PARTS - 1 else nc.gpsimd, "da_%d" % (g - g % 2))
             for_scalar, for_vector = bank(5 + g, "r_bank"), bank(2 + g, "r_bank")
             for place in range(2):
                 product_a(for_scalar[:, part(place)], g, 2 * place, quantized)
             for place in range(2):
                 product_a(for_vector[:, part(place)], g, 2 * place + 1, quantized)
-            empty = nc.vector.tensor_copy if g == 0 else nc.scalar.copy
-            empty(out=r_scalar[:, :, part(g)], in_=two_rows(for_scalar[:]))
+            nc.scalar.copy(out=r_scalar[:, :, part(g)], in_=two_rows(for_scalar[:]))
             nc.vector.tensor_copy(out=r_vector[:, :, part(g)], in_=two_rows(for_vector[:]))
             scalar_scatter(r_tok[0], slots_of(list_a, g * HALF, (g + 1) * HALF), r_scalar[:, 0, part(g)])
-        for first, stop in ((T // 2, T), (0, T // 2)):
-            scalar_scatter(r_tok[2], slots_of(list_a, first, stop), r_scalar[:, 1, first:stop])
-        for first, stop in ((0, HALF), (HALF, T)):
-            vector_scatter(r_tok[1], slots_of(list_a, first, stop), r_vector[:, 0, first:stop])
-        vector_scatter(r_tok[3], list_a[:], r_vector[:, 1, :])
+        sums = bank(2, "q3_bank")
+        product_b(sums[:, :HALF], 1, 3, dc_q[1])
+        staged = sbuf([P, HALF], F32, "q3_middle")
+        nc.vector.tensor_copy(out=staged[:], in_=sums[:, :HALF])
+        vector_scatter(q_tok[3], slots_of(list_b, C2, 2 * C2), staged[:])
+        for place in range(2):
+            vector_scatter(r_tok[2 * place + 1], list_a[:], r_vector[:, place, :])
 
+        scalar_scatter(r_tok[2], slots_of(list_a, T // 2, T), r_scalar[:, 1, T // 2 :])
         sums = bank(7, "q3_bank")
         product_b(sums[:, :HALF], 2, 3, dc_q[2])
-        staged = sbuf([P, HALF], F32, "q3_staged", "da_0")
+        staged = sbuf([P, HALF], F32, "q3_staged")
         nc.scalar.copy(out=staged[:], in_=sums[:, :HALF])
+        scalar_scatter(r_tok[2], slots_of(list_a, 0, T // 2), r_scalar[:, 1, : T // 2])
         scalar_scatter(q_tok[3], slots_of(list_b, 2 * C2, T), staged[:])
 
         def store_rows(queue, b, cols, total):
@@ -294,7 +301,7 @@ def tile_moe_plb_relu_kernel(
 
         for b in range(3):
             total = sbuf([P, T], F32, "total%d" % b)
-            nc.gpsimd.tensor_tensor(out=total[:], in0=r_tok[b][:], in1=q_tok[b][:], op=ALU.add)
+            nc.gpsimd.tensor_tensor(out=total[:], in0=r_tok[b][:, :T], in1=q_tok[b][:], op=ALU.add)
             store_rows(nc.sync, b, slice(0, T), total)
         total = sbuf([P, T], F32, "total3")
         for queue, t in ((nc.sync, 0), (nc.scalar, 1), (nc.sync, 2)):

@@ -28,6 +28,7 @@ QUADRANT = 32
 SCALE_ROWS = 4
 LINE = 16
 WIDE = 1024
+SHARE = 32
 
 
 def tile_moe_plb_relu_kernel(
@@ -148,14 +149,11 @@ def tile_moe_plb_relu_kernel(
                 out=dc_rows[e][:, tokens], in0=masked_early[:, e, tokens], in1=a_early[:, e, tokens], op=ALU.mult
             )
 
-        dh_into(early_banks[0][:], 0, long)
-        early_part(0, long, early_banks[0][:])
         for e in range(2):
             dh_into(early_banks[1][:, part(e)], e, short)
-        for e in range(2):
             early_part(e, short, early_banks[1][:, part(e)])
-        dh_into(early_banks[2][:], 1, long)
-        early_part(1, long, early_banks[2][:])
+            dh_into(early_banks[2 * e][:], e, long)
+            early_part(e, long, early_banks[2 * e][:])
 
         late_banks = [bank(PARTS + t, "dh_bank") for t in range(PARTS)]
         dc_late = sbuf([P, 2 * T], BF16, "dc_late")
@@ -224,26 +222,26 @@ def tile_moe_plb_relu_kernel(
         def vector_scatter(window, offsets, values):
             nc.vector.tensor_copy(window[:].indirect(offsets), values)
 
-        q_tok = [sbuf([P, T], F32, "q_tok%d" % b) for b in range(4)]
+        q_tok = [sbuf([P, WIDE if b == 1 else T], F32, "q_tok%d" % b) for b in range(4)]
         r_tok = [sbuf([P, WIDE if b % 2 else T], F32, "r_tok%d" % b) for b in range(4)]
 
         dc_q = []
-        groups = [(0, 0), (0, 2), (0, 3), (1, 0), (1, 2), (2, 0), (2, 2)]
-        for n in range(0, len(groups), 2):
-            sums = bank(6 + (n // 2) % 2, "q_bank")
-            for place, (f, b) in enumerate(groups[n : n + 2]):
+        groups = [[(0, 0)], [(0, 2), (0, 3)], [(1, 0), (1, 2)], [(2, 0), (2, 2)]]
+        for n, group in enumerate(groups):
+            sums = bank(6 + n % 2, "q_bank")
+            for place, (f, b) in enumerate(group):
                 if f == len(dc_q):
                     gather_pairs(dc_picked[f][:, HALF:], dc_late, slots_of(list_b, f * C2, (f + 1) * C2))
-                    dc_q.append(quantized_piece(dc_picked[f], "dc_%d" % f))
+                    dc_q.append(quantized_piece(dc_picked[f], "dc_%d" % f, tag=("dc_0", "dc_picked0", "dc_0")[f]))
                 product_b(sums[:, part(place)], f, b, dc_q[f])
-            width = HALF * len(groups[n : n + 2])
+            width = HALF * len(group)
             staged = sbuf([P, width], F32, "q_staged%d" % n)
             nc.scalar.copy(out=staged[:], in_=sums[:, :width])
-            for place, (f, b) in enumerate(groups[n : n + 2]):
+            for place, (f, b) in enumerate(group):
                 scalar_scatter(q_tok[b], slots_of(list_b, f * C2, (f + 1) * C2), staged[:, part(place)])
 
-        masked = [masked_early, sbuf([P, 2, T], F32, "masked_late", "dc_1")]
-        da_pair = [sbuf([P, 2 * T], BF16, "da_early", "dc_2"), sbuf([P, 2 * T], BF16, "da_late")]
+        masked = [masked_early, sbuf([P, 2, T], F32, "masked_late", "dc_picked0")]
+        da_pair = [sbuf([P, 2 * T], BF16, "da_early", "dc_0"), sbuf([P, 2 * T], BF16, "da_late")]
         for t in range(PARTS):
             gated(masked[1][:, :, part(t)], a_late[t], two_rows(late_banks[t][:]), ALU.is_gt)
         for h in range(2):
@@ -262,8 +260,7 @@ def tile_moe_plb_relu_kernel(
         sums = bank(1, "q1_bank")
         product_b(sums[:, :HALF], 2, 1, dc_q[2])
         nc.vector.tensor_copy(out=q1_staged[:, BANK:], in_=sums[:, :HALF])
-        vector_scatter(q_tok[1], slots_of(list_b, 0, BANK), q1_staged[:, :BANK])
-        vector_scatter(q_tok[1], slots_of(list_b, BANK, T), q1_staged[:, BANK:])
+        vector_scatter(q_tok[1], list_b[:], q1_staged[:])
 
         r_scalar = sbuf([P, 2, T], F32, "r_scalar")
         r_vector = sbuf([P, 2, T], F32, "r_vector")
@@ -282,27 +279,27 @@ def tile_moe_plb_relu_kernel(
             scalar_scatter(r_tok[0], slots_of(list_a, g * HALF, (g + 1) * HALF), r_scalar[:, 0, part(g)])
         sums = bank(2, "q3_bank")
         product_b(sums[:, :HALF], 1, 3, dc_q[1])
-        staged = sbuf([P, HALF], F32, "q3_middle")
-        nc.vector.tensor_copy(out=staged[:], in_=sums[:, :HALF])
-        vector_scatter(q_tok[3], slots_of(list_b, C2, 2 * C2), staged[:])
+        q3_staged = sbuf([P, BANK], F32, "q3_staged")
+        nc.vector.tensor_copy(out=q3_staged[:, :HALF], in_=sums[:, :HALF])
+        vector_scatter(q_tok[3], slots_of(list_b, C2, 2 * C2 - SHARE), q3_staged[:, : HALF - SHARE])
         for place in range(2):
             vector_scatter(r_tok[2 * place + 1], list_a[:], r_vector[:, place, :])
 
         scalar_scatter(r_tok[2], slots_of(list_a, T // 2, T), r_scalar[:, 1, T // 2 :])
         sums = bank(7, "q3_bank")
         product_b(sums[:, :HALF], 2, 3, dc_q[2])
-        staged = sbuf([P, HALF], F32, "q3_staged")
-        nc.scalar.copy(out=staged[:], in_=sums[:, :HALF])
+        nc.scalar.copy(out=q3_staged[:, HALF:], in_=sums[:, :HALF])
         scalar_scatter(r_tok[2], slots_of(list_a, 0, T // 2), r_scalar[:, 1, : T // 2])
-        scalar_scatter(q_tok[3], slots_of(list_b, 2 * C2, T), staged[:])
+        scalar_scatter(q_tok[3], slots_of(list_b, 2 * C2 - SHARE, T), q3_staged[:, HALF - SHARE :])
 
         def store_rows(queue, b, cols, total):
             queue.dma_start(out=out[b * P : (b + 1) * P, cols], in_=total[:, cols])
 
         for b in range(3):
             total = sbuf([P, T], F32, "total%d" % b)
-            nc.gpsimd.tensor_tensor(out=total[:], in0=r_tok[b][:, :T], in1=q_tok[b][:], op=ALU.add)
-            store_rows(nc.sync, b, slice(0, T), total)
+            for cols in (slice(0, T // 2), slice(T // 2, T)) if b == 2 else (slice(0, T),):
+                nc.gpsimd.tensor_tensor(out=total[:, cols], in0=r_tok[b][:, cols], in1=q_tok[b][:, cols], op=ALU.add)
+                store_rows(nc.sync, b, cols, total)
         total = sbuf([P, T], F32, "total3")
         for queue, t in ((nc.sync, 0), (nc.scalar, 1), (nc.sync, 2)):
             nc.vector.tensor_tensor(out=total[:, part(t)], in0=r_tok[3][:, part(t)], in1=q_tok[3][:, part(t)], op=ALU.add)

@@ -28,7 +28,7 @@ QUADRANT = 32
 SCALE_ROWS = 4
 LINE = 16
 WIDE = 1024
-SHARE = 32
+SHARE = 128
 
 
 def tile_moe_plb_relu_kernel(
@@ -282,6 +282,7 @@ def tile_moe_plb_relu_kernel(
         q3_staged = sbuf([P, BANK], F32, "q3_staged")
         nc.vector.tensor_copy(out=q3_staged[:, :HALF], in_=sums[:, :HALF])
         vector_scatter(q_tok[3], slots_of(list_b, C2, 2 * C2 - SHARE), q3_staged[:, : HALF - SHARE])
+        vector_scatter(r_tok[2], slots_of(list_a, 0, SHARE), r_scalar[:, 1, :SHARE])
         for place in range(2):
             vector_scatter(r_tok[2 * place + 1], list_a[:], r_vector[:, place, :])
 
@@ -289,7 +290,7 @@ def tile_moe_plb_relu_kernel(
         sums = bank(7, "q3_bank")
         product_b(sums[:, :HALF], 2, 3, dc_q[2])
         nc.scalar.copy(out=q3_staged[:, HALF:], in_=sums[:, :HALF])
-        scalar_scatter(r_tok[2], slots_of(list_a, 0, T // 2), r_scalar[:, 1, : T // 2])
+        scalar_scatter(r_tok[2], slots_of(list_a, SHARE, T // 2), r_scalar[:, 1, SHARE : T // 2])
         scalar_scatter(q_tok[3], slots_of(list_b, 2 * C2 - SHARE, T), q3_staged[:, HALF - SHARE :])
 
         def store_rows(queue, b, cols, total):

@@ -81,9 +81,10 @@ def tile_moe_plb_relu_kernel(
             a_late.extend(piece[:, :, part(t)] for t in range(count))
 
         list_b = sbuf([P, T // STRIPE], U16, "list_b")
-        nc.sync.dma_start(out=a_early[:, 0, :], in_=a_view[0][:, 0, :])
-        nc.sync.dma_start(list_b[:], offs2)
+        for tokens in (slice(BANK, T), slice(0, BANK)):
+            nc.sync.dma_start(out=a_early[:, 0, tokens], in_=a_view[0][:, 0, tokens])
         nc.sync.dma_start(out=a_early[:, 1, :], in_=a_view[0][:, 1, :])
+        nc.sync.dma_start(list_b[:], offs2)
         load_late(0, 2)
         load_late(2, 1)
         wb_codes = sbuf([P, E2, 2 * K], U8, "wb_codes")
@@ -268,7 +269,7 @@ def tile_moe_plb_relu_kernel(
             picked = sbuf([P, 2 * HALF], U32, "da_picked%d" % g, "da_picked%d" % (g % 2))
             for h in range(2):
                 gather_pairs(picked[:, part(h)], da_pair[h], slots_of(list_a, g * HALF, (g + 1) * HALF))
-            quantized = quantized_piece(picked, "da_%d" % g, nc.vector if g == PARTS - 1 else nc.gpsimd, "da_%d" % (g - g % 2))
+            quantized = quantized_piece(picked, "da_%d" % g, nc.vector)
             for_scalar, for_vector = bank(5 + g, "r_bank"), bank(2 + g, "r_bank")
             for place in range(2):
                 product_a(for_scalar[:, part(place)], g, 2 * place, quantized)
@@ -298,9 +299,8 @@ def tile_moe_plb_relu_kernel(
 
         for b in range(3):
             total = sbuf([P, T], F32, "total%d" % b)
-            for cols in (slice(0, T // 2), slice(T // 2, T)) if b == 2 else (slice(0, T),):
-                nc.gpsimd.tensor_tensor(out=total[:, cols], in0=r_tok[b][:, cols], in1=q_tok[b][:, cols], op=ALU.add)
-                store_rows(nc.sync, b, cols, total)
+            nc.gpsimd.tensor_tensor(out=total[:], in0=r_tok[b][:, :T], in1=q_tok[b][:, :T], op=ALU.add)
+            store_rows(nc.sync, b, slice(0, T), total)
         total = sbuf([P, T], F32, "total3")
         for queue, t in ((nc.sync, 0), (nc.scalar, 1), (nc.sync, 2)):
             nc.vector.tensor_tensor(out=total[:, part(t)], in0=r_tok[3][:, part(t)], in1=q_tok[3][:, part(t)], op=ALU.add)

@@ -28,7 +28,9 @@ QUADRANT = 32
 SCALE_ROWS = 4
 LINE = 16
 WIDE = 1024
-SHARE = 128
+FIRST = 128
+SIDE = T // 2
+HELD = 320
 
 
 def tile_moe_plb_relu_kernel(
@@ -37,10 +39,14 @@ def tile_moe_plb_relu_kernel(
     nc = tc.nc
     with ExitStack() as ctx:
         keep = ctx.enter_context(tc.tile_pool(name="keep", bufs=1))
+        placed = ctx.enter_context(tc.tile_pool(name="placed", bufs=1))
         psum = ctx.enter_context(tc.psum_pool(name="psum", bufs=1))
 
         def sbuf(shape, dtype, name, tag=None):
             return keep.tile(shape, dtype, name=name, tag=tag or name, align_bytes=64)
+
+        def at(offset, shape, dtype, name):
+            return placed.tile(shape, dtype, name=name, tag=name, align_bytes=64, offset=offset)
 
         def bank(index, name):
             return psum.tile([P, BANK], F32, name=name, tag="bank%d" % index)
@@ -56,12 +62,19 @@ def tile_moe_plb_relu_kernel(
         def part(t):
             return slice(t * HALF, (t + 1) * HALF)
 
+        long, short = slice(0, BANK), slice(BANK, T)
+
         w2_scale_raw = sbuf([P, PASSES, H], U8, "w2_scale_raw")
         dy_scale = sbuf([P, PASSES, T], U8, "dy_scale")
         wb_scale = sbuf([P, E2, K], U8, "wb_scale")
         wa_scale = sbuf([P, E1, K], U8, "wa_scale")
         for plane in (w2_scale_raw, dy_scale, wb_scale, wa_scale):
             nc.vector.memset(plane[:].bitcast(I32), 0)
+        dc_rows = [sbuf([P, WIDE], BF16, "dc_row%d" % e) for e in range(2)]
+        dc_late = sbuf([P, 2 * WIDE], BF16, "dc_late")
+        for row in dc_rows:
+            nc.vector.memset(row[:, T:], 0.0)
+        nc.vector.memset(dc_late[:, 2 * T :], 0.0)
 
         w2_raw = sbuf([P, PASSES, H], I32, "w2_raw")
         nc.sync.dma_start(out=w2_raw[:], in_=w2t_words.rearrange("s p i d -> p s (i d)").bitcast(I32))
@@ -73,26 +86,20 @@ def tile_moe_plb_relu_kernel(
         a_view = a.rearrange("(p h e) t -> h p e t", h=2, e=2)
         c_view = c.rearrange("(p h e) t -> h p e t", h=2, e=2)
         a_early = sbuf([P, 2, T], F32, "a_early")
-        a_late = []
-
-        def load_late(first, count):
-            piece = sbuf([P, 2, count * HALF], F32, "a_late%d" % first)
-            nc.sync.dma_start(out=piece[:], in_=a_view[1][:, :, first * HALF : (first + count) * HALF])
-            a_late.extend(piece[:, :, part(t)] for t in range(count))
-
+        nc.sync.dma_start(out=a_early[:, :, short], in_=a_view[0][:, :, short])
         list_b = sbuf([P, T // STRIPE], U16, "list_b")
-        for tokens in (slice(BANK, T), slice(0, BANK)):
-            nc.sync.dma_start(out=a_early[:, 0, tokens], in_=a_view[0][:, 0, tokens])
-        nc.sync.dma_start(out=a_early[:, 1, :], in_=a_view[0][:, 1, :])
         nc.sync.dma_start(list_b[:], offs2)
-        load_late(0, 2)
-        load_late(2, 1)
+        nc.sync.dma_start(out=a_early[:, :, long], in_=a_view[0][:, :, long])
+        a_late = [sbuf([P, 2, HALF], F32, "a_late%d" % t) for t in range(PARTS)]
+        for t in range(PARTS):
+            nc.sync.dma_start(out=a_late[t][:], in_=a_view[1][:, :, part(t)])
         wb_codes = sbuf([P, E2, 2 * K], U8, "wb_codes")
         nc.sync.dma_start(out=wb_codes[:].bitcast(I32), in_=wbt_words.rearrange("f s p w -> p (f s) w").bitcast(I32))
         load_scale_rows(wb_scale, wbt_scales.rearrange("f s b k -> (f s) b k"))
-        c_pair = [sbuf([P, 2, T], F32, "c_pair%d" % h) for h in range(2)]
-        for h in range(2):
-            nc.sync.dma_start(out=c_pair[h][:], in_=c_view[h])
+        c_early = sbuf([P, 2, T], F32, "c_early")
+        nc.sync.dma_start(out=c_early[:], in_=c_view[0])
+        c_late = sbuf([P, 2, T], F32, "c_late")
+        nc.sync.dma_start(out=c_late[:], in_=c_view[1])
         list_a = sbuf([P, T // STRIPE], U16, "list_a")
         nc.sync.dma_start(list_a[:], offs)
         wa_codes = sbuf([P, E1, K], I32, "wa_codes")
@@ -139,31 +146,30 @@ def tile_moe_plb_relu_kernel(
         def gated(dst, saved, sums, test):
             nc.vector.scalar_tensor_tensor(out=dst, in0=saved, scalar=0.0, in1=sums, op0=test, op1=ALU.mult)
 
-        long, short = slice(0, BANK), slice(BANK, T)
-        early_banks = [bank(n, "dh_bank") for n in range(PARTS)]
-        dc_rows = [sbuf([P, T], BF16, "dc_row%d" % e) for e in range(2)]
         masked_early = sbuf([P, 2, T], F32, "masked_early")
 
-        def early_part(e, tokens, sums):
+        def by_mask(e, tokens, sums):
             gated(masked_early[:, e, tokens], a_early[:, e, tokens], sums, ALU.is_gt)
             nc.gpsimd.tensor_tensor(
                 out=dc_rows[e][:, tokens], in0=masked_early[:, e, tokens], in1=a_early[:, e, tokens], op=ALU.mult
             )
 
-        for e in range(2):
-            dh_into(early_banks[1][:, part(e)], e, short)
-            early_part(e, short, early_banks[1][:, part(e)])
-            dh_into(early_banks[2 * e][:], e, long)
-            early_part(e, long, early_banks[2 * e][:])
+        early_banks = [bank(n, "dh_bank") for n in range(PARTS)]
+        for e, sums in enumerate((early_banks[1], bank(7, "dh_bank"))):
+            dh_into(sums[:, :HALF], e, short)
+            by_mask(e, short, sums[:, :HALF])
+        dh_into(early_banks[0][:], 0, long)
+        gated(dc_rows[0][:, long], a_early[:, 0, long], early_banks[0][:], ALU.max)
+        dh_into(early_banks[2][:], 1, long)
+        by_mask(1, long, early_banks[2][:])
 
         late_banks = [bank(PARTS + t, "dh_bank") for t in range(PARTS)]
-        dc_late = sbuf([P, 2 * T], BF16, "dc_late")
         for t in range(PARTS):
             for e in range(2):
                 dh_into(late_banks[t][:, part(e)], 2 + e, part(t))
             gated(
                 dc_late[:, t * BANK : (t + 1) * BANK].rearrange("p (t e) -> p t e", e=2),
-                a_late[t].rearrange("p e t -> p t e"),
+                a_late[t][:].rearrange("p e t -> p t e"),
                 late_banks[t][:].rearrange("p (e t) -> p t e", e=2),
                 ALU.max,
             )
@@ -171,134 +177,189 @@ def tile_moe_plb_relu_kernel(
         def slots_of(slot_list, first, stop):
             return slot_list[:, first // STRIPE : stop // STRIPE]
 
-        def gather_pairs(dst, pairs, slots):
-            nc.vector.tensor_copy(dst, pairs[:].bitcast(U32).indirect(slots))
+        def gather_pairs(dst, window, slots):
+            nc.vector.tensor_copy(dst, window.bitcast(U32).indirect(slots))
 
-        dc_picked = [sbuf([P, 2 * HALF], U32, "dc_picked%d" % f) for f in range(E2)]
-        for e in range(2):
-            for f in range(E2):
-                dst = dc_picked[f][:, :HALF].bitcast(BF16).rearrange("p (n e) -> p n e", e=2)[:, :, e]
-                nc.scalar.activation(dst, dc_rows[e][:].indirect(slots_of(list_b, f * C2, (f + 1) * C2)), COPY)
+        def gather_row(dst, step, e, slots):
+            nc.scalar.activation(dst.rearrange("p (n e) -> p n e", e=step)[:, :, e], dc_rows[e][:].indirect(slots), COPY)
 
-        def quantized_piece(picked, name, weaver=nc.vector, tag=None):
-            woven = sbuf([P, HALF * PACK], BF16, name, tag)
-            weaver.tensor_copy(
-                out=woven[:].bitcast(U32).rearrange("p (n h) -> p n h", h=2),
-                in_=picked[:].rearrange("p (h n) -> p n h", h=2),
-            )
-            codes = sbuf([P, HALF], U32, name + "_codes")
-            scale = sbuf([P, HALF], U8, name + "_scale")
-            nc.vector.quantize_mx(out=codes[:].bitcast(FP8X4), scales=scale[:], in_=woven[:])
-            return codes, scale
+        def weave(engine, woven, planes):
+            engine.tensor_copy(out=woven.bitcast(U32).rearrange("p (n h) -> p n h", h=2), in_=planes)
 
-        def product_b(dst, f, b, quantized):
-            codes, scale = quantized
+        def quantize(name, values, first, stop, tag=None):
+            codes = sbuf([P, stop - first], U32, name + "_codes", tag)
+            scale = sbuf([P, stop - first], U8, name + "_scale")
+            nc.vector.quantize_mx(out=codes[:].bitcast(FP8X4), scales=scale[:], in_=values)
+            return first, codes, scale
+
+        def product(dst, weights, fmt, scale_rows, e, b, quantized, first, stop):
+            base, codes, scale = quantized
+            width = weights.shape[2] // PACK
             nc.tensor.matmul_mx(
                 out=dst,
-                lhsT=wb_codes[:, f, 2 * b * P : 2 * (b + 1) * P].bitcast(FP4X4),
-                lhsT_scale=wb_scale[:, f, b * P : (b + 1) * P],
-                rhs=codes[:].bitcast(FP8X4),
-                rhs_scale=scale[:],
+                lhsT=weights[:, e, b * width : (b + 1) * width].bitcast(fmt),
+                lhsT_scale=scale_rows[:, e, b * P : (b + 1) * P],
+                rhs=codes[:, first - base : stop - base].bitcast(FP8X4),
+                rhs_scale=scale[:, first - base : stop - base],
                 start=True,
                 stop=True,
             )
 
-        def product_a(dst, g, b, quantized):
-            codes, scale = quantized
-            for u in range(HALF // C1):
-                e, cols = g * (HALF // C1) + u, slice(u * C1, (u + 1) * C1)
-                nc.tensor.matmul_mx(
-                    out=dst[:, cols],
-                    lhsT=wa_codes[:, e, b * P : (b + 1) * P].bitcast(FP8X4),
-                    lhsT_scale=wa_scale[:, e, b * P : (b + 1) * P],
-                    rhs=codes[:, cols].bitcast(FP8X4),
-                    rhs_scale=scale[:, cols],
-                    start=True,
-                    stop=True,
-                )
+        def products_b(dst, b, quantized, first, stop):
+            for lo in range(first - first % C2, stop, C2):
+                lo, hi = max(lo, first), min(lo + C2, stop)
+                product(dst[:, lo - first : hi - first], wb_codes, FP4X4, wb_scale, lo // C2, b, quantized, lo, hi)
 
-        def scalar_scatter(window, offsets, values):
-            nc.scalar.activation(window[:].indirect(offsets), values, COPY)
+        def products_a(dst, b, quantized, first, stop):
+            for lo in range(first, stop, C1):
+                product(dst[:, lo - first : lo - first + C1], wa_codes, FP8X4, wa_scale, lo // C1, b, quantized, lo, lo + C1)
 
-        def vector_scatter(window, offsets, values):
-            nc.vector.tensor_copy(window[:].indirect(offsets), values)
+        def scalar_scatter(window, slot_list, first, stop, values):
+            nc.scalar.activation(window[:].indirect(slots_of(slot_list, first, stop)), values, COPY)
 
-        q_tok = [sbuf([P, WIDE if b == 1 else T], F32, "q_tok%d" % b) for b in range(4)]
-        r_tok = [sbuf([P, WIDE if b % 2 else T], F32, "r_tok%d" % b) for b in range(4)]
+        def vector_scatter(window, slot_list, first, stop, values):
+            nc.vector.tensor_copy(window[:].indirect(slots_of(slot_list, first, stop)), values)
 
-        dc_q = []
-        groups = [[(0, 0)], [(0, 2), (0, 3)], [(1, 0), (1, 2)], [(2, 0), (2, 2)]]
-        for n, group in enumerate(groups):
-            sums = bank(6 + n % 2, "q_bank")
-            for place, (f, b) in enumerate(group):
-                if f == len(dc_q):
-                    gather_pairs(dc_picked[f][:, HALF:], dc_late, slots_of(list_b, f * C2, (f + 1) * C2))
-                    dc_q.append(quantized_piece(dc_picked[f], "dc_%d" % f, tag=("dc_0", "dc_picked0", "dc_0")[f]))
-                product_b(sums[:, part(place)], f, b, dc_q[f])
-            width = HALF * len(group)
-            staged = sbuf([P, width], F32, "q_staged%d" % n)
-            nc.scalar.copy(out=staged[:], in_=sums[:, :width])
-            for place, (f, b) in enumerate(group):
-                scalar_scatter(q_tok[b], slots_of(list_b, f * C2, (f + 1) * C2), staged[:, part(place)])
+        q_tok = [sbuf([P, T], F32, "q_tok%d" % b) for b in range(4)]
 
-        masked = [masked_early, sbuf([P, 2, T], F32, "masked_late", "dc_picked0")]
-        da_pair = [sbuf([P, 2 * T], BF16, "da_early", "dc_0"), sbuf([P, 2 * T], BF16, "da_late")]
-        for t in range(PARTS):
-            gated(masked[1][:, :, part(t)], a_late[t], two_rows(late_banks[t][:]), ALU.is_gt)
-        for h in range(2):
+        REST = T - FIRST
+        head, rest = slots_of(list_b, 0, FIRST), slots_of(list_b, FIRST, T)
+        picked_rest = sbuf([P, 2 * REST], U32, "picked_rest")
+        woven_head = picked_rest[:, REST : REST + 2 * FIRST]
+        for e in range(2):
+            gather_row(woven_head.bitcast(BF16), PACK, e, head)
+            gather_row(picked_rest[:, :REST].bitcast(BF16), 2, e, rest)
+        gather_pairs(woven_head.rearrange("p (n h) -> p n h", h=2)[:, :, 1], dc_late[:], head)
+        for t in range(2):
+            gated(masked_early[:, 0, part(t)], a_early[:, 0, part(t)], early_banks[0][:, part(t)], ALU.is_gt)
+        masked_late = sbuf([P, 2, T], F32, "masked_late")
+        for e in range(2):
+            gated(masked_late[:, e, part(0)], a_late[0][:, e, :], late_banks[0][:, part(e)], ALU.is_gt)
+        dc_head = quantize("dc_head", woven_head.bitcast(BF16), 0, FIRST)
+        staged = []
+        for index, blocks in ((1, (1, 3)), (7, (0, 2))):
+            sums = bank(index, "q_bank")
+            for place, b in enumerate(blocks):
+                products_b(sums[:, place * FIRST : (place + 1) * FIRST], b, dc_head, 0, FIRST)
+            staged.append(sbuf([P, 2 * FIRST], F32, "q_staged_head%d" % index))
+            nc.scalar.copy(out=staged[-1][:], in_=sums[:, : 2 * FIRST])
+        for place, b in enumerate((1, 3, 0, 2)):
+            scalar_scatter(q_tok[b], list_b, 0, FIRST, staged[place // 2][:, place % 2 * FIRST : (place % 2 + 1) * FIRST])
+
+        def da_into(dst, masked, saved):
             nc.gpsimd.tensor_tensor(
-                out=da_pair[h][:].rearrange("p (g i e) -> p g e i", i=4, e=2),
-                in0=masked[h][:].rearrange("p e (g i) -> p g e i", i=4),
-                in1=c_pair[h][:].rearrange("p e (g i) -> p g e i", i=4),
+                out=dst.rearrange("p (g i e) -> p g e i", i=4, e=2),
+                in0=masked.rearrange("p e (g i) -> p g e i", i=4),
+                in1=saved.rearrange("p e (g i) -> p g e i", i=4),
                 op=ALU.mult,
             )
 
-        q1_staged = sbuf([P, T], F32, "q1_staged")
-        sums = bank(0, "q1_bank")
-        for f in range(2):
-            product_b(sums[:, part(f)], f, 1, dc_q[f])
-        nc.vector.tensor_copy(out=q1_staged[:, :BANK], in_=sums[:])
-        sums = bank(1, "q1_bank")
-        product_b(sums[:, :HALF], 2, 1, dc_q[2])
-        nc.vector.tensor_copy(out=q1_staged[:, BANK:], in_=sums[:, :HALF])
-        vector_scatter(q_tok[1], list_b[:], q1_staged[:])
+        MID = BANK - FIRST
+        gather_pairs(picked_rest[:, REST:], dc_late[:], rest)
+        planes = picked_rest[:].rearrange("p (h n) -> p n h", h=2)
+        gated(masked_late[:, :, part(1)], a_late[1][:], two_rows(late_banks[1][:]), ALU.is_gt)
+        woven_rest = at(0, [P, PACK * REST], BF16, "woven_rest")
+        weave(nc.vector, woven_rest[:, PACK * MID :], planes[:, MID:, :])
+        weave(nc.vector, woven_rest[:, : PACK * MID], planes[:, :MID, :])
+        dc_last = quantize("dc_last", woven_rest[:, PACK * MID :], BANK, T)
+        dc_mid = quantize("dc_mid", woven_rest[:, : PACK * MID], FIRST, BANK)
+        gated(masked_late[:, :, part(2)], a_late[2][:], two_rows(late_banks[2][:]), ALU.is_gt)
 
-        r_scalar = sbuf([P, 2, T], F32, "r_scalar")
-        r_vector = sbuf([P, 2, T], F32, "r_vector")
-        for g in range(PARTS):
-            picked = sbuf([P, 2 * HALF], U32, "da_picked%d" % g, "da_picked%d" % (g % 2))
-            for h in range(2):
-                gather_pairs(picked[:, part(h)], da_pair[h], slots_of(list_a, g * HALF, (g + 1) * HALF))
-            quantized = quantized_piece(picked, "da_%d" % g, nc.vector)
-            for_scalar, for_vector = bank(5 + g, "r_bank"), bank(2 + g, "r_bank")
-            for place in range(2):
-                product_a(for_scalar[:, part(place)], g, 2 * place, quantized)
-            for place in range(2):
-                product_a(for_vector[:, part(place)], g, 2 * place + 1, quantized)
-            nc.scalar.copy(out=r_scalar[:, :, part(g)], in_=two_rows(for_scalar[:]))
-            nc.vector.tensor_copy(out=r_vector[:, :, part(g)], in_=two_rows(for_vector[:]))
-            scalar_scatter(r_tok[0], slots_of(list_a, g * HALF, (g + 1) * HALF), r_scalar[:, 0, part(g)])
-        sums = bank(2, "q3_bank")
-        product_b(sums[:, :HALF], 1, 3, dc_q[1])
-        q3_staged = sbuf([P, BANK], F32, "q3_staged")
-        nc.vector.tensor_copy(out=q3_staged[:, :HALF], in_=sums[:, :HALF])
-        vector_scatter(q_tok[3], slots_of(list_b, C2, 2 * C2 - SHARE), q3_staged[:, : HALF - SHARE])
-        vector_scatter(r_tok[2], slots_of(list_a, 0, SHARE), r_scalar[:, 1, :SHARE])
-        for place in range(2):
-            vector_scatter(r_tok[2 * place + 1], list_a[:], r_vector[:, place, :])
+        da_early = at(0, [P, 2 * T], BF16, "da_early")
+        da_into(da_early[:], masked_early[:], c_early[:])
+        da_late = at(4 * T, [P, 2 * T], BF16, "da_late")
+        da_into(da_late[:], masked_late[:], c_late[:])
 
-        scalar_scatter(r_tok[2], slots_of(list_a, T // 2, T), r_scalar[:, 1, T // 2 :])
-        sums = bank(7, "q3_bank")
-        product_b(sums[:, :HALF], 2, 3, dc_q[2])
-        nc.scalar.copy(out=q3_staged[:, HALF:], in_=sums[:, :HALF])
-        scalar_scatter(r_tok[2], slots_of(list_a, SHARE, T // 2), r_scalar[:, 1, SHARE : T // 2])
-        scalar_scatter(q_tok[3], slots_of(list_b, 2 * C2 - SHARE, T), q3_staged[:, HALF - SHARE :])
+        def q_sums(index, b, first, stop):
+            sums = bank(index, "q_bank")
+            products_b(sums, b, dc_mid if first < BANK else dc_last, first, stop)
+            return sums
+
+        def staged(move, name, sums, width):
+            values = sbuf([P, width], F32, name)
+            move(out=values[:], in_=sums[:, :width])
+            return values
+
+        last0, last1, last2 = q_sums(2, 0, BANK, T), q_sums(6, 1, BANK, T), q_sums(1, 2, BANK, T - FIRST)
+        mid2, mid0, mid1 = q_sums(0, 2, FIRST, BANK), q_sums(3, 0, FIRST, BANK), q_sums(7, 1, FIRST, BANK)
+        last0_staged = staged(nc.scalar.copy, "last0_staged", last0, HALF)
+        last2_staged = staged(nc.scalar.copy, "last2_staged", last2, FIRST)
+        mid3, share2, last3 = q_sums(2, 3, FIRST, BANK), q_sums(4, 2, T - FIRST, T), q_sums(5, 3, BANK, T)
+        last1_staged = staged(nc.vector.tensor_copy, "last1_staged", last1, HALF)
+        mid2_staged = staged(nc.vector.tensor_copy, "mid2_staged", mid2, MID)
+        vector_scatter(q_tok[1], list_b, BANK, T, last1_staged[:])
+        vector_scatter(q_tok[2], list_b, FIRST, BANK, mid2_staged[:])
+
+        scalar_scatter(q_tok[0], list_b, BANK, T, last0_staged[:])
+        mid0_staged = staged(nc.scalar.copy, "mid0_staged", mid0, MID)
+        mid1_staged = staged(nc.scalar.copy, "mid1_staged", mid1, MID)
+        scalar_scatter(q_tok[0], list_b, FIRST, BANK, mid0_staged[:])
+        mid3_staged = staged(nc.scalar.copy, "mid3_staged", mid3, MID)
+        scalar_scatter(q_tok[1], list_b, FIRST, BANK, mid1_staged[:])
+        scalar_scatter(q_tok[2], list_b, BANK, T - FIRST, last2_staged[:])
+        scalar_scatter(q_tok[3], list_b, FIRST, T - HELD, mid3_staged[:, : T - HELD - FIRST])
+
+        sides = [(0, SIDE), (SIDE, T)]
+        picked = [sbuf([P, 2 * SIDE], U32, "picked_da%d" % n) for n in range(2)]
+        for h, pairs in enumerate((da_early, da_late)):
+            for n, side in enumerate(sides):
+                gather_pairs(picked[n][:, h * SIDE : (h + 1) * SIDE], pairs[:], slots_of(list_a, *side))
+        woven = [sbuf([P, PACK * SIDE], BF16, "woven_da%d" % n) for n in range(2)]
+        for n in range(2):
+            weave(nc.vector, woven[n][:], picked[n][:].rearrange("p (h n) -> p n h", h=2))
+        da_q = [quantize("da%d" % n, woven[n][:], *sides[n]) for n in range(2)]
+        share_staged = sbuf([P, FIRST], F32, "share_staged", "woven_da1")
+        nc.vector.tensor_copy(out=share_staged[:], in_=share2[:, :FIRST])
+        vector_scatter(q_tok[2], list_b, T - FIRST, T, share_staged[:])
+
+        def r_sums(index, b, first, stop):
+            sums = bank(index, "r_bank")
+            products_a(sums, b, da_q[first // SIDE], first, stop)
+            return sums
+
+        r_staged = [sbuf([P, T], F32, "r_staged%d" % b) for b in range(4)]
+        r_tok = [sbuf([P, WIDE if b == 3 else T], F32, "r_tok%d" % b) for b in range(4)]
+
+        def stage(move, sums, b, first, stop):
+            move(out=r_staged[b][:, first:stop], in_=sums[:, : stop - first])
+
+        def send(scatter, b, first, stop):
+            scatter(r_tok[b], list_a, first, stop, r_staged[b][:, first:stop])
+
+        front0 = r_sums(1, 0, 0, SIDE)
+        stage(nc.scalar.copy, front0, 0, 0, SIDE)
+        front1 = r_sums(6, 1, 0, SIDE)
+        products_a(front1[:, SIDE:], 2, da_q[0], 0, C1)
+        front2, front3 = r_sums(3, 2, C1, SIDE), r_sums(0, 3, 0, SIDE)
+        back0, back1, back2, back3 = [r_sums(index, b, SIDE, T) for b, index in enumerate((2, 7, 1, 4))]
+
+        front1_staged = sbuf([P, BANK], F32, "front1_staged")
+        nc.vector.tensor_copy(out=front1_staged[:], in_=front1[:])
+        stage(nc.vector.tensor_copy, front3, 3, 0, SIDE)
+        vector_scatter(r_tok[1], list_a, 0, SIDE, front1_staged[:, :SIDE])
+        stage(nc.vector.tensor_copy, back1, 1, SIDE, T)
+        vector_scatter(r_tok[2], list_a, 0, C1, front1_staged[:, SIDE:])
+        stage(nc.vector.tensor_copy, back3, 3, SIDE, T)
+        send(vector_scatter, 1, SIDE, T)
+        send(vector_scatter, 3, 0, T)
+
+        stage(nc.scalar.copy, front2, 2, C1, SIDE)
+        send(scalar_scatter, 0, 0, SIDE)
+        stage(nc.scalar.copy, back0, 0, SIDE, T)
+        stage(nc.scalar.copy, back2, 2, SIDE, T)
+        send(scalar_scatter, 0, SIDE, T)
+        send(scalar_scatter, 2, SIDE, T)
+        q3_held = sbuf([P, HELD], F32, "q3_held", "r_staged0")
+        nc.scalar.copy(out=q3_held[:, HELD - HALF :], in_=last3[:, :HALF])
+        nc.scalar.copy(out=q3_held[:, : HELD - HALF], in_=mid3_staged[:, MID - HELD + HALF :])
+        send(scalar_scatter, 2, C1, SIDE)
+        scalar_scatter(q_tok[3], list_b, T - HELD, T, q3_held[:])
 
         def store_rows(queue, b, cols, total):
             queue.dma_start(out=out[b * P : (b + 1) * P, cols], in_=total[:, cols])
 
         for b in range(3):
-            total = sbuf([P, T], F32, "total%d" % b)
+            total = sbuf([P, T], F32, "total%d" % b, "q_tok%d" % (b - 1) if b else None)
             nc.gpsimd.tensor_tensor(out=total[:], in0=r_tok[b][:, :T], in1=q_tok[b][:, :T], op=ALU.add)
             store_rows(nc.sync, b, slice(0, T), total)
         total = sbuf([P, T], F32, "total3")

@@ -30,7 +30,6 @@ LINE = 16
 WIDE = 1024
 FIRST = 128
 SIDE = T // 2
-HELD = 320
 
 
 def tile_moe_plb_relu_kernel(
@@ -71,10 +70,9 @@ def tile_moe_plb_relu_kernel(
         for plane in (w2_scale_raw, dy_scale, wb_scale, wa_scale):
             nc.vector.memset(plane[:].bitcast(I32), 0)
         dc_rows = [sbuf([P, WIDE], BF16, "dc_row%d" % e) for e in range(2)]
-        dc_late = sbuf([P, 2 * WIDE], BF16, "dc_late")
+        dc_late = sbuf([P, 2 * T], BF16, "dc_late")
         for row in dc_rows:
             nc.vector.memset(row[:, T:], 0.0)
-        nc.vector.memset(dc_late[:, 2 * T :], 0.0)
 
         w2_raw = sbuf([P, PASSES, H], I32, "w2_raw")
         nc.sync.dma_start(out=w2_raw[:], in_=w2t_words.rearrange("s p i d -> p s (i d)").bitcast(I32))
@@ -86,13 +84,16 @@ def tile_moe_plb_relu_kernel(
         a_view = a.rearrange("(p h e) t -> h p e t", h=2, e=2)
         c_view = c.rearrange("(p h e) t -> h p e t", h=2, e=2)
         a_early = sbuf([P, 2, T], F32, "a_early")
-        nc.sync.dma_start(out=a_early[:, :, short], in_=a_view[0][:, :, short])
+        for tokens in (short, long):
+            nc.sync.dma_start(out=a_early[:, 0, tokens], in_=a_view[0][:, 0, tokens])
+        nc.sync.dma_start(out=a_early[:, 1, :], in_=a_view[0][:, 1, :])
         list_b = sbuf([P, T // STRIPE], U16, "list_b")
         nc.sync.dma_start(list_b[:], offs2)
-        nc.sync.dma_start(out=a_early[:, :, long], in_=a_view[0][:, :, long])
-        a_late = [sbuf([P, 2, HALF], F32, "a_late%d" % t) for t in range(PARTS)]
-        for t in range(PARTS):
-            nc.sync.dma_start(out=a_late[t][:], in_=a_view[1][:, :, part(t)])
+        a_late = []
+        for n, tokens in enumerate((long, short)):
+            piece = sbuf([P, 2, tokens.stop - tokens.start], F32, "a_late%d" % n)
+            nc.sync.dma_start(out=piece[:], in_=a_view[1][:, :, tokens])
+            a_late.extend(piece[:, :, part(t)] for t in range(2 - n))
         wb_codes = sbuf([P, E2, 2 * K], U8, "wb_codes")
         nc.sync.dma_start(out=wb_codes[:].bitcast(I32), in_=wbt_words.rearrange("f s p w -> p (f s) w").bitcast(I32))
         load_scale_rows(wb_scale, wbt_scales.rearrange("f s b k -> (f s) b k"))
@@ -155,11 +156,13 @@ def tile_moe_plb_relu_kernel(
             )
 
         early_banks = [bank(n, "dh_bank") for n in range(PARTS)]
-        for e, sums in enumerate((early_banks[1], bank(7, "dh_bank"))):
-            dh_into(sums[:, :HALF], e, short)
-            by_mask(e, short, sums[:, :HALF])
+        dh_into(early_banks[1][:, :HALF], 0, short)
+        by_mask(0, short, early_banks[1][:, :HALF])
         dh_into(early_banks[0][:], 0, long)
         gated(dc_rows[0][:, long], a_early[:, 0, long], early_banks[0][:], ALU.max)
+        sums = bank(7, "dh_bank")
+        dh_into(sums[:, :HALF], 1, short)
+        by_mask(1, short, sums[:, :HALF])
         dh_into(early_banks[2][:], 1, long)
         by_mask(1, long, early_banks[2][:])
 
@@ -169,7 +172,7 @@ def tile_moe_plb_relu_kernel(
                 dh_into(late_banks[t][:, part(e)], 2 + e, part(t))
             gated(
                 dc_late[:, t * BANK : (t + 1) * BANK].rearrange("p (t e) -> p t e", e=2),
-                a_late[t][:].rearrange("p e t -> p t e"),
+                a_late[t].rearrange("p e t -> p t e"),
                 late_banks[t][:].rearrange("p (e t) -> p t e", e=2),
                 ALU.max,
             )
@@ -225,16 +228,16 @@ def tile_moe_plb_relu_kernel(
         REST = T - FIRST
         head, rest = slots_of(list_b, 0, FIRST), slots_of(list_b, FIRST, T)
         picked_rest = sbuf([P, 2 * REST], U32, "picked_rest")
-        woven_head = picked_rest[:, REST : REST + 2 * FIRST]
+        woven_head = picked_rest[:, REST + BANK - FIRST - FIRST : REST + BANK]
         for e in range(2):
             gather_row(woven_head.bitcast(BF16), PACK, e, head)
             gather_row(picked_rest[:, :REST].bitcast(BF16), 2, e, rest)
         gather_pairs(woven_head.rearrange("p (n h) -> p n h", h=2)[:, :, 1], dc_late[:], head)
         for t in range(2):
             gated(masked_early[:, 0, part(t)], a_early[:, 0, part(t)], early_banks[0][:, part(t)], ALU.is_gt)
-        masked_late = sbuf([P, 2, T], F32, "masked_late")
+        masked_first = sbuf([P, 2, HALF], F32, "masked_first")
         for e in range(2):
-            gated(masked_late[:, e, part(0)], a_late[0][:, e, :], late_banks[0][:, part(e)], ALU.is_gt)
+            gated(masked_first[:, e, :], a_late[0][:, e, :], late_banks[0][:, part(e)], ALU.is_gt)
         dc_head = quantize("dc_head", woven_head.bitcast(BF16), 0, FIRST)
         staged = []
         for index, blocks in ((1, (1, 3)), (7, (0, 2))):
@@ -255,20 +258,23 @@ def tile_moe_plb_relu_kernel(
             )
 
         MID = BANK - FIRST
-        gather_pairs(picked_rest[:, REST:], dc_late[:], rest)
+        gather_pairs(picked_rest[:, REST + MID :], dc_late[:], slots_of(list_b, BANK, T))
+        gather_pairs(picked_rest[:, REST : REST + MID], dc_late[:], slots_of(list_b, FIRST, BANK))
         planes = picked_rest[:].rearrange("p (h n) -> p n h", h=2)
-        gated(masked_late[:, :, part(1)], a_late[1][:], two_rows(late_banks[1][:]), ALU.is_gt)
-        woven_rest = at(0, [P, PACK * REST], BF16, "woven_rest")
+        woven_rest = at(4 * T, [P, PACK * REST], BF16, "woven_rest")
         weave(nc.vector, woven_rest[:, PACK * MID :], planes[:, MID:, :])
         weave(nc.vector, woven_rest[:, : PACK * MID], planes[:, :MID, :])
         dc_last = quantize("dc_last", woven_rest[:, PACK * MID :], BANK, T)
         dc_mid = quantize("dc_mid", woven_rest[:, : PACK * MID], FIRST, BANK)
-        gated(masked_late[:, :, part(2)], a_late[2][:], two_rows(late_banks[2][:]), ALU.is_gt)
+        masked_late = at(WIDE + 8 * T, [P, 2, BANK], F32, "masked_late")
+        for t in range(1, PARTS):
+            gated(masked_late[:, :, part(t - 1)], a_late[t], two_rows(late_banks[t][:]), ALU.is_gt)
 
-        da_early = at(0, [P, 2 * T], BF16, "da_early")
+        da_early = at(WIDE, [P, 2 * T], BF16, "da_early")
         da_into(da_early[:], masked_early[:], c_early[:])
-        da_late = at(4 * T, [P, 2 * T], BF16, "da_late")
-        da_into(da_late[:], masked_late[:], c_late[:])
+        da_late = at(WIDE + 4 * T, [P, 2 * T], BF16, "da_late")
+        da_into(da_late[:, :BANK], masked_first[:], c_late[:, :, :HALF])
+        da_into(da_late[:, BANK:], masked_late[:], c_late[:, :, HALF:])
 
         def q_sums(index, b, first, stop):
             sums = bank(index, "q_bank")
@@ -284,7 +290,8 @@ def tile_moe_plb_relu_kernel(
         mid2, mid0, mid1 = q_sums(0, 2, FIRST, BANK), q_sums(3, 0, FIRST, BANK), q_sums(7, 1, FIRST, BANK)
         last0_staged = staged(nc.scalar.copy, "last0_staged", last0, HALF)
         last2_staged = staged(nc.scalar.copy, "last2_staged", last2, FIRST)
-        mid3, share2, last3 = q_sums(2, 3, FIRST, BANK), q_sums(4, 2, T - FIRST, T), q_sums(5, 3, BANK, T)
+        mid3, share2, held3 = q_sums(2, 3, FIRST, SIDE), q_sums(4, 2, T - FIRST, T), q_sums(5, 3, SIDE, BANK)
+        products_b(held3[:, BANK - SIDE :], 3, dc_last, BANK, T)
         last1_staged = staged(nc.vector.tensor_copy, "last1_staged", last1, HALF)
         mid2_staged = staged(nc.vector.tensor_copy, "mid2_staged", mid2, MID)
         vector_scatter(q_tok[1], list_b, BANK, T, last1_staged[:])
@@ -294,10 +301,10 @@ def tile_moe_plb_relu_kernel(
         mid0_staged = staged(nc.scalar.copy, "mid0_staged", mid0, MID)
         mid1_staged = staged(nc.scalar.copy, "mid1_staged", mid1, MID)
         scalar_scatter(q_tok[0], list_b, FIRST, BANK, mid0_staged[:])
-        mid3_staged = staged(nc.scalar.copy, "mid3_staged", mid3, MID)
+        mid3_staged = staged(nc.scalar.copy, "mid3_staged", mid3, SIDE - FIRST)
         scalar_scatter(q_tok[1], list_b, FIRST, BANK, mid1_staged[:])
         scalar_scatter(q_tok[2], list_b, BANK, T - FIRST, last2_staged[:])
-        scalar_scatter(q_tok[3], list_b, FIRST, T - HELD, mid3_staged[:, : T - HELD - FIRST])
+        scalar_scatter(q_tok[3], list_b, FIRST, SIDE, mid3_staged[:])
 
         sides = [(0, SIDE), (SIDE, T)]
         picked = [sbuf([P, 2 * SIDE], U32, "picked_da%d" % n) for n in range(2)]
@@ -349,11 +356,10 @@ def tile_moe_plb_relu_kernel(
         stage(nc.scalar.copy, back2, 2, SIDE, T)
         send(scalar_scatter, 0, SIDE, T)
         send(scalar_scatter, 2, SIDE, T)
-        q3_held = sbuf([P, HELD], F32, "q3_held", "r_staged0")
-        nc.scalar.copy(out=q3_held[:, HELD - HALF :], in_=last3[:, :HALF])
-        nc.scalar.copy(out=q3_held[:, : HELD - HALF], in_=mid3_staged[:, MID - HELD + HALF :])
+        q3_held = sbuf([P, SIDE], F32, "q3_held", "r_staged0")
+        nc.scalar.copy(out=q3_held[:], in_=held3[:, :SIDE])
         send(scalar_scatter, 2, C1, SIDE)
-        scalar_scatter(q_tok[3], list_b, T - HELD, T, q3_held[:])
+        scalar_scatter(q_tok[3], list_b, SIDE, T, q3_held[:])
 
         def store_rows(queue, b, cols, total):
             queue.dma_start(out=out[b * P : (b + 1) * P, cols], in_=total[:, cols])

@@ -30,6 +30,8 @@ LINE = 16
 WIDE = 1024
 FIRST = 128
 SIDE = T // 2
+SHARE = 192
+SHIFT = 64
 
 
 def tile_moe_plb_relu_kernel(
@@ -84,11 +86,10 @@ def tile_moe_plb_relu_kernel(
         a_view = a.rearrange("(p h e) t -> h p e t", h=2, e=2)
         c_view = c.rearrange("(p h e) t -> h p e t", h=2, e=2)
         a_early = sbuf([P, 2, T], F32, "a_early")
-        for tokens in (short, long):
-            nc.sync.dma_start(out=a_early[:, 0, tokens], in_=a_view[0][:, 0, tokens])
-        nc.sync.dma_start(out=a_early[:, 1, :], in_=a_view[0][:, 1, :])
+        nc.sync.dma_start(out=a_early[:, :, short], in_=a_view[0][:, :, short])
         list_b = sbuf([P, T // STRIPE], U16, "list_b")
         nc.sync.dma_start(list_b[:], offs2)
+        nc.sync.dma_start(out=a_early[:, :, long], in_=a_view[0][:, :, long])
         a_late = []
         for n, tokens in enumerate((long, short)):
             piece = sbuf([P, 2, tokens.stop - tokens.start], F32, "a_late%d" % n)
@@ -156,13 +157,11 @@ def tile_moe_plb_relu_kernel(
             )
 
         early_banks = [bank(n, "dh_bank") for n in range(PARTS)]
-        dh_into(early_banks[1][:, :HALF], 0, short)
-        by_mask(0, short, early_banks[1][:, :HALF])
+        for e, sums in enumerate((early_banks[1], bank(7, "dh_bank"))):
+            dh_into(sums[:, :HALF], e, short)
+            by_mask(e, short, sums[:, :HALF])
         dh_into(early_banks[0][:], 0, long)
         gated(dc_rows[0][:, long], a_early[:, 0, long], early_banks[0][:], ALU.max)
-        sums = bank(7, "dh_bank")
-        dh_into(sums[:, :HALF], 1, short)
-        by_mask(1, short, sums[:, :HALF])
         dh_into(early_banks[2][:], 1, long)
         by_mask(1, long, early_banks[2][:])
 
@@ -289,13 +288,14 @@ def tile_moe_plb_relu_kernel(
         last0, last1, last2 = q_sums(2, 0, BANK, T), q_sums(6, 1, BANK, T), q_sums(1, 2, BANK, T - FIRST)
         mid2, mid0, mid1 = q_sums(0, 2, FIRST, BANK), q_sums(3, 0, FIRST, BANK), q_sums(7, 1, FIRST, BANK)
         last0_staged = staged(nc.scalar.copy, "last0_staged", last0, HALF)
-        last2_staged = staged(nc.scalar.copy, "last2_staged", last2, FIRST)
+        q2_staged = sbuf([P, BANK], F32, "q2_staged")
+        nc.scalar.copy(out=q2_staged[:, MID:], in_=last2[:, :FIRST])
         mid3, share2, held3 = q_sums(2, 3, FIRST, SIDE), q_sums(4, 2, T - FIRST, T), q_sums(5, 3, SIDE, BANK)
         products_b(held3[:, BANK - SIDE :], 3, dc_last, BANK, T)
         last1_staged = staged(nc.vector.tensor_copy, "last1_staged", last1, HALF)
-        mid2_staged = staged(nc.vector.tensor_copy, "mid2_staged", mid2, MID)
+        nc.vector.tensor_copy(out=q2_staged[:, :MID], in_=mid2[:, :MID])
         vector_scatter(q_tok[1], list_b, BANK, T, last1_staged[:])
-        vector_scatter(q_tok[2], list_b, FIRST, BANK, mid2_staged[:])
+        vector_scatter(q_tok[2], list_b, FIRST, BANK - SHIFT, q2_staged[:, : MID - SHIFT])
 
         scalar_scatter(q_tok[0], list_b, BANK, T, last0_staged[:])
         mid0_staged = staged(nc.scalar.copy, "mid0_staged", mid0, MID)
@@ -303,7 +303,7 @@ def tile_moe_plb_relu_kernel(
         scalar_scatter(q_tok[0], list_b, FIRST, BANK, mid0_staged[:])
         mid3_staged = staged(nc.scalar.copy, "mid3_staged", mid3, SIDE - FIRST)
         scalar_scatter(q_tok[1], list_b, FIRST, BANK, mid1_staged[:])
-        scalar_scatter(q_tok[2], list_b, BANK, T - FIRST, last2_staged[:])
+        scalar_scatter(q_tok[2], list_b, BANK - SHIFT, T - FIRST, q2_staged[:, MID - SHIFT :])
         scalar_scatter(q_tok[3], list_b, FIRST, SIDE, mid3_staged[:])
 
         sides = [(0, SIDE), (SIDE, T)]
@@ -336,21 +336,19 @@ def tile_moe_plb_relu_kernel(
         front0 = r_sums(1, 0, 0, SIDE)
         stage(nc.scalar.copy, front0, 0, 0, SIDE)
         front1 = r_sums(6, 1, 0, SIDE)
-        products_a(front1[:, SIDE:], 2, da_q[0], 0, C1)
-        front2, front3 = r_sums(3, 2, C1, SIDE), r_sums(0, 3, 0, SIDE)
+        front2, front3 = r_sums(3, 2, 0, SIDE), r_sums(0, 3, 0, SIDE)
         back0, back1, back2, back3 = [r_sums(index, b, SIDE, T) for b, index in enumerate((2, 7, 1, 4))]
 
-        front1_staged = sbuf([P, BANK], F32, "front1_staged")
-        nc.vector.tensor_copy(out=front1_staged[:], in_=front1[:])
+        stage(nc.scalar.copy, front2, 2, 0, SIDE)
+        stage(nc.vector.tensor_copy, front1, 1, 0, SIDE)
         stage(nc.vector.tensor_copy, front3, 3, 0, SIDE)
-        vector_scatter(r_tok[1], list_a, 0, SIDE, front1_staged[:, :SIDE])
+        send(vector_scatter, 1, 0, SIDE)
         stage(nc.vector.tensor_copy, back1, 1, SIDE, T)
-        vector_scatter(r_tok[2], list_a, 0, C1, front1_staged[:, SIDE:])
+        send(vector_scatter, 2, 0, SHARE)
         stage(nc.vector.tensor_copy, back3, 3, SIDE, T)
         send(vector_scatter, 1, SIDE, T)
         send(vector_scatter, 3, 0, T)
 
-        stage(nc.scalar.copy, front2, 2, C1, SIDE)
         send(scalar_scatter, 0, 0, SIDE)
         stage(nc.scalar.copy, back0, 0, SIDE, T)
         stage(nc.scalar.copy, back2, 2, SIDE, T)
@@ -358,7 +356,7 @@ def tile_moe_plb_relu_kernel(
         send(scalar_scatter, 2, SIDE, T)
         q3_held = sbuf([P, SIDE], F32, "q3_held", "r_staged0")
         nc.scalar.copy(out=q3_held[:], in_=held3[:, :SIDE])
-        send(scalar_scatter, 2, C1, SIDE)
+        send(scalar_scatter, 2, SHARE, SIDE)
         scalar_scatter(q_tok[3], list_b, SIDE, T, q3_held[:])
 
         def store_rows(queue, b, cols, total):

@@ -30,7 +30,7 @@ LINE = 16
 WIDE = 1024
 FIRST = 128
 SIDE = T // 2
-SHARE = 192
+SHARE = 224
 SHIFT = 64
 
 
@@ -98,10 +98,12 @@ def tile_moe_plb_relu_kernel(
         wb_codes = sbuf([P, E2, 2 * K], U8, "wb_codes")
         nc.sync.dma_start(out=wb_codes[:].bitcast(I32), in_=wbt_words.rearrange("f s p w -> p (f s) w").bitcast(I32))
         load_scale_rows(wb_scale, wbt_scales.rearrange("f s b k -> (f s) b k"))
+        c_first = sbuf([P, 2, HALF], F32, "c_first")
+        nc.sync.dma_start(out=c_first[:], in_=c_view[1][:, :, :HALF])
         c_early = sbuf([P, 2, T], F32, "c_early")
         nc.sync.dma_start(out=c_early[:], in_=c_view[0])
-        c_late = sbuf([P, 2, T], F32, "c_late")
-        nc.sync.dma_start(out=c_late[:], in_=c_view[1])
+        c_late = sbuf([P, 2, BANK], F32, "c_late")
+        nc.sync.dma_start(out=c_late[:], in_=c_view[1][:, :, HALF:])
         list_a = sbuf([P, T // STRIPE], U16, "list_a")
         nc.sync.dma_start(list_a[:], offs)
         wa_codes = sbuf([P, E1, K], I32, "wa_codes")
@@ -227,16 +229,16 @@ def tile_moe_plb_relu_kernel(
         REST = T - FIRST
         head, rest = slots_of(list_b, 0, FIRST), slots_of(list_b, FIRST, T)
         picked_rest = sbuf([P, 2 * REST], U32, "picked_rest")
-        woven_head = picked_rest[:, REST + BANK - FIRST - FIRST : REST + BANK]
+        woven_head = at(0, [P, 2 * FIRST], U32, "woven_head")[:]
         for e in range(2):
             gather_row(woven_head.bitcast(BF16), PACK, e, head)
             gather_row(picked_rest[:, :REST].bitcast(BF16), 2, e, rest)
         gather_pairs(woven_head.rearrange("p (n h) -> p n h", h=2)[:, :, 1], dc_late[:], head)
-        for t in range(2):
-            gated(masked_early[:, 0, part(t)], a_early[:, 0, part(t)], early_banks[0][:, part(t)], ALU.is_gt)
         masked_first = sbuf([P, 2, HALF], F32, "masked_first")
         for e in range(2):
             gated(masked_first[:, e, :], a_late[0][:, e, :], late_banks[0][:, part(e)], ALU.is_gt)
+        for t in range(2):
+            gated(masked_early[:, 0, part(t)], a_early[:, 0, part(t)], early_banks[0][:, part(t)], ALU.is_gt)
         dc_head = quantize("dc_head", woven_head.bitcast(BF16), 0, FIRST)
         staged = []
         for index, blocks in ((1, (1, 3)), (7, (0, 2))):
@@ -256,24 +258,26 @@ def tile_moe_plb_relu_kernel(
                 op=ALU.mult,
             )
 
+        da_late = at(0, [P, 2 * T], BF16, "da_late")
+        da_into(da_late[:, :BANK], masked_first[:], c_first[:])
+
         MID = BANK - FIRST
         gather_pairs(picked_rest[:, REST + MID :], dc_late[:], slots_of(list_b, BANK, T))
         gather_pairs(picked_rest[:, REST : REST + MID], dc_late[:], slots_of(list_b, FIRST, BANK))
         planes = picked_rest[:].rearrange("p (h n) -> p n h", h=2)
-        woven_rest = at(4 * T, [P, PACK * REST], BF16, "woven_rest")
-        weave(nc.vector, woven_rest[:, PACK * MID :], planes[:, MID:, :])
-        weave(nc.vector, woven_rest[:, : PACK * MID], planes[:, :MID, :])
-        dc_last = quantize("dc_last", woven_rest[:, PACK * MID :], BANK, T)
-        dc_mid = quantize("dc_mid", woven_rest[:, : PACK * MID], FIRST, BANK)
-        masked_late = at(WIDE + 8 * T, [P, 2, BANK], F32, "masked_late")
+        woven_mid = at(4 * T, [P, PACK * MID], BF16, "woven_mid")
+        woven_last = at(8 * T, [P, PACK * HALF], BF16, "woven_last")
+        weave(nc.vector, woven_last[:], planes[:, MID:, :])
+        weave(nc.vector, woven_mid[:], planes[:, :MID, :])
+        dc_last = quantize("dc_last", woven_last[:], BANK, T)
+        dc_mid = quantize("dc_mid", woven_mid[:], FIRST, BANK)
+        masked_late = at(8 * T, [P, 2, BANK], F32, "masked_late")
         for t in range(1, PARTS):
             gated(masked_late[:, :, part(t - 1)], a_late[t], two_rows(late_banks[t][:]), ALU.is_gt)
 
-        da_early = at(WIDE, [P, 2 * T], BF16, "da_early")
+        da_early = at(4 * T, [P, 2 * T], BF16, "da_early")
         da_into(da_early[:], masked_early[:], c_early[:])
-        da_late = at(WIDE + 4 * T, [P, 2 * T], BF16, "da_late")
-        da_into(da_late[:, :BANK], masked_first[:], c_late[:, :, :HALF])
-        da_into(da_late[:, BANK:], masked_late[:], c_late[:, :, HALF:])
+        da_into(da_late[:, BANK:], masked_late[:], c_late[:])
 
         def q_sums(index, b, first, stop):
             sums = bank(index, "q_bank")
@@ -314,9 +318,10 @@ def tile_moe_plb_relu_kernel(
         woven = [sbuf([P, PACK * SIDE], BF16, "woven_da%d" % n) for n in range(2)]
         for n in range(2):
             weave(nc.vector, woven[n][:], picked[n][:].rearrange("p (h n) -> p n h", h=2))
-        da_q = [quantize("da%d" % n, woven[n][:], *sides[n]) for n in range(2)]
-        share_staged = sbuf([P, FIRST], F32, "share_staged", "woven_da1")
+        da_q = [quantize("da0", woven[0][:], *sides[0])]
+        share_staged = sbuf([P, FIRST], F32, "share_staged", "picked_da1")
         nc.vector.tensor_copy(out=share_staged[:], in_=share2[:, :FIRST])
+        da_q.append(quantize("da1", woven[1][:], *sides[1]))
         vector_scatter(q_tok[2], list_b, T - FIRST, T, share_staged[:])
 
         def r_sums(index, b, first, stop):
@@ -333,9 +338,8 @@ def tile_moe_plb_relu_kernel(
         def send(scatter, b, first, stop):
             scatter(r_tok[b], list_a, first, stop, r_staged[b][:, first:stop])
 
-        front0 = r_sums(1, 0, 0, SIDE)
+        front1, front0 = r_sums(6, 1, 0, SIDE), r_sums(1, 0, 0, SIDE)
         stage(nc.scalar.copy, front0, 0, 0, SIDE)
-        front1 = r_sums(6, 1, 0, SIDE)
         front2, front3 = r_sums(3, 2, 0, SIDE), r_sums(0, 3, 0, SIDE)
         back0, back1, back2, back3 = [r_sums(index, b, SIDE, T) for b, index in enumerate((2, 7, 1, 4))]
 

@@ -73,8 +73,6 @@ def tile_moe_plb_relu_kernel(
             nc.vector.memset(plane[:].bitcast(I32), 0)
         dc_rows = [sbuf([P, WIDE], BF16, "dc_row%d" % e) for e in range(2)]
         dc_late = sbuf([P, 2 * T], BF16, "dc_late")
-        for row in dc_rows:
-            nc.vector.memset(row[:, T:], 0.0)
 
         w2_raw = sbuf([P, PASSES, H], I32, "w2_raw")
         nc.sync.dma_start(out=w2_raw[:], in_=w2t_words.rearrange("s p i d -> p s (i d)").bitcast(I32))
@@ -87,19 +85,20 @@ def tile_moe_plb_relu_kernel(
         c_view = c.rearrange("(p h e) t -> h p e t", h=2, e=2)
         a_early = sbuf([P, 2, T], F32, "a_early")
         nc.sync.dma_start(out=a_early[:, :, short], in_=a_view[0][:, :, short])
+        for e in range(2):
+            nc.sync.dma_start(out=a_early[:, e, long], in_=a_view[0][:, e, long])
         list_b = sbuf([P, T // STRIPE], U16, "list_b")
         nc.sync.dma_start(list_b[:], offs2)
-        nc.sync.dma_start(out=a_early[:, :, long], in_=a_view[0][:, :, long])
         a_late = []
         for n, tokens in enumerate((long, short)):
             piece = sbuf([P, 2, tokens.stop - tokens.start], F32, "a_late%d" % n)
             nc.sync.dma_start(out=piece[:], in_=a_view[1][:, :, tokens])
             a_late.extend(piece[:, :, part(t)] for t in range(2 - n))
+        c_first = sbuf([P, 2, HALF], F32, "c_first")
+        nc.sync.dma_start(out=c_first[:], in_=c_view[1][:, :, :HALF])
         wb_codes = sbuf([P, E2, 2 * K], U8, "wb_codes")
         nc.sync.dma_start(out=wb_codes[:].bitcast(I32), in_=wbt_words.rearrange("f s p w -> p (f s) w").bitcast(I32))
         load_scale_rows(wb_scale, wbt_scales.rearrange("f s b k -> (f s) b k"))
-        c_first = sbuf([P, 2, HALF], F32, "c_first")
-        nc.sync.dma_start(out=c_first[:], in_=c_view[1][:, :, :HALF])
         c_early = sbuf([P, 2, T], F32, "c_early")
         nc.sync.dma_start(out=c_early[:], in_=c_view[0])
         c_late = sbuf([P, 2, BANK], F32, "c_late")
@@ -162,8 +161,10 @@ def tile_moe_plb_relu_kernel(
         for e, sums in enumerate((early_banks[1], bank(7, "dh_bank"))):
             dh_into(sums[:, :HALF], e, short)
             by_mask(e, short, sums[:, :HALF])
-        dh_into(early_banks[0][:], 0, long)
-        gated(dc_rows[0][:, long], a_early[:, 0, long], early_banks[0][:], ALU.max)
+        direct_banks = [early_banks[0], bank(6, "dh_bank")]
+        for t in range(2):
+            dh_into(direct_banks[t][:, :HALF], 0, part(t))
+            gated(dc_rows[0][:, part(t)], a_early[:, 0, part(t)], direct_banks[t][:, :HALF], ALU.max)
         dh_into(early_banks[2][:], 1, long)
         by_mask(1, long, early_banks[2][:])
 
@@ -238,7 +239,7 @@ def tile_moe_plb_relu_kernel(
         for e in range(2):
             gated(masked_first[:, e, :], a_late[0][:, e, :], late_banks[0][:, part(e)], ALU.is_gt)
         for t in range(2):
-            gated(masked_early[:, 0, part(t)], a_early[:, 0, part(t)], early_banks[0][:, part(t)], ALU.is_gt)
+            gated(masked_early[:, 0, part(t)], a_early[:, 0, part(t)], direct_banks[t][:, :HALF], ALU.is_gt)
         dc_head = quantize("dc_head", woven_head.bitcast(BF16), 0, FIRST)
         staged = []
         for index, blocks in ((1, (1, 3)), (7, (0, 2))):
@@ -258,26 +259,26 @@ def tile_moe_plb_relu_kernel(
                 op=ALU.mult,
             )
 
-        da_late = at(0, [P, 2 * T], BF16, "da_late")
+        da_late = at(0, [P, 2 * WIDE], BF16, "da_late")
         da_into(da_late[:, :BANK], masked_first[:], c_first[:])
 
         MID = BANK - FIRST
         gather_pairs(picked_rest[:, REST + MID :], dc_late[:], slots_of(list_b, BANK, T))
         gather_pairs(picked_rest[:, REST : REST + MID], dc_late[:], slots_of(list_b, FIRST, BANK))
         planes = picked_rest[:].rearrange("p (h n) -> p n h", h=2)
-        woven_mid = at(4 * T, [P, PACK * MID], BF16, "woven_mid")
-        woven_last = at(8 * T, [P, PACK * HALF], BF16, "woven_last")
+        woven_mid = at(4 * WIDE, [P, PACK * MID], BF16, "woven_mid")
+        woven_last = at(8 * WIDE, [P, PACK * HALF], BF16, "woven_last")
         weave(nc.vector, woven_last[:], planes[:, MID:, :])
         weave(nc.vector, woven_mid[:], planes[:, :MID, :])
         dc_last = quantize("dc_last", woven_last[:], BANK, T)
         dc_mid = quantize("dc_mid", woven_mid[:], FIRST, BANK)
-        masked_late = at(8 * T, [P, 2, BANK], F32, "masked_late")
+        masked_late = at(8 * WIDE, [P, 2, BANK], F32, "masked_late")
         for t in range(1, PARTS):
             gated(masked_late[:, :, part(t - 1)], a_late[t], two_rows(late_banks[t][:]), ALU.is_gt)
 
-        da_early = at(4 * T, [P, 2 * T], BF16, "da_early")
-        da_into(da_early[:], masked_early[:], c_early[:])
-        da_into(da_late[:, BANK:], masked_late[:], c_late[:])
+        da_early = at(4 * WIDE, [P, 2 * WIDE], BF16, "da_early")
+        da_into(da_early[:, : 2 * T], masked_early[:], c_early[:])
+        da_into(da_late[:, BANK : 2 * T], masked_late[:], c_late[:])
 
         def q_sums(index, b, first, stop):
             sums = bank(index, "q_bank")
@@ -289,7 +290,7 @@ def tile_moe_plb_relu_kernel(
             move(out=values[:], in_=sums[:, :width])
             return values
 
-        last0, last1, last2 = q_sums(2, 0, BANK, T), q_sums(6, 1, BANK, T), q_sums(1, 2, BANK, T - FIRST)
+        last1, last0, last2 = q_sums(6, 1, BANK, T), q_sums(2, 0, BANK, T), q_sums(1, 2, BANK, T - FIRST)
         mid2, mid0, mid1 = q_sums(0, 2, FIRST, BANK), q_sums(3, 0, FIRST, BANK), q_sums(7, 1, FIRST, BANK)
         last0_staged = staged(nc.scalar.copy, "last0_staged", last0, HALF)
         q2_staged = sbuf([P, BANK], F32, "q2_staged")
@@ -311,17 +312,15 @@ def tile_moe_plb_relu_kernel(
         scalar_scatter(q_tok[3], list_b, FIRST, SIDE, mid3_staged[:])
 
         sides = [(0, SIDE), (SIDE, T)]
-        picked = [sbuf([P, 2 * SIDE], U32, "picked_da%d" % n) for n in range(2)]
+        picked = sbuf([P, 2 * T], U32, "picked_da")
         for h, pairs in enumerate((da_early, da_late)):
-            for n, side in enumerate(sides):
-                gather_pairs(picked[n][:, h * SIDE : (h + 1) * SIDE], pairs[:], slots_of(list_a, *side))
-        woven = [sbuf([P, PACK * SIDE], BF16, "woven_da%d" % n) for n in range(2)]
-        for n in range(2):
-            weave(nc.vector, woven[n][:], picked[n][:].rearrange("p (h n) -> p n h", h=2))
-        da_q = [quantize("da0", woven[0][:], *sides[0])]
-        share_staged = sbuf([P, FIRST], F32, "share_staged", "picked_da1")
+            gather_pairs(picked[:, h * T : (h + 1) * T], pairs[:], list_a[:])
+        share_staged = at(0, [P, FIRST], F32, "share_staged")
         nc.vector.tensor_copy(out=share_staged[:], in_=share2[:, :FIRST])
-        da_q.append(quantize("da1", woven[1][:], *sides[1]))
+        woven = [sbuf([P, PACK * SIDE], BF16, "woven_da%d" % n) for n in range(2)]
+        for n, (first, stop) in enumerate(sides):
+            weave(nc.vector, woven[n][:], picked[:].rearrange("p (h n) -> p n h", h=2)[:, first:stop, :])
+        da_q = [quantize("da%d" % n, woven[n][:], *sides[n]) for n in range(2)]
         vector_scatter(q_tok[2], list_b, T - FIRST, T, share_staged[:])
 
         def r_sums(index, b, first, stop):

@@ -329,7 +329,8 @@ def tile_moe_plb_relu_kernel(
             return sums
 
         r_staged = [sbuf([P, T], F32, "r_staged%d" % b) for b in range(4)]
-        r_tok = [sbuf([P, WIDE if b == 3 else T], F32, "r_tok%d" % b) for b in range(4)]
+        r_tok = [sbuf([P, WIDE if b == 3 else T], F32, "r_tok%d" % b, None if b else "c_late") for b in range(4)]
+        nc.gpsimd.tensor_copy(out=r_tok[0][:], in_=q_tok[0][:])
 
         def stage(move, sums, b, first, stop):
             move(out=r_staged[b][:, first:stop], in_=sums[:, : stop - first])
@@ -347,19 +348,19 @@ def tile_moe_plb_relu_kernel(
         stage(nc.vector.tensor_copy, front3, 3, 0, SIDE)
         send(vector_scatter, 1, 0, SIDE)
         stage(nc.vector.tensor_copy, back1, 1, SIDE, T)
-        send(vector_scatter, 2, 0, SHARE)
+        send(vector_scatter, 0, 0, SHARE)
         stage(nc.vector.tensor_copy, back3, 3, SIDE, T)
         send(vector_scatter, 1, SIDE, T)
         send(vector_scatter, 3, 0, T)
 
-        send(scalar_scatter, 0, 0, SIDE)
+        scalar_scatter(q_tok[0], list_a, SHARE, SIDE, r_staged[0][:, SHARE:SIDE])
         stage(nc.scalar.copy, back0, 0, SIDE, T)
         stage(nc.scalar.copy, back2, 2, SIDE, T)
-        send(scalar_scatter, 0, SIDE, T)
+        scalar_scatter(q_tok[0], list_a, SIDE, T, r_staged[0][:, SIDE:])
         send(scalar_scatter, 2, SIDE, T)
         q3_held = sbuf([P, SIDE], F32, "q3_held", "r_staged0")
         nc.scalar.copy(out=q3_held[:], in_=held3[:, :SIDE])
-        send(scalar_scatter, 2, SHARE, SIDE)
+        send(scalar_scatter, 2, 0, SIDE)
         scalar_scatter(q_tok[3], list_b, SIDE, T, q3_held[:])
 
         def store_rows(queue, b, cols, total):

from contextlib import ExitStack

import concourse.mybir as mybir

K, T, H, N = 512, 768, 512, 1024
E1, C1, E2, C2 = 6, 128, 3, 256
FLOPS = 2 * T * H * (N + 2 * K)

F32 = mybir.dt.float32
BF16 = mybir.dt.bfloat16
I32 = mybir.dt.int32
U32 = mybir.dt.uint32
U16 = mybir.dt.uint16
U8 = mybir.dt.uint8
FP8X4 = mybir.dt.float8_e4m3fn_x4
FP4X4 = mybir.dt.float4_e2m1fn_x4
ALU = mybir.AluOpType
COPY = mybir.ActivationFunctionType.Copy

P = 128
PACK = 4
PASSES = N // (P * PACK)
BANK = 512
HALF = BANK // 2
PARTS = T // HALF
STRIPE = 16
QUADRANT = 32
SCALE_ROWS = 4
LINE = 16
WIDE = 1024
FIRST = 128
SIDE = T // 2
SHARE = 224
SHIFT = 64


def tile_moe_plb_relu_kernel(
    tc, dy_words, dy_scales, w2t_words, w2t_scales, wat_words, wat_scales, wbt_words, wbt_scales, a, c, offs, offs2, out
):
    nc = tc.nc
    with ExitStack() as ctx:
        keep = ctx.enter_context(tc.tile_pool(name="keep", bufs=1))
        placed = ctx.enter_context(tc.tile_pool(name="placed", bufs=1))
        psum = ctx.enter_context(tc.psum_pool(name="psum", bufs=1))

        def sbuf(shape, dtype, name, tag=None):
            return keep.tile(shape, dtype, name=name, tag=tag or name, align_bytes=64)

        def at(offset, shape, dtype, name):
            return placed.tile(shape, dtype, name=name, tag=name, align_bytes=64, offset=offset)

        def bank(index, name):
            return psum.tile([P, BANK], F32, name=name, tag="bank%d" % index)

        def load_scale_rows(scale, source, first=0):
            by_row = source.rearrange("m (g r) w -> r g m w", r=SCALE_ROWS)
            for r in range(SCALE_ROWS):
                nc.sync.dma_start(out=scale[first + r : P : QUADRANT, :, :].bitcast(I32), in_=by_row[r].bitcast(I32))

        def two_rows(flat):
            return flat.rearrange("p (e t) -> p e t", e=2)

        def part(t):
            return slice(t * HALF, (t + 1) * HALF)

        long, short = slice(0, BANK), slice(BANK, T)

        w2_scale_raw = sbuf([P, PASSES, H], U8, "w2_scale_raw")
        dy_scale = sbuf([P, PASSES, T], U8, "dy_scale")
        wb_scale = sbuf([P, E2, K], U8, "wb_scale")
        wa_scale = sbuf([P, E1, K], U8, "wa_scale")
        for plane in (w2_scale_raw, dy_scale, wb_scale, wa_scale):
            nc.vector.memset(plane[:].bitcast(I32), 0)
        dc_rows = [sbuf([P, WIDE], BF16, "dc_row%d" % e) for e in range(2)]
        dc_late = sbuf([P, 2 * T], BF16, "dc_late")

        w2_raw = sbuf([P, PASSES, H], I32, "w2_raw")
        nc.sync.dma_start(out=w2_raw[:], in_=w2t_words.rearrange("s p i d -> p s (i d)").bitcast(I32))
        load_scale_rows(w2_scale_raw, w2t_scales)
        dy_codes = sbuf([P, PASSES, T], I32, "dy_codes")
        nc.sync.dma_start(out=dy_codes[:], in_=dy_words.rearrange("s p t d -> p s (t d)").bitcast(I32))
        load_scale_rows(dy_scale, dy_scales, SCALE_ROWS)

        a_view = a.rearrange("(p h e) t -> h p e t", h=2, e=2)
        c_view = c.rearrange("(p h e) t -> h p e t", h=2, e=2)
        a_early = sbuf([P, 2, T], F32, "a_early")
        nc.sync.dma_start(out=a_early[:, :, short], in_=a_view[0][:, :, short])
        for e in range(2):
            nc.sync.dma_start(out=a_early[:, e, long], in_=a_view[0][:, e, long])
        list_b = sbuf([P, T // STRIPE], U16, "list_b")
        nc.sync.dma_start(list_b[:], offs2)
        a_late = []
        for n, tokens in enumerate((long, short)):
            piece = sbuf([P, 2, tokens.stop - tokens.start], F32, "a_late%d" % n)
            nc.sync.dma_start(out=piece[:], in_=a_view[1][:, :, tokens])
            a_late.extend(piece[:, :, part(t)] for t in range(2 - n))
        c_first = sbuf([P, 2, HALF], F32, "c_first")
        nc.sync.dma_start(out=c_first[:], in_=c_view[1][:, :, :HALF])
        wb_codes = sbuf([P, E2, 2 * K], U8, "wb_codes")
        nc.sync.dma_start(out=wb_codes[:].bitcast(I32), in_=wbt_words.rearrange("f s p w -> p (f s) w").bitcast(I32))
        load_scale_rows(wb_scale, wbt_scales.rearrange("f s b k -> (f s) b k"))
        c_early = sbuf([P, 2, T], F32, "c_early")
        nc.sync.dma_start(out=c_early[:], in_=c_view[0])
        c_late = sbuf([P, 2, BANK], F32, "c_late")
        nc.sync.dma_start(out=c_late[:], in_=c_view[1][:, :, HALF:])
        list_a = sbuf([P, T // STRIPE], U16, "list_a")
        nc.sync.dma_start(list_a[:], offs)
        wa_codes = sbuf([P, E1, K], I32, "wa_codes")
        nc.sync.dma_start(out=wa_codes[:], in_=wat_words.rearrange("e s p k d -> p (e s) (k d)").bitcast(I32))
        load_scale_rows(wa_scale, wat_scales.rearrange("e s b k -> (e s) b k"))

        w2_codes = sbuf([P, PASSES, H], I32, "w2_codes")
        w2_scale = sbuf([P, PASSES, H], U8, "w2_scale")
        for s, move in enumerate((nc.vector.tensor_copy, nc.scalar.copy)):
            move(
                out=w2_codes[:, s, :].bitcast(U32).rearrange("p (j g m) -> p g j m", j=PACK, m=LINE // PACK),
                in_=w2_raw[:, s, :].bitcast(U32).rearrange("p (g m j) -> p g j m", j=PACK, m=LINE // PACK),
            )
        nc.vector.tensor_copy(
            out=w2_scale[:].rearrange("p s (j g m) -> p s g j m", j=PACK, m=LINE),
            in_=w2_scale_raw[:].rearrange("p s (g m j) -> p s g j m", j=PACK, m=LINE),
        )

        warm = bank(6, "warm_bank")
        for s in range(PASSES):
            nc.tensor.matmul_mx(
                out=warm[:],
                lhsT=w2_raw[:, s, :P].bitcast(FP8X4),
                lhsT_scale=w2_scale_raw[:, s, :P],
                rhs=w2_raw[:, s, :].bitcast(FP8X4),
                rhs_scale=w2_scale_raw[:, s, :],
                start=True,
                stop=True,
            )

        def dh_into(dst, j, tokens):
            cols = slice(j * P, (j + 1) * P)
            for s in range(PASSES):
                nc.tensor.matmul_mx(
                    out=dst,
                    lhsT=w2_codes[:, s, cols].bitcast(FP8X4),
                    lhsT_scale=w2_scale[:, s, cols],
                    rhs=dy_codes[:, s, tokens].bitcast(FP8X4),
                    rhs_scale=dy_scale[SCALE_ROWS:, s, tokens],
                    start=(s == 0),
                    stop=(s == PASSES - 1),
                )

        def gated(dst, saved, sums, test):
            nc.vector.scalar_tensor_tensor(out=dst, in0=saved, scalar=0.0, in1=sums, op0=test, op1=ALU.mult)

        masked_early = sbuf([P, 2, T], F32, "masked_early")

        def by_mask(e, tokens, sums):
            gated(masked_early[:, e, tokens], a_early[:, e, tokens], sums, ALU.is_gt)
            nc.gpsimd.tensor_tensor(
                out=dc_rows[e][:, tokens], in0=masked_early[:, e, tokens], in1=a_early[:, e, tokens], op=ALU.mult
            )

        early_banks = [bank(n, "dh_bank") for n in range(PARTS)]
        for e, sums in enumerate((early_banks[1], bank(7, "dh_bank"))):
            dh_into(sums[:, :HALF], e, short)
            by_mask(e, short, sums[:, :HALF])
        direct_banks = [early_banks[0], bank(6, "dh_bank")]
        for t in range(2):
            dh_into(direct_banks[t][:, :HALF], 0, part(t))
            gated(dc_rows[0][:, part(t)], a_early[:, 0, part(t)], direct_banks[t][:, :HALF], ALU.max)
        dh_into(early_banks[2][:], 1, long)
        by_mask(1, long, early_banks[2][:])

        late_banks = [bank(PARTS + t, "dh_bank") for t in range(PARTS)]
        for t in range(PARTS):
            for e in range(2):
                dh_into(late_banks[t][:, part(e)], 2 + e, part(t))
            gated(
                dc_late[:, t * BANK : (t + 1) * BANK].rearrange("p (t e) -> p t e", e=2),
                a_late[t].rearrange("p e t -> p t e"),
                late_banks[t][:].rearrange("p (e t) -> p t e", e=2),
                ALU.max,
            )

        def slots_of(slot_list, first, stop):
            return slot_list[:, first // STRIPE : stop // STRIPE]

        def gather_pairs(dst, window, slots):
            nc.vector.tensor_copy(dst, window.bitcast(U32).indirect(slots))

        def gather_row(dst, step, e, slots):
            nc.scalar.activation(dst.rearrange("p (n e) -> p n e", e=step)[:, :, e], dc_rows[e][:].indirect(slots), COPY)

        def weave(engine, woven, planes):
            engine.tensor_copy(out=woven.bitcast(U32).rearrange("p (n h) -> p n h", h=2), in_=planes)

        def quantize(name, values, first, stop, tag=None):
            codes = sbuf([P, stop - first], U32, name + "_codes", tag)
            scale = sbuf([P, stop - first], U8, name + "_scale")
            nc.vector.quantize_mx(out=codes[:].bitcast(FP8X4), scales=scale[:], in_=values)
            return first, codes, scale

        def product(dst, weights, fmt, scale_rows, e, b, quantized, first, stop):
            base, codes, scale = quantized
            width = weights.shape[2] // PACK
            nc.tensor.matmul_mx(
                out=dst,
                lhsT=weights[:, e, b * width : (b + 1) * width].bitcast(fmt),
                lhsT_scale=scale_rows[:, e, b * P : (b + 1) * P],
                rhs=codes[:, first - base : stop - base].bitcast(FP8X4),
                rhs_scale=scale[:, first - base : stop - base],
                start=True,
                stop=True,
            )

        def products_b(dst, b, quantized, first, stop):
            for lo in range(first - first % C2, stop, C2):
                lo, hi = max(lo, first), min(lo + C2, stop)
                product(dst[:, lo - first : hi - first], wb_codes, FP4X4, wb_scale, lo // C2, b, quantized, lo, hi)

        def products_a(dst, b, quantized, first, stop):
            for lo in range(first, stop, C1):
                product(dst[:, lo - first : lo - first + C1], wa_codes, FP8X4, wa_scale, lo // C1, b, quantized, lo, lo + C1)

        def scalar_scatter(window, slot_list, first, stop, values):
            nc.scalar.activation(window[:].indirect(slots_of(slot_list, first, stop)), values, COPY)

        def vector_scatter(window, slot_list, first, stop, values):
            nc.vector.tensor_copy(window[:].indirect(slots_of(slot_list, first, stop)), values)

        q_tok = [sbuf([P, T], F32, "q_tok%d" % b) for b in range(4)]

        REST = T - FIRST
        head, rest = slots_of(list_b, 0, FIRST), slots_of(list_b, FIRST, T)
        picked_rest = sbuf([P, 2 * REST], U32, "picked_rest")
        woven_head = at(0, [P, 2 * FIRST], U32, "woven_head")[:]
        for e in range(2):
            gather_row(woven_head.bitcast(BF16), PACK, e, head)
            gather_row(picked_rest[:, :REST].bitcast(BF16), 2, e, rest)
        gather_pairs(woven_head.rearrange("p (n h) -> p n h", h=2)[:, :, 1], dc_late[:], head)
        masked_first = sbuf([P, 2, HALF], F32, "masked_first")
        for e in range(2):
            gated(masked_first[:, e, :], a_late[0][:, e, :], late_banks[0][:, part(e)], ALU.is_gt)
        for t in range(2):
            gated(masked_early[:, 0, part(t)], a_early[:, 0, part(t)], direct_banks[t][:, :HALF], ALU.is_gt)
        dc_head = quantize("dc_head", woven_head.bitcast(BF16), 0, FIRST)
        staged = []
        for index, blocks in ((1, (1, 3)), (7, (0, 2))):
            sums = bank(index, "q_bank")
            for place, b in enumerate(blocks):
                products_b(sums[:, place * FIRST : (place + 1) * FIRST], b, dc_head, 0, FIRST)
            staged.append(sbuf([P, 2 * FIRST], F32, "q_staged_head%d" % index))
            nc.scalar.copy(out=staged[-1][:], in_=sums[:, : 2 * FIRST])
        for place, b in enumerate((1, 3, 0, 2)):
            scalar_scatter(q_tok[b], list_b, 0, FIRST, staged[place // 2][:, place % 2 * FIRST : (place % 2 + 1) * FIRST])

        def da_into(dst, masked, saved):
            nc.gpsimd.tensor_tensor(
                out=dst.rearrange("p (g i e) -> p g e i", i=4, e=2),
                in0=masked.rearrange("p e (g i) -> p g e i", i=4),
                in1=saved.rearrange("p e (g i) -> p g e i", i=4),
                op=ALU.mult,
            )

        da_late = at(0, [P, 2 * WIDE], BF16, "da_late")
        da_into(da_late[:, :BANK], masked_first[:], c_first[:])

        MID = BANK - FIRST
        gather_pairs(picked_rest[:, REST + MID :], dc_late[:], slots_of(list_b, BANK, T))
        gather_pairs(picked_rest[:, REST : REST + MID], dc_late[:], slots_of(list_b, FIRST, BANK))
        planes = picked_rest[:].rearrange("p (h n) -> p n h", h=2)
        woven_mid = at(4 * WIDE, [P, PACK * MID], BF16, "woven_mid")
        woven_last = at(8 * WIDE, [P, PACK * HALF], BF16, "woven_last")
        weave(nc.vector, woven_last[:], planes[:, MID:, :])
        weave(nc.vector, woven_mid[:], planes[:, :MID, :])
        dc_last = quantize("dc_last", woven_last[:], BANK, T)
        dc_mid = quantize("dc_mid", woven_mid[:], FIRST, BANK)
        masked_late = at(8 * WIDE, [P, 2, BANK], F32, "masked_late")
        for t in range(1, PARTS):
            gated(masked_late[:, :, part(t - 1)], a_late[t], two_rows(late_banks[t][:]), ALU.is_gt)

        da_early = at(4 * WIDE, [P, 2 * WIDE], BF16, "da_early")
        da_into(da_early[:, : 2 * T], masked_early[:], c_early[:])
        da_into(da_late[:, BANK : 2 * T], masked_late[:], c_late[:])

        def q_sums(index, b, first, stop):
            sums = bank(index, "q_bank")
            products_b(sums, b, dc_mid if first < BANK else dc_last, first, stop)
            return sums

        def staged(move, name, sums, width):
            values = sbuf([P, width], F32, name)
            move(out=values[:], in_=sums[:, :width])
            return values

        last1, last0, last2 = q_sums(6, 1, BANK, T), q_sums(2, 0, BANK, T), q_sums(1, 2, BANK, T - FIRST)
        mid2, mid0, mid1 = q_sums(0, 2, FIRST, BANK), q_sums(3, 0, FIRST, BANK), q_sums(7, 1, FIRST, BANK)
        last0_staged = staged(nc.scalar.copy, "last0_staged", last0, HALF)
        q2_staged = sbuf([P, BANK], F32, "q2_staged")
        nc.scalar.copy(out=q2_staged[:, MID:], in_=last2[:, :FIRST])
        mid3, share2, held3 = q_sums(2, 3, FIRST, SIDE), q_sums(4, 2, T - FIRST, T), q_sums(5, 3, SIDE, BANK)
        products_b(held3[:, BANK - SIDE :], 3, dc_last, BANK, T)
        last1_staged = staged(nc.vector.tensor_copy, "last1_staged", last1, HALF)
        nc.vector.tensor_copy(out=q2_staged[:, :MID], in_=mid2[:, :MID])
        vector_scatter(q_tok[1], list_b, BANK, T, last1_staged[:])
        vector_scatter(q_tok[2], list_b, FIRST, BANK - SHIFT, q2_staged[:, : MID - SHIFT])

        scalar_scatter(q_tok[0], list_b, BANK, T, last0_staged[:])
        mid0_staged = staged(nc.scalar.copy, "mid0_staged", mid0, MID)
        mid1_staged = staged(nc.scalar.copy, "mid1_staged", mid1, MID)
        scalar_scatter(q_tok[0], list_b, FIRST, BANK, mid0_staged[:])
        mid3_staged = staged(nc.scalar.copy, "mid3_staged", mid3, SIDE - FIRST)
        scalar_scatter(q_tok[1], list_b, FIRST, BANK, mid1_staged[:])
        scalar_scatter(q_tok[2], list_b, BANK - SHIFT, T - FIRST, q2_staged[:, MID - SHIFT :])
        scalar_scatter(q_tok[3], list_b, FIRST, SIDE, mid3_staged[:])

        sides = [(0, SIDE), (SIDE, T)]
        picked = sbuf([P, 2 * T], U32, "picked_da")
        for h, pairs in enumerate((da_early, da_late)):
            gather_pairs(picked[:, h * T : (h + 1) * T], pairs[:], list_a[:])
        share_staged = at(0, [P, FIRST], F32, "share_staged")
        nc.vector.tensor_copy(out=share_staged[:], in_=share2[:, :FIRST])
        woven = [sbuf([P, PACK * SIDE], BF16, "woven_da%d" % n) for n in range(2)]
        for n, (first, stop) in enumerate(sides):
            weave(nc.vector, woven[n][:], picked[:].rearrange("p (h n) -> p n h", h=2)[:, first:stop, :])
        da_q = [quantize("da%d" % n, woven[n][:], *sides[n]) for n in range(2)]
        vector_scatter(q_tok[2], list_b, T - FIRST, T, share_staged[:])

        def r_sums(index, b, first, stop):
            sums = bank(index, "r_bank")
            products_a(sums, b, da_q[first // SIDE], first, stop)
            return sums

        r_staged = [sbuf([P, T], F32, "r_staged%d" % b) for b in range(4)]
        r_tok = [sbuf([P, WIDE if b == 3 else T], F32, "r_tok%d" % b, None if b else "c_late") for b in range(4)]
        nc.gpsimd.tensor_copy(out=r_tok[0][:], in_=q_tok[0][:])

        def stage(move, sums, b, first, stop):
            move(out=r_staged[b][:, first:stop], in_=sums[:, : stop - first])

        def send(scatter, b, first, stop):
            scatter(r_tok[b], list_a, first, stop, r_staged[b][:, first:stop])

        front1, front0 = r_sums(6, 1, 0, SIDE), r_sums(1, 0, 0, SIDE)
        stage(nc.scalar.copy, front0, 0, 0, SIDE)
        front2, front3 = r_sums(3, 2, 0, SIDE), r_sums(0, 3, 0, SIDE)
        back0, back1, back2, back3 = [r_sums(index, b, SIDE, T) for b, index in enumerate((2, 7, 1, 4))]

        stage(nc.scalar.copy, front2, 2, 0, SIDE)
        stage(nc.vector.tensor_copy, front1, 1, 0, SIDE)
        stage(nc.vector.tensor_copy, front3, 3, 0, SIDE)
        send(vector_scatter, 1, 0, SIDE)
        stage(nc.vector.tensor_copy, back1, 1, SIDE, T)
        send(vector_scatter, 0, 0, SHARE)
        stage(nc.vector.tensor_copy, back3, 3, SIDE, T)
        send(vector_scatter, 1, SIDE, T)
        send(vector_scatter, 3, 0, T)

        scalar_scatter(q_tok[0], list_a, SHARE, SIDE, r_staged[0][:, SHARE:SIDE])
        stage(nc.scalar.copy, back0, 0, SIDE, T)
        stage(nc.scalar.copy, back2, 2, SIDE, T)
        scalar_scatter(q_tok[0], list_a, SIDE, T, r_staged[0][:, SIDE:])
        send(scalar_scatter, 2, SIDE, T)
        q3_held = sbuf([P, SIDE], F32, "q3_held", "r_staged0")
        nc.scalar.copy(out=q3_held[:], in_=held3[:, :SIDE])
        send(scalar_scatter, 2, 0, SIDE)
        scalar_scatter(q_tok[3], list_b, SIDE, T, q3_held[:])

        def store_rows(queue, b, cols, total):
            queue.dma_start(out=out[b * P : (b + 1) * P, cols], in_=total[:, cols])

        for b in range(3):
            total = sbuf([P, T], F32, "total%d" % b, "q_tok%d" % (b - 1) if b else None)
            nc.gpsimd.tensor_tensor(out=total[:], in0=r_tok[b][:, :T], in1=q_tok[b][:, :T], op=ALU.add)
            store_rows(nc.sync, b, slice(0, T), total)
        total = sbuf([P, T], F32, "total3")
        for queue, t in ((nc.sync, 0), (nc.scalar, 1), (nc.sync, 2)):
            nc.vector.tensor_tensor(out=total[:, part(t)], in0=r_tok[3][:, part(t)], in1=q_tok[3][:, part(t)], op=ALU.add)
            store_rows(queue, 3, part(t), total)
